import numpy as np, ml_dtypes
CORES = [8,136,40,168]
N = 4
BF = ml_dtypes.bfloat16
W, C, DH, S = 2048, 128, 256, 4
HI, LO, HA, HB = 11, 5, 1, 2
B, DB = W // C, DH // C
WT = np.array([37, 101, 59, 203, 83, 149, 11, 173, 67, 229, 127, 43, 191, 23, 251, 109])
def num(z):
    return np.sum(z * WT[:, None], axis=-2) & 4095
def place(u):
    return ((2741 * u) >> 5) & (DH - 1)
def pack(X, D, P, Q, z, l):
    a = np.ascontiguousarray
    return {"xr": a(X.reshape(N, 128, W)).astype(np.float32).astype(BF), "dr": a(D.reshape(N, 128, 2 * DH)).astype(np.int32),
            "pl": a(P.reshape(N, 128, C)).astype(np.int32), "ql": a(Q.reshape(N, 128, C)).astype(np.int32),
            "zq": a(z.reshape(N, 128, C)).astype(np.float32).astype(BF), "sd": a(l).astype(np.int32)}
def order(rng):
    return np.argsort(rng.random((8, W)), axis=1)
def over(pm):
    return np.broadcast_to(pm[None, :, None, :], (N, 8, 16, W))
def lay(pm, v):
    X = np.zeros((N, 8, 16, W), np.int64); np.put_along_axis(X, over(pm), v.astype(np.int64), 3)
    return X
def lanes(rng, pm, m):
    b = rng.integers(0, 16, (N, 8, 1, m)); t = rng.integers(0, W // 16, (N, 8, 16, m)); near = rng.random((N, 8, 1, m)) < 0.5
    return np.take_along_axis(over(pm), np.where(near, b * (W // 16) + t, rng.integers(0, W, (N, 8, 16, m))), 3)
def parts(rng):
    pm = order(rng)
    mid = np.repeat(rng.integers(60, 196, (N, 8, 16, 16)), W // 16, axis=3); amp = np.repeat(rng.choice(np.array([12.0, 40.0, 120.0]), (N, 8, 1, 16)), W // 16, axis=3)
    X = lay(pm, np.clip(np.floor(mid + amp * (2 * rng.random((N, 8, 16, W)) - 1)), 0, 255))
    return pm, X, lanes(rng, pm, 2 * DH), lanes(rng, pm, C), lanes(rng, pm, C), rng.integers(0, 256, (N, 8, 16, C)), rng.integers(0, 2, (N, 8, C))
def setup_inputs(rng):
    return pack(*parts(rng)[1:])
def setup_inputs_ends(rng):
    X = 255 * rng.integers(0, 2, (N, 8, 16, W)); dif = rng.choice(np.array([2, 3, 8, 16]), (N, 8)); dif[:, 7] = 16
    alt = np.argsort(rng.random((N, 8, 16)), axis=2) < dif[:, :, None]
    X[..., W - 1] = np.where(alt, 255 - X[..., 0], X[..., 0])
    cnt = rng.choice(np.array([0, LO - 1, LO, HI - 1, HI, 15, 16]), (N, 8, 1, 2 * DH))
    D = np.where(np.argsort(rng.random((N, 8, 16, 2 * DH)), axis=2) < cnt, W - 1, 0)
    kind = rng.integers(0, 3, (N, 8, 1, C)); Q = (W - 1) * np.where(kind == 2, rng.integers(0, 2, (N, 8, 16, C)), kind)
    P = (W - 1) * rng.integers(0, 2, (N, 8, 16, C)); l = rng.integers(0, 2, (N, 8, C))
    last = X[..., W - 1:]; half = np.argsort(rng.random((N, 8, 16, C)), axis=2) < 8; zk = rng.integers(0, 8, (N, 8, 1, C))
    z = 255 * rng.integers(0, 2, (N, 8, 16, C))
    z = np.where(zk == 0, 0, np.where(zk == 1, 255, np.where(zk == 2, 255 - last, np.where(zk == 3, X[..., :1], np.where(zk == 4, np.where(half, last, 255 - last), z)))))
    z[:, 7, :, C - 1] = 255 - X[:, 7, :, W - 1]; Q[:, 7, :, C - 1] = W - 1; l[:, 7, C - 1] = 1
    col = DH + place(num(z[:, 7, :, C - 1:]))[:, 0]
    for r in range(N): D[r, 7, :, col[r]] = W - 1
    return pack(X, D, P, Q, z, l)
def setup_inputs_corners(rng):
    pm = order(rng); V = W // 8; o = over(pm)
    b0 = rng.integers(2, 254, (N, 8, 16, 1)); b0[:, 1] = rng.integers(0, 3, (N, 16, 1)); b0[:, 6] = rng.integers(253, 256, (N, 16, 1))
    m = np.repeat(np.array([0, 0, 1, 2, 2, 3, 3, 4]), V)
    out = np.argsort(rng.random((N, 8, 16, W)), axis=2) < m
    by = 2 * rng.integers(0, 2, (N, 8, 16, W)) - 1; by = np.where(b0 == 0, 1, np.where(b0 == 255, -1, by))
    X = lay(pm, b0 + np.where(out, by, 0))
    cnt = rng.choice(np.array([0, LO - 1, LO, HI - 1, HI, 15, 16]), (N, 8, 1, 2 * DH)); odd = rng.random((N, 8, 1, 2 * DH)) < 0.35
    t = rng.integers(0, 2 * V, (N, 8, 16, 2 * DH)); t1 = t % V
    j = np.where(np.argsort(rng.random((N, 8, 16, 2 * DH)), axis=2) < cnt, np.where(odd, 2 * V + t1, 3 * V + t), np.where(odd, 3 * V + t1, 5 * V + t))
    D = np.take_along_axis(o, j, 3)
    own = B * np.arange(C) + rng.integers(0, B, (N, 8, 16, C)); ed = (W - 1) * rng.integers(0, 2, (N, 8, 16, C)); kind = rng.integers(0, 8, (N, 8, 1, C))
    Q = np.where(kind == 0, own, np.where(kind == 1, ed, np.take_along_axis(o, rng.integers(0, 2 * V, (N, 8, 16, C)), 3)))
    kind = rng.integers(0, 4, (N, 8, 1, C)); P = np.where(kind == 0, own, np.where(kind == 1, ed, np.take_along_axis(o, rng.integers(0, 8 * V, (N, 8, 16, C)), 3)))
    zk = rng.integers(0, 5, (N, 8, 1, C)); z = np.where(zk == 0, 0, np.where(zk == 1, 255, np.where(zk == 2, b0, rng.integers(0, 256, (N, 8, 16, C)))))
    l = (rng.random((N, 8, C)) < rng.choice(np.array([0.0, 0.5, 1.0]), (N, 8, 1))).astype(np.int64)
    return pack(X, D, P, Q, z, l)
def setup_inputs_crowd(rng):
    pm, X, D, P, Q, z, l = parts(rng)
    ix = np.zeros((8, C), np.int64)
    for g in (1, 3, 5, 7):
        e = C - 1 if g < 4 else int(rng.integers(1, C)); ix[g, e] = e
    w = np.broadcast_to(ix[None, :, None, :], (N, 8, 16, C))
    P, Q, z = [np.take_along_axis(v, w, 3) for v in (P, Q, z)]; l = np.take_along_axis(l, np.broadcast_to(ix[None], (N, 8, C)), 2)
    for v in (P, Q, z, l): v[1:, :2] = v[:1, :2]
    Q[:, 2:4] = Q[:, 2:4, :1].copy(); D[:, 2:4] = D[:, 2:4, :1].copy()
    D[:, 4:6] = Q[:, 4:6, :, :1]; D[:, 5, 15] = rng.integers(0, W, (N, 2 * DH))
    return pack(X, D, P, Q, z, l)
def setup_inputs_drops(rng):
    pm, X, D, P, Q, z, l = parts(rng); dg = (np.arange(8) % 3 != 2)[:, None, None]
    X1 = rng.integers(0, 101, X.shape); X1[..., W - 1] = 255
    Q1 = rng.integers(0, W - 1, Q.shape); z1 = rng.integers(0, 101, z.shape)
    if W == 4096:
        one = np.zeros((16, 1), np.int64); one[14] = 16; one[6] = 7
        pool = rng.integers(0, 101, (16, 32768)); pool = np.concatenate([one, pool[:, num(pool) >= 4064]], axis=1)
        high = np.argsort(rng.random((N, 8, 1, C)), axis=3) < C // 2
        z1 = np.where(high, np.moveaxis(pool[:, rng.integers(0, pool.shape[1], (N, 8, C))], 0, 2), z1)
        Q1 = np.where(high, rng.integers(W - 32, W - 1, Q.shape), Q1)
        z1[:, 7, :, C - 1] = one[:, 0]; Q1[:, 7, :, C - 1] = rng.integers(W - 32, W - 1, (N, 16)); Q1[:, 7, 15, C - 1] = 4075
    return pack(np.where(dg, X1, X), np.where(dg, W - 1, D), P, np.where(dg, Q1, Q), np.where(dg, z1, z), l)
def setup_inputs_spread(rng):
    e = rng.choice(np.array([1.0, 1.0, 3.0]), (N, 8, 1, 1))
    X = (np.exp2(8 * rng.random((N, 8, 1, W))) * rng.random((N, 8, 16, W))).astype(np.int64); z = (np.exp2(8 * rng.random((N, 8, 1, C))) * rng.random((N, 8, 16, C))).astype(np.int64)
    D, P, Q = [(W * rng.random((N, 8, 16, k)) ** e).astype(np.int64) for k in (2 * DH, C, C)]
    l = (rng.random((N, 8, C)) < rng.random((N, 8, 1))).astype(np.int64)
    return pack(X, D, P, Q, z, l)
def check_inputs(d):
    bad = []
    for k, lo, hi in (("xr", 0, 255), ("dr", 0, W - 1), ("pl", 0, W - 1), ("ql", 0, W - 1), ("zq", 0, 255), ("sd", 0, 1)):
        a = np.asarray(d[k]).astype(np.float64)
        if not (np.min(a) >= lo and np.max(a) <= hi): bad.append("range of " + k)
        elif np.any(a != np.floor(a)): bad.append("whole numbers in " + k)
    return bad
def go_on(v):
    h = C // 2
    return np.concatenate([np.roll(v[..., :h], HA, axis=0), np.roll(v[..., h:], HB, axis=0)], axis=-1)
def reference(xr, dr, pl, ql, zq, sd):
    X = xr.astype(np.float32).astype(np.int64).reshape(N, 8, 16, W); D = dr.astype(np.int64).reshape(N, 8, 16, 2 * DH)
    P = pl.astype(np.int64).reshape(N, 8, 16, C); Q = ql.astype(np.int64).reshape(N, 8, 16, C)
    z = zq.astype(np.float32).astype(np.int64).reshape(N, 8, 16, C); l = sd.astype(np.int64); A = np.zeros((N, 8, C), np.int64)
    c = np.arange(C); lane = np.arange(16)[:, None]
    for step in range(S):
        u = num(z)
        E = np.take_along_axis(D, (DH * l + place(u))[:, :, None, :], 3)
        x = np.take_along_axis(X, E.reshape(N, 8, 1, 16 * C), 3).reshape(N, 8, 16, 16, C)
        y = np.take_along_axis(X, Q.reshape(N, 8, 1, 16 * C), 3).reshape(N, 8, 16, 16, C)
        lo = np.min(y, axis=3); hi = np.max(y, axis=3)
        rows = np.sum((lo[:, :, :, None, :] <= x) & (x <= hi[:, :, :, None, :]), axis=2)
        ok = rows >= 14 + (A & 1)[:, :, None, :]; n = np.sum(ok, axis=2)
        dist = np.sum(np.abs(x - z[:, :, :, None, :]), axis=2)
        beta = np.argmin(np.where(ok, dist, 2 ** 20), axis=2)
        xb = np.take_along_axis(x, beta[:, :, None, None, :], 3)[:, :, :, 0, :]
        P1 = np.where(ok, E, P); made = (((Q * u[:, :, None, :]) >> 5) + Q + 37 * lane) & (W - 1)
        cont = (n >= HI)[:, :, None, :]; drop = (n < LO)[:, :, None, :]
        z = np.where(cont, np.abs(z - xb), np.where(drop, np.abs(z - hi), (z + xb) >> 1))
        u1 = num(z)
        dc = (DH * (1 - l) + DB * c + (u1 & (DB - 1)))[:, :, None, :]
        np.put_along_axis(D, dc, np.where(cont, P1, np.take_along_axis(D, dc, 3)), 3)
        xc = (B * c + (u1 & (B - 1)))[:, :, None, :]
        np.put_along_axis(X, xc, (np.take_along_axis(X, xc, 3) + z) >> 1, 3)
        P, Q = np.where(cont, P1, Q), np.where(cont, Q, np.where(drop, made, P1))
        l = np.where(n >= HI, l, 1 - l); A = A + (n < LO)
        if step < S - 1: P, Q, z, l, A = [go_on(v) for v in (P, Q, z, l, A)]
    return {"yx": X.reshape(N, 128, W).astype(np.float32).astype(BF), "yd": D.reshape(N, 128, 2 * DH).astype(np.float32), "yp": P.reshape(N, 128, C).astype(np.float32),
            "yq": Q.reshape(N, 128, C).astype(np.float32), "yz": z.reshape(N, 128, C).astype(np.float32).astype(BF), "ys": (2 * A + l).astype(np.float32)}

@@ -1,0 +1,619 @@
+from concourse.bass import DstId, RemoteDMATransfer
+from concourse.mybir import AluOpType as ALU, AxisListType as AX, ActivationFunctionType as AF
+
+WT = [37, 101, 59, 203, 83, 149, 11, 173, 67, 229, 127, 43, 191, 23, 251, 109]
+STEPS = 4
+OPT = {"vy": 16, "vx": 0, "bp": 0, "pm": 1, "e": 1, "early": 0, "early0": 0, "xa": 0, "ubp": 0}
+S = 192
+WW = 704
+MW = 272
+BIG = 65536.0
+MAGIC = 12582912.0
+
+
+def _sb(cols, dt):
+    return ("sbuf", [128, cols], {"b": "bfloat16", "f": "float32", "i": "int32", "u": "uint16"}[dt])
+
+
+SCRATCH = {
+    "X": _sb(2048, "b"), "Di": _sb(512, "i"), "D": _sb(1536, "f"),
+    "yy": _sb(2048, "b"), "xx": _sb(2048, "b"), "hs": _sb(2048, "b"), "ls": _sb(2048, "b"),
+    "aa": _sb(2048, "b"), "bb": _sb(2048, "b"), "ad": _sb(2048, "b"),
+    "W": _sb(STEPS * WW, "f"), "PQi": _sb(256, "i"), "Fi": _sb(128, "i"),
+    "m1": _sb(512, "u"), "m2": _sb(STEPS * MW, "b"), "o1": _sb(384, "u"), "o2": _sb(STEPS * MW, "b"), "o3": _sb(1024, "f"),
+    "A1": _sb(256, "i"), "A2": _sb(8, "i"), "A3": _sb(16, "i"), "A4": _sb(128, "b"), "mask": _sb(256, "b"), "bo": _sb(16, "u"),
+    "col": _sb(8, "f"), "wrow": _sb(16, "f"), "I": _sb(128, "b"), "nI": _sb(128, "b"), "hI": _sb(128, "b"), "If": _sb(128, "f"),
+    "krow": _sb(128, "b"), "c30": _sb(128, "b"), "half": _sb(128, "b"), "cq": _sb(128, "b"), "cM": _sb(128, "b"),
+    "rmax": _sb(512, "b"), "rmin": _sb(512, "b"),
+    "Dq": _sb(8, "b"), "W8": _sb(16, "b"), "R8": _sb(16, "b"), "C": _sb(128, "b"), "W2": _sb(16, "b"),
+    "Rk": _sb(32, "b"), "Rc": _sb(40, "b"), "Rd": _sb(16, "b"), "Re": _sb(16, "b"), "RL": _sb(128, "b"),
+    "kwin": _sb(8, "f"), "cb": _sb(8, "f"), "cs": _sb(8, "f"), "shift": _sb(64, "b"),
+    "ri": _sb(16, "i"), "rt": _sb(16, "i"), "lr": _sb(256, "b"), "ce": _sb(8, "u"), "E": _sb(128, "u"), "nE": _sb(128, "f"),
+    "okN": _sb(128, "b"), "xo": _sb(128, "b"),
+    "uw": _sb(8, "f"), "ub": _sb(128, "f"), "u1": _sb(128, "i"), "u2": _sb(128, "i"), "eT": _sb(512, "b"),
+    "zw": _sb(384, "b"), "zs": _sb(128, "b"), "DkS": _sb(128, "f"), "key": _sb(128, "f"), "ms": _sb(128, "f"),
+    "okT": _sb(128, "b"), "ns": _sb(128, "b"),
+    "wi": _sb(8, "i"), "wj": _sb(16, "i"), "lb": _sb(256, "b"), "of": _sb(40, "u"), "kN": _sb(128, "b"),
+    "tb": _sb(128, "b"), "t1": _sb(128, "f"), "t3": _sb(128, "f"), "fa": _sb(144, "f"),
+    "vi": _sb(16, "i"), "vj": _sb(16, "i"), "lv": _sb(256, "b"), "oo": _sb(8, "u"), "od": _sb(8, "u"),
+    "xn": _sb(128, "i"), "sS": _sb(128, "f"),
+}
+for _n in ("pA", "pB"):
+    SCRATCH[_n] = ("psum", [128, 1024], "bfloat16") if OPT["bp"] else ("psum", [128, 512], "float32")
+for _n in ("pD0", "pD1", "pL", "pK", "pS", "pT"):
+    SCRATCH[_n] = ("psum", [128, 512], "float32")
+NDMA = 16
+SEMAPHORES = (["eV", "eA", "eP", "eG", "sent"] + ["d%d" % i for i in range(NDMA)]
+              + ["r%d_%d" % (m, s) for m in (1, 2, 3) for s in range(1, STEPS)])
+
+
+def rank_program(g, core, T, topo):
+    rank = T.rank_of(core)
+    if rank is None:
+        return
+    n = len(T.cores)
+    Q = {"V": g.vector, "A": g.scalar, "P": g.tensor, "G": g, "S": g.sync}
+    ops = []
+
+    def v(name, a=None, b=None, st=1, p=None):
+        t = T[name]
+        a = 0 if a is None else a
+        b = t.shape[1] if b is None else b
+        cs = slice(a, b, st) if st != 1 else slice(a, b)
+        ap = t[:, cs] if p is None else t[p, cs]
+        bits = ((1 << b) - (1 << a)) if st == 1 else sum(1 << c for c in range(a, b, st))
+        return {"ap": ap, "r": [(name, bits)]}
+
+    def ind(win, off):
+        return {"ap": win["ap"].indirect(off["ap"]), "r": win["r"], "x": off["r"]}
+
+    def regs(xs):
+        out = []
+        for x in xs:
+            if isinstance(x, dict):
+                out += x["r"] + x.get("x", [])
+        return out
+
+    def a_(x):
+        return x["ap"] if isinstance(x, dict) else x
+
+    def add(q, call, out, ins, token=None):
+        ops.append([q, call, regs(ins) + out.get("x", []), out["r"], token])
+
+    def cp(out, x):
+        add("V", lambda e: e.tensor_copy(a_(out), a_(x)), out, [x])
+
+    def tt(out, x, y, op):
+        add("V", lambda e: e.tensor_tensor(a_(out), a_(x), a_(y), op), out, [x, y])
+
+    def ts(out, x, s1, op0, s2=None, op1=None):
+        if op1 is None:
+            add("V", lambda e: e.tensor_scalar(a_(out), a_(x), a_(s1), None, op0), out, [x, s1])
+        else:
+            add("V", lambda e: e.tensor_scalar(a_(out), a_(x), a_(s1), a_(s2), op0, op1), out, [x, s1, s2])
+
+    def scan(out, d0, d1, op0, op1):
+        add("V", lambda e: e.tensor_tensor_scan(a_(out), a_(d0), a_(d1), 0.0, op0, op1), out, [d0, d1])
+
+    def red(out, x):
+        add("V", lambda e: e.tensor_reduce(a_(out), a_(x), AX.X, ALU.add), out, [x])
+
+    def fill(out, c):
+        add("V", lambda e: e.memset(a_(out), c), out, [])
+
+    def act(out, x, f=None, bias=0.0, scale=1.0):
+        f = AF.Identity if f is None else f
+        add("A", lambda e: e.activation(a_(out), a_(x), f, bias=a_(bias), scale=a_(scale)), out, [x, bias, scale])
+
+    def mm(out, l, r, start=True, stop=True):
+        add("P", lambda e: e.matmul(a_(out), a_(l), a_(r), start, stop), out, [l, r])
+
+    def tr(out, x, ident):
+        add("P", lambda e: e.transpose(a_(out), a_(x), a_(ident)), out, [x, ident])
+
+    def iota(out, pat, base, cm, small=False):
+        if small:
+            add("G", lambda e: e.iota(a_(out), pat, base, cm, allow_small_or_imprecise_dtypes=True), out, [])
+        else:
+            add("G", lambda e: e.iota(a_(out), pat, base, cm), out, [])
+
+    nd = [0]
+
+    def dma(q, out, x):
+        sem = "d%d" % nd[0]
+        nd[0] += 1
+        add(q, lambda e: e.dma_start(a_(out), a_(x)), out if isinstance(out, dict) else {"r": []}, [x], (sem, 16, "dma"))
+
+    to = [T.cores[(rank + 1) % n], T.cores[(rank + 2) % n]]
+    eng = [e for e in topo.engines(core, to[0]) if e in topo.engines(core, to[1])]
+    per = len(eng) // 2
+    masks = [sum(1 << e for e in eng[:per]), sum(1 << e for e in eng[per:2 * per])]
+    nsent = [0]
+
+    def send(m, s):
+        src, dst, sem = "o%d" % m, ("m1", "m2", "W")[m - 1], "r%d_%d" % (m, s + 1)
+        w = (64, MW // 2, 128)[m - 1]
+        so, do = 2 * w * s, (WW * (s + 1) + 2 * S - 64 if m == 3 else 2 * w * (s + 1))
+
+        def call(e):
+            trs = []
+            for h in range(2):
+                rid, pid = topo.addr(to[h], core)
+                trs.append(RemoteDMATransfer(
+                    dst_ids=[DstId(rid=rid, pnc=pid)], dma_engine_mask=masks[h], remote_sem=T.sem[sem],
+                    src=T[src][:, so + w * h:so + w * h + w], dst=T[dst][:, do + w * h:do + w * h + w]))
+            return e.remote_dma_fused(trs, local_sem=T.sem.sent)
+        nsent[0] += 2 * per
+        add("G", call, {"r": []}, [v(src, so, so + 2 * w)], ("sent", nsent[0], "remote"))
+        add("X", None, v(dst, do, do + 2 * w), [], (sem, 2 * per, "arrive"))
+
+    fill(v("Fi"), 0)
+    dma("S", v("X"), T.xr[:])
+    dma("A", v("PQi", 64, 192), T.ql[:])
+    dma("A", v("m2", 72, 200), T.zq[:])
+    dma("S", v("Fi", p=slice(0, 128, 16)), T.sd[:])
+    dma("S", v("Di"), T.dr[:])
+    dma("S", v("PQi", 0, 64), T.pl[:, 0:64])
+    dma("S", v("PQi", 192, 256), T.pl[:, 64:128])
+
+    iota(v("A2"), [[-16, 8]], 0, 1)
+    iota(v("A1"), [[0, 16], [-1, 16]], 128, 1)
+    iota(v("col", 0, 1), [[0, 1]], 0, 1, True)
+    iota(v("A4"), [[1, 128]], 0, -1, True)
+    iota(v("A3"), [[1, 16]], 0, 0)
+    for r in range(0, 16, 2):
+        iota(v("wrow", r, r + 2), [[WT[r + 1] - WT[r], 2]], WT[r], 0, True)
+    iota(v("krow"), [[0, 8], [1, 16]], 0, 0, True)
+
+    def mk(j):
+        return v("mask", j, j + 1)
+
+    Dq = v("Dq")
+    CN = {"sel0": 0, "g16": 1, "gB": 2, "128th": 3, "h": 4, "vb": 5, "4": 6, "rs": 7}
+
+    def C(k, a=0, e=8):
+        return v("C", 8 * CN[k] + a, 8 * CN[k] + e)
+
+    fill(v("rmax"), 1.0)
+    ts(v("A2"), v("A2"), 4, ALU.arith_shift_right)
+    fill(v("rmin"), 0.0)
+    ts(Dq, v("A2"), 0.0, ALU.is_equal)
+    ts(v("A1"), v("A1"), 15, ALU.bitwise_and)
+    fill(v("rmax", 0, 512, 16), 0.0)
+    fill(v("rmin", 0, 512, 16), 4194304.0)
+    ts(v("mask"), v("A1"), 0.0, ALU.is_equal)
+    act(C("128th"), Dq, scale=1.0 / 128)
+    act(C("g16"), Dq, scale=16.0)
+    act(C("gB"), Dq, scale=-BIG)
+    act(C("h"), Dq, scale=0.5)
+    act(C("vb"), Dq, scale=-1.0 / 2048)
+    act(C("4"), Dq, scale=4.0)
+    act(v("Rk", 0, 8), Dq)
+    act(v("Rk", 8, 16), Dq, scale=128.0)
+    act(v("Rk", 16, 20), v("Dq", 0, 4), scale=-float(S))
+    act(v("Rk", 20, 28), Dq, scale=float(S))
+    act(v("Rk", 28, 32), v("Dq", 4, 8), scale=-float(S))
+    act(v("Rc", 16, 24), Dq, scale=v("col", 0, 1))
+    act(v("Rc", 8, 16), Dq, scale=0.0)
+    act(v("Rd", 0, 4), v("Dq", 0, 4), scale=3.0 * S)
+    act(v("Rc", 0, 8), v("Rc", 16, 24), scale=16.0)
+    act(v("Rc", 24, 28), v("Rc", 16, 20))
+    act(v("Rc", 28, 36), v("Rc", 16, 24))
+    act(v("Rc", 36, 40), v("Rc", 20, 24))
+    act(v("Rd", 4, 12), Dq, scale=0.0)
+    act(v("Rd", 12, 16), v("Dq", 4, 8), scale=3.0 * S)
+    act(v("Re", 8, 16), v("Rc", 16, 24), scale=-1.0 / 64)
+    ts(C("sel0"), Dq, mk(0), ALU.mult)
+    ts(v("R8", 0, 8), Dq, mk(1), ALU.mult, BIG / 2, ALU.mult)
+    fill(v("m2", 0, 8), -1.0)
+    fill(v("m2", MW - 8, MW), -1.0)
+    ts(v("I"), v("A4"), 0.0, ALU.is_equal)
+    cp(v("bo"), v("A3"))
+    ts(v("kwin"), v("A3", 0, 8), 0.5, ALU.mult)
+    ts(v("col", 2, 3), v("A1", 0, 1), 1184.0, ALU.mult)
+    red(v("col", 3, 4), v("mask", 2, 6))
+    ts(v("m2", 8, 72), v("Fi", 0, 64), 2.0, ALU.mult, -1.0, ALU.add)
+    ts(v("m2", 200, 264), v("Fi", 64, 128), 2.0, ALU.mult, -1.0, ALU.add)
+    cp(v("m1", 0, 128), v("PQi", 64, 192))
+    tt(v("wrow"), v("wrow"), v("mask", 0, 16), ALU.mult)
+    red(v("col", 1, 2), v("wrow"))
+    ts(v("W8", 0, 8), Dq, v("col", 1, 2), ALU.mult)
+    bo8 = v("bo", 0, 8)
+    act(v("col", 5, 6), mk(0), scale=-1.25, bias=0.5)
+    act(v("nI"), v("I"), scale=-1.0)
+    act(v("col", 6, 7), mk(1), scale=-0.75, bias=v("col", 5, 6))
+    act(v("hI"), v("I"), scale=0.5)
+    act(v("cb", 0, 4), v("mask", 2, 6), scale=-0.75, bias=v("col", 6, 7))
+    act(v("If"), v("I"))
+    act(v("cs", 0, 4), v("cb", 0, 4), scale=-1.0, bias=-0.75)
+    for name, c in (("c30", 30.5 * BIG), ("half", 0.5), ("cq", -0.25), ("cM", MAGIC)):
+        act(v(name), v("I"), scale=0.0, bias=c)
+    act(v("RL"), ind(v("R8", 0, 8), bo8))
+    act(v("shift"), ind(v("cs", 0, 4), v("bo", 0, 4)))
+
+    def late_constants(part):
+        if part == 0:
+            cp(v("D", 0, 512), v("Di"))
+            return
+        if part == 1:
+            cp(v("W", 2 * S - 64, 3 * S), v("PQi"))
+            return
+        act(v("col", 4, 5), mk(0), scale=0.5, bias=v("col", 3, 4))
+        act(v("W2", 0, 8), v("W8", 0, 8), scale=2.0)
+        act(v("W2", 8, 16), v("W8", 0, 8), scale=16.0)
+        act(C("rs"), Dq, scale=v("col", 4, 5))
+
+    LO, HI = slice(0, 64), slice(64, 128)
+    I, m128 = v("I"), v("mask", 0, 128)
+    Xw = v("X")
+    DB = (("pD0", "pD1"), ("pT", "pS"))
+
+    for s in range(STEPS):
+        b = MW * s
+        last = s == STEPS - 1
+        z, Flo, Fhi = v("m2", b + 72, b + 200), v("m2", b + 8, b + 72), v("m2", b + 200, b + 264)
+        Llo, Lhi = v("m2", b + 4, b + 8), v("m2", b + 264, b + 268)
+
+        def W(a=0, e=WW):
+            return v("W", WW * s + a, WW * s + e)
+
+        Plo, Phi, Qa, P1 = W(2 * S - 64, 2 * S), W(2 * S + 128, 3 * S), W(2 * S, 2 * S + 128), W(S, S + 128)
+
+        def gy(a, e, q="A"):
+            (act if q == "A" else cp)(v("yy", 16 * a, 16 * e), ind(Xw, v("m1", 128 * s + a, 128 * s + e)))
+
+        def sc_hi(q):
+            scan(v("hs", 512 * q, 512 * q + 512), v("rmax"), v("yy", 512 * q, 512 * q + 512), ALU.mult, ALU.max)
+
+        def sc_lo(q):
+            scan(v("ls", 512 * q, 512 * q + 512), v("rmin"), v("yy", 512 * q, 512 * q + 512), ALU.max, ALU.min)
+
+        def bcast(h, part):
+            pb = ("pA", "pB")[h]
+            for j, src in enumerate(("ls", "hs")):
+                ends = v(src, 1024 * h + 15, 1024 * h + 1024, 16)
+                if OPT["bp"] and part == 0:
+                    tr(v(pb, 512 + 128 * j, 640 + 128 * j, p=LO), ends, I)
+                for kk in range(4):
+                    out = v(pb, 256 * j + kk, 256 * j + 256, 4)
+                    if OPT["bp"] and part == 2:
+                        tr(out, v("eT", 256 * h + 128 * j, 256 * h + 128 * j + 128, p=LO), v("I", 0, 64, p=LO))
+                    if not OPT["bp"] and part == 0:
+                        mm(out, I, ends)
+            if OPT["bp"] and part == 1:
+                cp(v("eT", 256 * h, 256 * h + 256, p=LO), v(pb, 512, 768, p=LO))
+
+        def gx(a, e, q="A"):
+            (act if q == "A" else cp)(v("xx", 16 * a, 16 * e), ind(Xw, v("E", a, e)))
+
+        def dz(h, m):
+            for kk in range(8):
+                mm(v(DB[h][m], kk, 512, 8), v("nI"), v("m2", b + 72 + 64 * h, b + 136 + 64 * h), kk == 0, False)
+
+        def dx(h, m):
+            mm(v(DB[h][m]), I, v("xx", 1024 * h + m, 1024 * h + 1024, 2), False, True)
+
+        def absd(h, m):
+            o = 1024 * m + 512 * h
+            act(v("ad", o, o + 512), v(DB[h][m]), AF.Abs)
+
+        def made(part):
+            if part == 0:
+                tt(v("pK", 256, 384), v("pK", 256, 384), Qa, ALU.mult)
+            elif part == 1:
+                ts(v("u1"), v("pK", 256, 384), v("col", 2, 3), ALU.add)
+                mm(v("pK", 0, 128), I, v("krow"), True, False)
+            elif part == 2:
+                ts(v("u2"), v("u1"), 5, ALU.arith_shift_right, 2047, ALU.bitwise_and)
+            else:
+                cp(W(0, 128), v("u2"))
+
+        def sum_d(m):
+            for kk in range(8):
+                mm(v("pK", m + 2 * kk, 128, 16), v("ad", 1024 * m + kk, 1024 * m + 1024, 8), C("g16"), False, m == 1 and kk == 7)
+
+        def cmp(h, m, j):
+            o = 512 * m + 256 * h
+            tt(v(("aa", "bb")[j], o, o + 256), v("xx", 1024 * h + m, 1024 * h + 1024, 4),
+               v(("pA", "pB")[h], 256 * j, 256 * j + 256), (ALU.is_ge, ALU.is_le)[j])
+
+        def sum_c(m, j):
+            for kk in range(4):
+                mm(v("pL", m + 4 * kk, 128, 16), v(("aa", "bb")[j], 512 * m + kk, 512 * m + 512, 4), C("gB"), False,
+                   m == 3 and j == 1 and kk == 3)
+
+        vy, vx = (OPT["vy"] if s else 0), OPT["vx"]
+        early = OPT["early"] if s else OPT["early0"]
+        if vy:
+            gy(0, vy, "V")
+        for q in range(4 - early):
+            if 32 * q + 32 > vy:
+                gy(max(32 * q, vy), 32 * q + 32)
+        if s > 0 and OPT["e"] < 2:
+            sc_hi(0)
+        mm(v("pS", 0, 8), z, v("W8", 0, 8))
+        if s == 0:
+            mm(v("pS", 8, 16, p=LO), Flo, C("sel0"))
+            mm(v("pS", 8, 16, p=HI), Fhi, C("sel0"))
+            cp(v("ri"), v("pS", 0, 16))
+            tt(v("lr", 128, 256), ind(v("ri"), v("bo", 8, 16)), m128, ALU.mult)
+            mm(v("pT", 0, 8), v("lr", 128, 256), Dq)
+            cp(Llo, v("pT", 0, 4))
+            cp(Lhi, v("pT", 4, 8))
+        else:
+            if OPT["e"] < 2:
+                sc_lo(0)
+            cp(v("ri", 0, 8), v("pS", 0, 8))
+        mm(v("pS", 16, 20), I, Llo, True, False)
+        mm(v("pS", 20, 24), I, Lhi, False, False)
+        ts(v("rt", 0, 8), v("ri", 0, 8), 4095, ALU.bitwise_and)
+        ts(v("rt", 8, 16), v("rt", 0, 8), 2741.0, ALU.mult)
+        ts(v("uw"), v("rt", 0, 8), 32.0, ALU.add)
+        ts(v("vj", 0, 8), v("rt", 8, 16), 5, ALU.arith_shift_right, 255, ALU.bitwise_and)
+        tt(v("lr", 0, 128), ind(v("vj", 0, 8), bo8), m128, ALU.mult)
+        mm(v("pS", 16, 24), v("lr", 0, 128), C("128th"), False, True)
+        if s == 0:
+            late_constants(0)
+        elif OPT["e"] < 2:
+            sc_hi(1)
+        ts(v("ce"), v("pS", 16, 24), 128.0, ALU.mult, 128.0, ALU.add)
+        cp(v("E"), ind(v("D", 0, 512), v("ce")))
+        if s == 0:
+            late_constants(1)
+        (cp if OPT["ubp"] else act)(v("ub"), ind(v("uw"), bo8))
+        gx(vx, 64)
+        for q in range(4 - early, 4):
+            gy(32 * q, 32 * q + 32)
+        gx(64, 128)
+        if s == 0 or OPT["e"] == 2:
+            sc_hi(0)
+            sc_lo(0)
+            sc_hi(1)
+        sc_lo(1)
+        bcast(0, 0)
+        if early < 2:
+            sc_hi(2)
+        bcast(0, 1)
+        bcast(0, 2)
+        mm(v("pL", 0, 128), I, v("c30"), True, False)
+        mm(v("pL", 0, 128, p=LO), Flo, v("RL"), False, False)
+        mm(v("pL", 0, 128, p=HI), Fhi, v("RL"), False, False)
+        dz(0, 0)
+        dz(0, 1)
+        mm(v("pK", 256, 384), v("ub"), v("If"))
+        if early < 2:
+            sc_lo(2)
+        if not early:
+            sc_hi(3)
+            sc_lo(3)
+            bcast(1, 0)
+            bcast(1, 1)
+            bcast(1, 2)
+        made(0)
+        made(1)
+        if vx:
+            gx(0, vx, "V")
+
+        dx(0, 0)
+        dx(0, 1)
+        dz(1, 0)
+        dz(1, 1)
+        for m in range(4):
+            cmp(0, m, 0)
+            cmp(0, m, 1)
+            if early == 2 and m == 1:
+                sc_hi(2)
+                sc_lo(2)
+            if early and m == early:
+                sc_hi(3)
+                sc_lo(3)
+                bcast(1, 0)
+            if early and m == early + 1:
+                bcast(1, 1)
+                bcast(1, 2)
+        dx(1, 0)
+        dx(1, 1)
+        absd(0, 0)
+        absd(1, 0)
+        mm(v("pD0", 128, 256), I, z, True, False)
+        mm(v("pD0", 128, 256), v("nI"), v("hs", 15, 2048, 16), False, True)
+        absd(0, 1)
+        absd(1, 1)
+        cmp(1, 0, 0)
+        cmp(1, 0, 1)
+        sum_d(0)
+        sum_c(0, 0)
+        sum_c(0, 1)
+        mm(v("pT", 0, 40), m128, v("Rc"), True, False)
+        mm(v("pT", 24, 40), m128, v("Rd"), False, False)
+        cmp(1, 1, 0)
+        cmp(1, 1, 1)
+        sum_c(1, 0)
+        sum_c(1, 1)
+        act(v("zw", 0, 128), v("pD0", 128, 256))
+        for j in range(2):
+            cmp(1, 2, j)
+            sum_c(2, j)
+        sum_d(1)
+        act(v("DkS"), v("pK", 0, 128))
+        act(v("nE"), ind(v("D", 0, 512), v("ce")), scale=-1.0)
+        for j in range(2):
+            cmp(1, 3, j)
+            sum_c(3, j)
+        mm(v("pD0", 0, 128), I, v("half"), True, False)
+        mm(v("pA", 0, 128), v("If"), v("nE"), True, False)
+        mm(v("pA", 0, 64), v("If"), Plo, False, False)
+        mm(v("pA", 64, 128), v("If"), Phi, False, True)
+        mm(v("pK", 128, 136), m128, v("Rc", 0, 8), True, False)
+        mm(v("pD1", 0, 8), m128, v("Re", 8, 16), True, False)
+        mm(v("pD1", 0, 4), I, Llo, False, False)
+        mm(v("pD1", 4, 8), I, Lhi, False, False)
+        mm(v("pS", 384, 512), I, v("cq"), True, False)
+
+        made(2)
+        tt(v("key"), v("pL", 0, 128), v("DkS"), ALU.max)
+        made(3)
+        act(v("okT"), v("key"), AF.Sign, bias=BIG - 0.5, scale=-1.0)
+        act(v("zw", 128, 256), z, scale=0.5)
+        scan(v("ms"), v("rmin", 0, 128), v("key"), ALU.max, ALU.min)
+        mm(v("pD0", 0, 128), v("okT"), v("hI"), False, True)
+        act(v("okN"), v("pD0", 0, 128))
+        act(v("zw", 256, 384), z, scale=-1.0)
+        act(W(3 * S, 3 * S + 128), Qa)
+        if s == 0:
+            late_constants(2)
+        mm(v("pL", 128, 200), I, v("m2", b, b + 72), True, False)
+        mm(v("pL", 200, 272), I, v("m2", b + 200, b + 272), False, False)
+        mm(v("pL", 132, 136), I, v("shift", 16 * s, 16 * s + 4), False, False)
+        mm(v("pL", 264, 268), I, v("shift", 16 * s, 16 * s + 4), False, False)
+        scan(v("ns"), v("rmax", 0, 128), v("okT"), ALU.mult, ALU.add)
+        cp(v("wi"), v("ms", 15, 128, 16))
+        ts(v("wj", 8, 16), v("ns", 15, 128, 16), 1.0 / 12.0, ALU.mult, 6.5 / 6.0, ALU.add)
+        ts(v("wj", 0, 8), v("wi"), 15, ALU.bitwise_and)
+        tt(v("lb"), ind(v("wj"), v("bo")), v("mask"), ALU.mult)
+        lk = v("lb", 128, 256)
+        mm(v("pT", 0, 8), v("lb", 0, 128), Dq, False, False)
+        mm(v("pT", 8, 40), lk, v("Rk"), False, True)
+        mm(v("pD1", 0, 8), lk, C("4"), False, False)
+        mm(v("pL", 132, 136), lk, C("h", 0, 4), False, False)
+        mm(v("pL", 264, 268), lk, C("h", 4, 8), False, False)
+        mm(v("pD0", 0, 128), I, v("cq"), True, False)
+        tt(v("pA", 0, 128), v("pA", 0, 128), v("okN"), ALU.mult)
+        cp(v("of"), v("pT", 0, 40))
+        act(v("kN"), ind(v("kwin"), v("of", 8, 16)))
+        act(v("zs"), ind(v("zw"), v("of", 16, 24)))
+        mm(v("pL", 136, 264), I, v("kN"), False, True)
+        mm(v("pS", 384, 512), I, v("zs"), False, False)
+        tt(W(S, S + 64), Plo, v("pA", 0, 64), ALU.subtract)
+        tt(W(S + 64, S + 128), Phi, v("pA", 64, 128), ALU.subtract)
+        if not last:
+            cp(v("o1", 128 * s, 128 * s + 128), ind(W(), v("of", 28, 36)))
+            send(1, s)
+        tt(v("tb"), ind(v("xx"), v("of", 0, 8)), v("kN"), ALU.mult)
+        act(v("fa"), v("pL", 128, 272), AF.Abs, bias=v("cb", s, s + 1))
+        act(v("o2", b, b + 72), v("fa", 0, 72), AF.Sign, bias=-1.0)
+        zn = v("o2", b + 72, b + 200)
+        if OPT["pm"]:
+            mm(v("pS", 384, 512), I, v("tb"), False, False)
+            mm(v("pS", 384, 512), I, v("cM"), False, True)
+            act(zn, v("pS", 384, 512), AF.Abs, bias=-MAGIC)
+        else:
+            mm(v("pS", 384, 512), I, v("tb"), False, True)
+            act(v("t3"), v("pS", 384, 512), bias=MAGIC)
+            act(zn, v("t3"), AF.Abs, bias=-MAGIC)
+        act(v("o2", b + 200, b + 272), v("fa", 72, 144), AF.Sign, bias=-1.0)
+        if not last:
+            send(2, s)
+        act(v("o3", 256 * s, 256 * s + 256), ind(W(), v("of", 24, 40)))
+        if not last:
+            send(3, s)
+        else:
+            dma("S", T.yz[:], zn)
+            dma("S", T.yq[:], v("o3", 256 * s + 64, 256 * s + 192))
+            dma("S", T.yp[:, 0:64], v("o3", 256 * s, 256 * s + 64))
+            dma("S", T.yp[:, 64:128], v("o3", 256 * s + 192, 256 * s + 256))
+        mm(v("pS", 0, 16), zn, v("W2"))
+        mm(v("pD0", 0, 128), v("hI"), zn, False, False)
+        if last:
+            mm(v("pT", 0, 64, p=slice(0, 8)), C("rs"), v("o2", b + 8, b + 72))
+            mm(v("pT", 64, 128, p=slice(0, 8)), C("rs"), v("o2", b + 200, b + 264))
+            act(v("sS", p=slice(0, 8)), v("pT", 0, 128, p=slice(0, 8)), bias=4.5)
+            dma("S", T.ys[:], v("sS", p=slice(0, 8)))
+        cp(v("vi"), v("pS", 0, 16))
+        ts(v("vj"), v("vi"), 31, ALU.bitwise_and)
+        tt(v("lv", 0, 128), ind(v("vj"), bo8), m128, ALU.mult)
+        mm(v("pK", 128, 136), v("lv", 0, 128), C("h"), False, True)
+        tt(v("lv", 128, 256), ind(v("vj"), v("bo", 8, 16)), m128, ALU.mult)
+        mm(v("pD1", 0, 8), v("lv", 128, 256), C("vb"), False, True)
+        cp(v("oo"), v("pK", 128, 136))
+        if OPT["xa"]:
+            act(v("xo"), ind(Xw, v("oo")))
+            mm(v("pD0", 0, 128), v("hI"), v("xo"), False, False)
+            mm(v("pD0", 0, 128), I, v("cM"), False, True)
+            act(v("xo", 0, 128), v("pD0", 0, 128), bias=-MAGIC)
+            ts(v("od"), v("pD1", 0, 8), -128.0, ALU.mult, 1152.0, ALU.add)
+            cp(ind(v("D"), v("od")), P1)
+            if last:
+                dma("S", T.yd[:], v("D", 0, 512))
+            cp(ind(Xw, v("oo")), v("xo"))
+            if last:
+                dma("A", T.yx[:], Xw)
+        else:
+            mm(v("pD0", 0, 128), I, v("cM"), False, True)
+            tt(v("t1"), ind(Xw, v("oo")), zn, ALU.add)
+            ts(v("od"), v("pD1", 0, 8), -128.0, ALU.mult, 1152.0, ALU.add)
+            ts(v("xn"), v("t1"), 0.5, ALU.mult, -0.25, ALU.add)
+            cp(ind(Xw, v("oo")), v("xn"))
+            if last:
+                dma("A", T.yx[:], Xw)
+            cp(ind(v("D"), v("od")), P1)
+            if last:
+                dma("S", T.yd[:], v("D", 0, 512))
+
+    def meet(r1, r2):
+        for x in r1:
+            for y in r2:
+                if x[0] == y[0] and x[1] & y[1]:
+                    return True
+        return False
+
+    def lane(o):
+        return o[0] if o[4] is None else o[4][0]
+
+    bk = [set(x[0] for x in o[2] + o[3] if SCRATCH[x[0]][0] == "psum") for o in ops]
+    touched = {}
+    known = {q: {} for q in Q}
+    clock, waits = [], []
+    for j, o in enumerate(ops):
+        best = {}
+        names = set(x[0] for x in o[2] + o[3])
+        for i in set(i for nm in names for i in touched.get(nm, [])):
+            e = ops[i]
+            if best.get(lane(e), -1) > i:
+                continue
+            same = e[0] == o[0] and e[4] is None and o[4] is None
+            if same and o[0] == "P":
+                continue
+            if meet(e[3], o[2]) or meet(e[3], o[3]) or meet(e[2], o[3]) or (not same and bk[i] & bk[j]):
+                best[lane(e)] = i
+        for nm in names:
+            touched.setdefault(nm, []).append(j)
+        k = known.get(o[0], {})
+        w = []
+        for i in sorted(best.values(), reverse=True):
+            if k.get(lane(ops[i]), -1) < i:
+                w.append(i)
+                for kk, vv in clock[i].items():
+                    if k.get(kk, -1) < vv:
+                        k[kk] = vv
+        waits.append(w)
+        c = dict(k)
+        c[lane(o)] = j
+        clock.append(c)
+    needed = set(i for w in waits for i in w)
+    count = {q: 0 for q in Q}
+    token = {}
+    for j, o in enumerate(ops):
+        if o[4] is not None:
+            token[j] = o[4][:2]
+        elif j in needed:
+            count[o[0]] += 1
+            token[j] = ("e" + o[0], count[o[0]])
+    top = {}
+    for j, o in enumerate(ops):
+        if j in token:
+            top[token[j][0]] = max(top.get(token[j][0], 0), token[j][1])
+        if o[0] == "X":
+            continue
+        e = Q[o[0]]
+        for i in waits[j]:
+            e.wait_ge(T.sem[token[i][0]], token[i][1])
+        inst = o[1](e)
+        if o[4] is None:
+            if j in token:
+                inst.then_inc(T.sem[token[j][0]], 1)
+        elif o[4][2] == "dma":
+            inst.then_inc(T.sem[o[4][0]], 16)
+    for name in sorted(top):
+        if name[0] != "e":
+            g.wait_ge(T.sem[name], top[name])

@@ -3,7 +3,7 @@ from concourse.mybir import AluOpType as ALU, AxisListType as AX, ActivationFunc
 
 WT = [37, 101, 59, 203, 83, 149, 11, 173, 67, 229, 127, 43, 191, 23, 251, 109]
 STEPS = 4
-OPT = {"vy": 16, "vx": 0, "bp": 0, "pm": 1, "e": 1, "early": 0, "early0": 0, "xa": 0, "ubp": 0}
+OPT = {"vy": 20, "vx": 0, "bp": 0, "pm": 1, "e": 0, "early": 0, "early0": 0, "d1": 1, "mp": 0, "gc": 1, "ubp": 1}
 S = 192
 WW = 704
 MW = 272
@@ -28,8 +28,8 @@ SCRATCH = {
     "Dq": _sb(8, "b"), "W8": _sb(16, "b"), "R8": _sb(16, "b"), "C": _sb(128, "b"), "W2": _sb(16, "b"),
     "Rk": _sb(32, "b"), "Rc": _sb(40, "b"), "Rd": _sb(16, "b"), "Re": _sb(16, "b"), "RL": _sb(128, "b"),
     "kwin": _sb(8, "f"), "cb": _sb(8, "f"), "cs": _sb(8, "f"), "shift": _sb(64, "b"),
-    "ri": _sb(16, "i"), "rt": _sb(16, "i"), "lr": _sb(256, "b"), "ce": _sb(8, "u"), "E": _sb(128, "u"), "nE": _sb(128, "f"),
-    "okN": _sb(128, "b"), "xo": _sb(128, "b"),
+    "ri": _sb(16, "i"), "rt": _sb(16, "i"), "lr": _sb(256, "b"), "ce": _sb(8, "u"), "E": _sb(128, "u"), "dEP": _sb(128, "f"),
+    "kb": _sb(16, "b"), "kT": _sb(128, "b"),
     "uw": _sb(8, "f"), "ub": _sb(128, "f"), "u1": _sb(128, "i"), "u2": _sb(128, "i"), "eT": _sb(512, "b"),
     "zw": _sb(384, "b"), "zs": _sb(128, "b"), "DkS": _sb(128, "f"), "key": _sb(128, "f"), "ms": _sb(128, "f"),
     "okT": _sb(128, "b"), "ns": _sb(128, "b"),
@@ -117,6 +117,9 @@ def rank_program(g, core, T, topo):
         else:
             add("G", lambda e: e.iota(a_(out), pat, base, cm), out, [])
 
+    def gcopy(out, x):
+        add("G", lambda e: e.affine_select(a_(out), a_(x), [[0, 128]], ALU.is_ge, 0.0, 0, 0), out, [x])
+
     nd = [0]
 
     def dma(q, out, x):
@@ -177,6 +180,8 @@ def rank_program(g, core, T, topo):
     fill(v("rmax"), 1.0)
     ts(v("A2"), v("A2"), 4, ALU.arith_shift_right)
     fill(v("rmin"), 0.0)
+    for name, c in (("c30", 30.5 * BIG), ("half", 0.5), ("cq", -0.25), ("cM", MAGIC)):
+        fill(v(name), c)
     ts(Dq, v("A2"), 0.0, ALU.is_equal)
     ts(v("A1"), v("A1"), 15, ALU.bitwise_and)
     fill(v("rmax", 0, 512, 16), 0.0)
@@ -226,8 +231,6 @@ def rank_program(g, core, T, topo):
     act(v("cb", 0, 4), v("mask", 2, 6), scale=-0.75, bias=v("col", 6, 7))
     act(v("If"), v("I"))
     act(v("cs", 0, 4), v("cb", 0, 4), scale=-1.0, bias=-0.75)
-    for name, c in (("c30", 30.5 * BIG), ("half", 0.5), ("cq", -0.25), ("cM", MAGIC)):
-        act(v(name), v("I"), scale=0.0, bias=c)
     act(v("RL"), ind(v("R8", 0, 8), bo8))
     act(v("shift"), ind(v("cs", 0, 4), v("bo", 0, 4)))
 
@@ -246,6 +249,8 @@ def rank_program(g, core, T, topo):
     LO, HI = slice(0, 64), slice(64, 128)
     I, m128 = v("I"), v("mask", 0, 128)
     Xw = v("X")
+    later = []
+    PE = "pK" if OPT["bp"] else "pA"
     DB = (("pD0", "pD1"), ("pT", "pS"))
 
     for s in range(STEPS):
@@ -305,6 +310,8 @@ def rank_program(g, core, T, topo):
                 mm(v("pK", 0, 128), I, v("krow"), True, False)
             elif part == 2:
                 ts(v("u2"), v("u1"), 5, ALU.arith_shift_right, 2047, ALU.bitwise_and)
+            elif OPT["gc"]:
+                gcopy(W(0, 128), v("u2"))
             else:
                 cp(W(0, 128), v("u2"))
 
@@ -324,13 +331,11 @@ def rank_program(g, core, T, topo):
 
         vy, vx = (OPT["vy"] if s else 0), OPT["vx"]
         early = OPT["early"] if s else OPT["early0"]
-        if vy:
+        if vy and OPT["e"] == 1:
             gy(0, vy, "V")
         for q in range(4 - early):
             if 32 * q + 32 > vy:
                 gy(max(32 * q, vy), 32 * q + 32)
-        if s > 0 and OPT["e"] < 2:
-            sc_hi(0)
         mm(v("pS", 0, 8), z, v("W8", 0, 8))
         if s == 0:
             mm(v("pS", 8, 16, p=LO), Flo, C("sel0"))
@@ -341,22 +346,37 @@ def rank_program(g, core, T, topo):
             cp(Llo, v("pT", 0, 4))
             cp(Lhi, v("pT", 4, 8))
         else:
-            if OPT["e"] < 2:
-                sc_lo(0)
             cp(v("ri", 0, 8), v("pS", 0, 8))
+            if OPT["e"] == 0:
+                gy(0, vy, "V")
+            else:
+                cp(ind(v("D"), v("od")), later.pop())
         mm(v("pS", 16, 20), I, Llo, True, False)
         mm(v("pS", 20, 24), I, Lhi, False, False)
+        dz(0, 0)
+        mm(v("pL", 0, 128), I, v("c30"), True, False)
+        mm(v("pL", 0, 128, p=LO), Flo, v("RL"), False, False)
         ts(v("rt", 0, 8), v("ri", 0, 8), 4095, ALU.bitwise_and)
+        if s > 0 and OPT["e"] == 0:
+            cp(ind(v("D"), v("od")), later.pop())
+        elif s > 0:
+            sc_hi(0)
         ts(v("rt", 8, 16), v("rt", 0, 8), 2741.0, ALU.mult)
         ts(v("uw"), v("rt", 0, 8), 32.0, ALU.add)
+        if s > 0 and OPT["e"] == 0:
+            sc_hi(0)
         ts(v("vj", 0, 8), v("rt", 8, 16), 5, ALU.arith_shift_right, 255, ALU.bitwise_and)
+        if s > 0:
+            sc_lo(0)
         tt(v("lr", 0, 128), ind(v("vj", 0, 8), bo8), m128, ALU.mult)
         mm(v("pS", 16, 24), v("lr", 0, 128), C("128th"), False, True)
         if s == 0:
             late_constants(0)
-        elif OPT["e"] < 2:
+        else:
             sc_hi(1)
         ts(v("ce"), v("pS", 16, 24), 128.0, ALU.mult, 128.0, ALU.add)
+        if s > 0:
+            sc_lo(1)
         cp(v("E"), ind(v("D", 0, 512), v("ce")))
         if s == 0:
             late_constants(1)
@@ -365,133 +385,117 @@ def rank_program(g, core, T, topo):
         for q in range(4 - early, 4):
             gy(32 * q, 32 * q + 32)
         gx(64, 128)
-        if s == 0 or OPT["e"] == 2:
+        if s == 0:
             sc_hi(0)
             sc_lo(0)
             sc_hi(1)
-        sc_lo(1)
-        bcast(0, 0)
-        if early < 2:
-            sc_hi(2)
-        bcast(0, 1)
-        bcast(0, 2)
-        mm(v("pL", 0, 128), I, v("c30"), True, False)
-        mm(v("pL", 0, 128, p=LO), Flo, v("RL"), False, False)
+            sc_lo(1)
+        sc_hi(2)
         mm(v("pL", 0, 128, p=HI), Fhi, v("RL"), False, False)
-        dz(0, 0)
+        bcast(0, 0)
         dz(0, 1)
         mm(v("pK", 256, 384), v("ub"), v("If"))
-        if early < 2:
-            sc_lo(2)
-        if not early:
-            sc_hi(3)
-            sc_lo(3)
-            bcast(1, 0)
-            bcast(1, 1)
-            bcast(1, 2)
-        made(0)
-        made(1)
+        dz(1, 0)
+        dz(1, 1)
+        sc_lo(2)
+        gcopy(W(3 * S, 3 * S + 128), Qa)
+        sc_hi(3)
+        if OPT["mp"] == 0:
+            made(0)
+        sc_lo(3)
+        made(1 - OPT["mp"])
         if vx:
             gx(0, vx, "V")
 
         dx(0, 0)
         dx(0, 1)
-        dz(1, 0)
-        dz(1, 1)
+        bcast(1, 0)
         for m in range(4):
             cmp(0, m, 0)
+            if m + 2 - OPT["mp"] < 4:
+                made(m + 2 - OPT["mp"])
             cmp(0, m, 1)
-            if early == 2 and m == 1:
-                sc_hi(2)
-                sc_lo(2)
-            if early and m == early:
-                sc_hi(3)
-                sc_lo(3)
-                bcast(1, 0)
-            if early and m == early + 1:
-                bcast(1, 1)
-                bcast(1, 2)
         dx(1, 0)
         dx(1, 1)
         absd(0, 0)
-        absd(1, 0)
-        mm(v("pD0", 128, 256), I, z, True, False)
-        mm(v("pD0", 128, 256), v("nI"), v("hs", 15, 2048, 16), False, True)
         absd(0, 1)
+        absd(1, 0)
         absd(1, 1)
         cmp(1, 0, 0)
         cmp(1, 0, 1)
-        sum_d(0)
         sum_c(0, 0)
         sum_c(0, 1)
-        mm(v("pT", 0, 40), m128, v("Rc"), True, False)
-        mm(v("pT", 24, 40), m128, v("Rd"), False, False)
+        sum_d(0)
         cmp(1, 1, 0)
         cmp(1, 1, 1)
         sum_c(1, 0)
         sum_c(1, 1)
-        act(v("zw", 0, 128), v("pD0", 128, 256))
+        act(v("zw", 128, 256), z, scale=0.5)
+        act(v("zw", 256, 384), z, scale=-1.0)
+        if OPT["d1"]:
+            sum_d(1)
         for j in range(2):
             cmp(1, 2, j)
             sum_c(2, j)
-        sum_d(1)
+        if not OPT["d1"]:
+            sum_d(1)
         act(v("DkS"), v("pK", 0, 128))
-        act(v("nE"), ind(v("D", 0, 512), v("ce")), scale=-1.0)
         for j in range(2):
             cmp(1, 3, j)
             sum_c(3, j)
         mm(v("pD0", 0, 128), I, v("half"), True, False)
-        mm(v("pA", 0, 128), v("If"), v("nE"), True, False)
-        mm(v("pA", 0, 64), v("If"), Plo, False, False)
-        mm(v("pA", 64, 128), v("If"), Phi, False, True)
-        mm(v("pK", 128, 136), m128, v("Rc", 0, 8), True, False)
+        mm(v("pT", 0, 40), m128, v("Rc"), True, False)
+        mm(v("pT", 24, 40), m128, v("Rd"), False, False)
+        mm(v("pA", 0, 128), I, z, True, False)
+        mm(v("pA", 0, 128), v("nI"), v("hs", 15, 2048, 16), False, True)
+
+        tt(v("dEP", 0, 64), ind(v("D", 0, 512), v("ce", 0, 4)), Plo, ALU.subtract)
+        tt(v("dEP", 64, 128), ind(v("D", 0, 512), v("ce", 4, 8)), Phi, ALU.subtract)
+        tt(v("key"), v("pL", 0, 128), v("DkS"), ALU.max)
+        act(v("okT"), v("key"), AF.Sign, bias=BIG - 0.5, scale=-1.0)
+        scan(v("ms"), v("rmin", 0, 128), v("key"), ALU.max, ALU.min)
+        mm(v("pD0", 0, 128), v("okT"), v("hI"), False, True)
+        act(v("zw", 0, 128), v("pA", 0, 128))
+        if not OPT["gc"]:
+            act(W(3 * S, 3 * S + 128), Qa)
+        if s == 0:
+            late_constants(2)
+        mm(v("pK", 384, 392), m128, v("Rc", 0, 8), True, False)
         mm(v("pD1", 0, 8), m128, v("Re", 8, 16), True, False)
         mm(v("pD1", 0, 4), I, Llo, False, False)
         mm(v("pD1", 4, 8), I, Lhi, False, False)
         mm(v("pS", 384, 512), I, v("cq"), True, False)
-
-        made(2)
-        tt(v("key"), v("pL", 0, 128), v("DkS"), ALU.max)
-        made(3)
-        act(v("okT"), v("key"), AF.Sign, bias=BIG - 0.5, scale=-1.0)
-        act(v("zw", 128, 256), z, scale=0.5)
-        scan(v("ms"), v("rmin", 0, 128), v("key"), ALU.max, ALU.min)
-        mm(v("pD0", 0, 128), v("okT"), v("hI"), False, True)
-        act(v("okN"), v("pD0", 0, 128))
-        act(v("zw", 256, 384), z, scale=-1.0)
-        act(W(3 * S, 3 * S + 128), Qa)
-        if s == 0:
-            late_constants(2)
         mm(v("pL", 128, 200), I, v("m2", b, b + 72), True, False)
         mm(v("pL", 200, 272), I, v("m2", b + 200, b + 272), False, False)
         mm(v("pL", 132, 136), I, v("shift", 16 * s, 16 * s + 4), False, False)
         mm(v("pL", 264, 268), I, v("shift", 16 * s, 16 * s + 4), False, False)
-        scan(v("ns"), v("rmax", 0, 128), v("okT"), ALU.mult, ALU.add)
         cp(v("wi"), v("ms", 15, 128, 16))
-        ts(v("wj", 8, 16), v("ns", 15, 128, 16), 1.0 / 12.0, ALU.mult, 6.5 / 6.0, ALU.add)
+        scan(v("ns"), v("rmax", 0, 128), v("okT"), ALU.mult, ALU.add)
         ts(v("wj", 0, 8), v("wi"), 15, ALU.bitwise_and)
+        ts(v("wj", 8, 16), v("ns", 15, 128, 16), 1.0 / 12.0, ALU.mult, 6.5 / 6.0, ALU.add)
+        ts(v("kb", 0, 8), v("ns", 15, 128, 16), 1.0 / 12.0, ALU.mult, 160 + 6.5 / 6.0, ALU.add)
+        act(v("kT"), ind(v("kb", 0, 8), bo8), scale=0.5, bias=-80.0)
         tt(v("lb"), ind(v("wj"), v("bo")), v("mask"), ALU.mult)
+        mm(v("pB", 0, 128), v("kT"), I)
+        act(v("kN"), v("pB", 0, 128))
         lk = v("lb", 128, 256)
         mm(v("pT", 0, 8), v("lb", 0, 128), Dq, False, False)
         mm(v("pT", 8, 40), lk, v("Rk"), False, True)
         mm(v("pD1", 0, 8), lk, C("4"), False, False)
         mm(v("pL", 132, 136), lk, C("h", 0, 4), False, False)
         mm(v("pL", 264, 268), lk, C("h", 4, 8), False, False)
-        mm(v("pD0", 0, 128), I, v("cq"), True, False)
-        tt(v("pA", 0, 128), v("pA", 0, 128), v("okN"), ALU.mult)
-        cp(v("of"), v("pT", 0, 40))
-        act(v("kN"), ind(v("kwin"), v("of", 8, 16)))
-        act(v("zs"), ind(v("zw"), v("of", 16, 24)))
+        tt(v("pD0", 0, 128), v("pD0", 0, 128), v("dEP"), ALU.mult)
         mm(v("pL", 136, 264), I, v("kN"), False, True)
+        cp(v("of"), v("pT", 0, 40))
+        act(v("zs"), ind(v("zw"), v("of", 16, 24)))
         mm(v("pS", 384, 512), I, v("zs"), False, False)
-        tt(W(S, S + 64), Plo, v("pA", 0, 64), ALU.subtract)
-        tt(W(S + 64, S + 128), Phi, v("pA", 64, 128), ALU.subtract)
+        tt(W(S, S + 64), v("pD0", 0, 64), Plo, ALU.add)
+        tt(W(S + 64, S + 128), v("pD0", 64, 128), Phi, ALU.add)
+        tt(v("tb"), ind(v("xx"), v("of", 0, 8)), v("kN"), ALU.mult)
         if not last:
             cp(v("o1", 128 * s, 128 * s + 128), ind(W(), v("of", 28, 36)))
             send(1, s)
-        tt(v("tb"), ind(v("xx"), v("of", 0, 8)), v("kN"), ALU.mult)
         act(v("fa"), v("pL", 128, 272), AF.Abs, bias=v("cb", s, s + 1))
-        act(v("o2", b, b + 72), v("fa", 0, 72), AF.Sign, bias=-1.0)
         zn = v("o2", b + 72, b + 200)
         if OPT["pm"]:
             mm(v("pS", 384, 512), I, v("tb"), False, False)
@@ -501,6 +505,7 @@ def rank_program(g, core, T, topo):
             mm(v("pS", 384, 512), I, v("tb"), False, True)
             act(v("t3"), v("pS", 384, 512), bias=MAGIC)
             act(zn, v("t3"), AF.Abs, bias=-MAGIC)
+        act(v("o2", b, b + 72), v("fa", 0, 72), AF.Sign, bias=-1.0)
         act(v("o2", b + 200, b + 272), v("fa", 72, 144), AF.Sign, bias=-1.0)
         if not last:
             send(2, s)
@@ -513,7 +518,6 @@ def rank_program(g, core, T, topo):
             dma("S", T.yp[:, 0:64], v("o3", 256 * s, 256 * s + 64))
             dma("S", T.yp[:, 64:128], v("o3", 256 * s + 192, 256 * s + 256))
         mm(v("pS", 0, 16), zn, v("W2"))
-        mm(v("pD0", 0, 128), v("hI"), zn, False, False)
         if last:
             mm(v("pT", 0, 64, p=slice(0, 8)), C("rs"), v("o2", b + 8, b + 72))
             mm(v("pT", 64, 128, p=slice(0, 8)), C("rs"), v("o2", b + 200, b + 264))
@@ -522,33 +526,20 @@ def rank_program(g, core, T, topo):
         cp(v("vi"), v("pS", 0, 16))
         ts(v("vj"), v("vi"), 31, ALU.bitwise_and)
         tt(v("lv", 0, 128), ind(v("vj"), bo8), m128, ALU.mult)
-        mm(v("pK", 128, 136), v("lv", 0, 128), C("h"), False, True)
+        mm(v("pK", 384, 392), v("lv", 0, 128), C("h"), False, True)
         tt(v("lv", 128, 256), ind(v("vj"), v("bo", 8, 16)), m128, ALU.mult)
         mm(v("pD1", 0, 8), v("lv", 128, 256), C("vb"), False, True)
-        cp(v("oo"), v("pK", 128, 136))
-        if OPT["xa"]:
-            act(v("xo"), ind(Xw, v("oo")))
-            mm(v("pD0", 0, 128), v("hI"), v("xo"), False, False)
-            mm(v("pD0", 0, 128), I, v("cM"), False, True)
-            act(v("xo", 0, 128), v("pD0", 0, 128), bias=-MAGIC)
-            ts(v("od"), v("pD1", 0, 8), -128.0, ALU.mult, 1152.0, ALU.add)
-            cp(ind(v("D"), v("od")), P1)
-            if last:
-                dma("S", T.yd[:], v("D", 0, 512))
-            cp(ind(Xw, v("oo")), v("xo"))
-            if last:
-                dma("A", T.yx[:], Xw)
-        else:
-            mm(v("pD0", 0, 128), I, v("cM"), False, True)
-            tt(v("t1"), ind(Xw, v("oo")), zn, ALU.add)
-            ts(v("od"), v("pD1", 0, 8), -128.0, ALU.mult, 1152.0, ALU.add)
-            ts(v("xn"), v("t1"), 0.5, ALU.mult, -0.25, ALU.add)
-            cp(ind(Xw, v("oo")), v("xn"))
-            if last:
-                dma("A", T.yx[:], Xw)
-            cp(ind(v("D"), v("od")), P1)
-            if last:
-                dma("S", T.yd[:], v("D", 0, 512))
+        cp(v("oo"), v("pK", 384, 392))
+        tt(v("t1"), ind(Xw, v("oo")), zn, ALU.add)
+        ts(v("od"), v("pD1", 0, 8), -128.0, ALU.mult, 1152.0, ALU.add)
+        ts(v("xn"), v("t1"), 0.5, ALU.mult, -0.25, ALU.add)
+        cp(ind(Xw, v("oo")), v("xn"))
+        if last:
+            dma("A", T.yx[:], Xw)
+        later.append(P1)
+        if last:
+            cp(ind(v("D"), v("od")), later.pop())
+            dma("S", T.yd[:], v("D", 0, 512))
 
     def meet(r1, r2):
         for x in r1:

@@ -3,11 +3,14 @@ from concourse.mybir import AluOpType as ALU, AxisListType as AX, ActivationFunc
 
 WT = [37, 101, 59, 203, 83, 149, 11, 173, 67, 229, 127, 43, 191, 23, 251, 109]
 STEPS = 4
-OPT = {"vy": 20, "vx": 0, "bp": 0, "pm": 1, "e": 0, "early": 0, "early0": 0, "d1": 1, "mp": 0, "gc": 1, "ubp": 1}
-S = 192
-WW = 704
-MW = 272
-BIG = 65536.0
+OPT = {"lv": 0, "epos": 2, "y0": 16, "vy": 20, "cuts": [48, 80, 104], "nsg": 0, "zlate": 0, "okv": 0, "okn": 0, "si": 0,
+       "ord": "hHccaAccbccBpqccmekrnNPswxjKFlyfzogOVZt", "rounds": 2, "vx": 24,
+       "cost": {"cyc": 0.9, "fix": 25, "least": 55, "pe": 0.68, "gather": 1.3, "scatter": 2.5, "dma": 900, "byte": 0.43,
+                "issue": 350, "fly": 1700, "hop": 150}}
+COST = OPT["cost"]
+S = 256
+ZS = 2576
+ZH = 272
 MAGIC = 12582912.0
 
 
@@ -17,34 +20,30 @@ def _sb(cols, dt):
 
 SCRATCH = {
     "X": _sb(2048, "b"), "Di": _sb(512, "i"), "D": _sb(1536, "f"),
-    "yy": _sb(2048, "b"), "xx": _sb(2048, "b"), "hs": _sb(2048, "b"), "ls": _sb(2048, "b"),
+    "yy": _sb(2048, "b"), "xx": _sb(2048, "b"), "ls": _sb(2048, "b"),
     "aa": _sb(2048, "b"), "bb": _sb(2048, "b"), "ad": _sb(2048, "b"),
-    "W": _sb(STEPS * WW, "f"), "PQi": _sb(256, "i"), "Fi": _sb(128, "i"),
-    "m1": _sb(512, "u"), "m2": _sb(STEPS * MW, "b"), "o1": _sb(384, "u"), "o2": _sb(STEPS * MW, "b"), "o3": _sb(1024, "f"),
-    "A1": _sb(256, "i"), "A2": _sb(8, "i"), "A3": _sb(16, "i"), "A4": _sb(128, "b"), "mask": _sb(256, "b"), "bo": _sb(16, "u"),
-    "col": _sb(8, "f"), "wrow": _sb(16, "f"), "I": _sb(128, "b"), "nI": _sb(128, "b"), "hI": _sb(128, "b"), "If": _sb(128, "f"),
-    "krow": _sb(128, "b"), "c30": _sb(128, "b"), "half": _sb(128, "b"), "cq": _sb(128, "b"), "cM": _sb(128, "b"),
-    "rmax": _sb(512, "b"), "rmin": _sb(512, "b"),
-    "Dq": _sb(8, "b"), "W8": _sb(16, "b"), "R8": _sb(16, "b"), "C": _sb(128, "b"), "W2": _sb(16, "b"),
-    "Rk": _sb(32, "b"), "Rc": _sb(40, "b"), "Rd": _sb(16, "b"), "Re": _sb(16, "b"), "RL": _sb(128, "b"),
-    "kwin": _sb(8, "f"), "cb": _sb(8, "f"), "cs": _sb(8, "f"), "shift": _sb(64, "b"),
-    "ri": _sb(16, "i"), "rt": _sb(16, "i"), "lr": _sb(256, "b"), "ce": _sb(8, "u"), "E": _sb(128, "u"), "dEP": _sb(128, "f"),
-    "kb": _sb(16, "b"), "kT": _sb(128, "b"),
-    "uw": _sb(8, "f"), "ub": _sb(128, "f"), "u1": _sb(128, "i"), "u2": _sb(128, "i"), "eT": _sb(512, "b"),
-    "zw": _sb(384, "b"), "zs": _sb(128, "b"), "DkS": _sb(128, "f"), "key": _sb(128, "f"), "ms": _sb(128, "f"),
-    "okT": _sb(128, "b"), "ns": _sb(128, "b"),
-    "wi": _sb(8, "i"), "wj": _sb(16, "i"), "lb": _sb(256, "b"), "of": _sb(40, "u"), "kN": _sb(128, "b"),
-    "tb": _sb(128, "b"), "t1": _sb(128, "f"), "t3": _sb(128, "f"), "fa": _sb(144, "f"),
-    "vi": _sb(16, "i"), "vj": _sb(16, "i"), "lv": _sb(256, "b"), "oo": _sb(8, "u"), "od": _sb(8, "u"),
-    "xn": _sb(128, "i"), "sS": _sb(128, "f"),
+    "Z": _sb(STEPS * ZS + 16, "b"), "W": _sb(3 * S + 128, "i"), "Fi": _sb(128, "i"), "zl": _sb(128, "b"),
+    "m1": _sb(256 * STEPS, "u"), "o1": _sb(256 * STEPS, "u"), "o2": _sb(512 * STEPS, "b"),
+    "m3": _sb(8 * STEPS, "u"), "o3": _sb(16 * STEPS, "u"), "pq": _sb(256, "f"),
+    "A1": _sb(32, "i"), "A2": _sb(8, "i"), "A3": _sb(16, "i"), "m16": _sb(16, "b"), "mask": _sb(256, "b"),
+    "bo": _sb(16, "u"), "bx": _sb(16, "u"), "col": _sb(8, "f"), "wrow": _sb(16, "f"), "mul": _sb(16, "f"),
+    "rmax": _sb(512, "b"), "rmin": _sb(512, "b"), "cM": _sb(256, "b"),
+    "Dq": _sb(8, "b"), "C": _sb(320, "b"),
+    "E": _sb(128, "u"), "dEP": _sb(128, "f"), "u1": _sb(128, "i"), "u2": _sb(128, "i"),
+    "okT": _sb(128, "b"), "okN": _sb(128, "b"), "ms": _sb(128, "f"), "wi": _sb(8, "i"), "wj": _sb(8, "i"),
+    "lb": _sb(128, "b"), "lk": _sb(128, "b"), "of": _sb(16, "u"), "ob": _sb(8, "u"), "tb": _sb(128, "b"), "zt": _sb(128, "b"),
+    "zw": _sb(2 * S + 128, "b"), "DkS": _sb(128, "f"), "key": _sb(128, "f"), "MB": _sb(128, "b"), "mi": _sb(128, "i"),
+    "oS": _sb(128, "f"), "oo": _sb(8, "u"), "vi": _sb(16, "i"), "vj": _sb(16, "i"), "lv": _sb(256, "b"),
+    "t1": _sb(128, "f"), "xn": _sb(128, "i"), "sS": _sb(128, "f"),
 }
-for _n in ("pA", "pB"):
-    SCRATCH[_n] = ("psum", [128, 1024], "bfloat16") if OPT["bp"] else ("psum", [128, 512], "float32")
-for _n in ("pD0", "pD1", "pL", "pK", "pS", "pT"):
+for _n in ("one", "I", "nI", "hI", "nBI", "B", "Wp", "Wn", "RLp", "RLn", "Bk", "Bf", "cf", "krow", "c15", "cq", "half",
+           "M16", "M4k", "c2k", "c32", "r16", "nm"):
+    SCRATCH[_n] = _sb(128, "b")
+for _n in ("pA", "pB", "pD0", "pD1", "pD2", "pD3", "pL", "pK"):
     SCRATCH[_n] = ("psum", [128, 512], "float32")
 NDMA = 16
 SEMAPHORES = (["eV", "eA", "eP", "eG", "sent"] + ["d%d" % i for i in range(NDMA)]
-              + ["r%d_%d" % (m, s) for m in (1, 2, 3) for s in range(1, STEPS)])
+              + ["r%d_%d" % (m, s) for m in (1, 2, 3, 4) for s in range(1, STEPS)])
 
 
 def rank_program(g, core, T, topo):
@@ -62,10 +61,10 @@ def rank_program(g, core, T, topo):
         cs = slice(a, b, st) if st != 1 else slice(a, b)
         ap = t[:, cs] if p is None else t[p, cs]
         bits = ((1 << b) - (1 << a)) if st == 1 else sum(1 << c for c in range(a, b, st))
-        return {"ap": ap, "r": [(name, bits)]}
+        return {"ap": ap, "r": [(name, bits)], "n": len(range(a, b, st)), "t": SCRATCH[name][0][0] + SCRATCH[name][2][0]}
 
     def ind(win, off):
-        return {"ap": win["ap"].indirect(off["ap"]), "r": win["r"], "x": off["r"]}
+        return {"ap": win["ap"].indirect(off["ap"]), "r": win["r"], "x": off["r"], "n": 16 * off["n"], "t": win["t"]}
 
     def regs(xs):
         out = []
@@ -77,14 +76,39 @@ def rank_program(g, core, T, topo):
     def a_(x):
         return x["ap"] if isinstance(x, dict) else x
 
-    def add(q, call, out, ins, token=None):
-        ops.append([q, call, regs(ins) + out.get("x", []), out["r"], token])
+    moved, late = [0], []
+
+    def add(q, call, out, ins, token=None, both=False):
+        xs = [x for x in [out] + ins if isinstance(x, dict) and "n" in x]
+        w = max([x["n"] for x in xs] + [1])
+        if token is not None:
+            if token[2] == "dma" and not late:
+                moved[0] += w * (2 if xs[0]["t"][1] == "b" else 4)
+            hold, t = {"dma": (60, COST["dma"] + COST["byte"] * (w * 4 if late else moved[0])), "remote": (COST["issue"], COST["issue"]), "arrive": (0, COST["fly"])}[token[2]]
+        else:
+            if q == "P":
+                t = COST["pe"] * max(64, out["n"]) * (4 if ins[0]["t"][1] == "f" else 1)
+            elif q == "G":
+                t = 170 + 2 * COST["cyc"] * w
+            elif "x" in out:
+                t = 50 + COST["scatter"] * w
+            elif any("x" in x for x in xs):
+                t = 60 + COST["gather"] * w
+            else:
+                r = 1.0
+                if both and all(x["t"][0] == "s" for x in xs[1:]):
+                    r = 2.0
+                elif q == "V" and not both and all(x["t"][1] in "bu" for x in xs if x["n"] > 1):
+                    r = 0.5
+                t = max(COST["least"], COST["fix"] + COST["cyc"] * r * w)
+            hold = t
+        ops.append([q, call, regs(ins) + out.get("x", []), out["r"], token, hold, t])
 
     def cp(out, x):
         add("V", lambda e: e.tensor_copy(a_(out), a_(x)), out, [x])
 
     def tt(out, x, y, op):
-        add("V", lambda e: e.tensor_tensor(a_(out), a_(x), a_(y), op), out, [x, y])
+        add("V", lambda e: e.tensor_tensor(a_(out), a_(x), a_(y), op), out, [x, y], None, True)
 
     def ts(out, x, s1, op0, s2=None, op1=None):
         if op1 is None:
@@ -105,11 +129,14 @@ def rank_program(g, core, T, topo):
         f = AF.Identity if f is None else f
         add("A", lambda e: e.activation(a_(out), a_(x), f, bias=a_(bias), scale=a_(scale)), out, [x, bias, scale])
 
-    def mm(out, l, r, start=True, stop=True):
-        add("P", lambda e: e.matmul(a_(out), a_(l), a_(r), start, stop), out, [l, r])
+    group = {}
 
-    def tr(out, x, ident):
-        add("P", lambda e: e.transpose(a_(out), a_(x), a_(ident)), out, [x, ident])
+    def mm(out, l, r, start=False, stop=False):
+        end = group[out["r"][0][0]] = [stop]
+        add("P", lambda e: e.matmul(a_(out), a_(l), a_(r), start, end[0]), out, [l, r])
+
+    def close(bank):
+        group[bank][0] = True
 
     def iota(out, pat, base, cm, small=False):
         if small:
@@ -117,8 +144,14 @@ def rank_program(g, core, T, topo):
         else:
             add("G", lambda e: e.iota(a_(out), pat, base, cm), out, [])
 
-    def gcopy(out, x):
-        add("G", lambda e: e.affine_select(a_(out), a_(x), [[0, 128]], ALU.is_ge, 0.0, 0, 0), out, [x])
+    def gsel(out, x, pat, op, c, base, cm):
+        add("G", lambda e: e.affine_select(a_(out), a_(x), pat, op, c, base, cm), out, [x])
+
+    def gcopy(out, x, w=128):
+        gsel(out, x, [[0, w]], ALU.is_ge, 0.0, 0, 0)
+
+    def gfill(out, c):
+        gsel(out, v("one"), [[0, 128]], ALU.is_gt, c, 0, 0)
 
     nd = [0]
 
@@ -129,171 +162,211 @@ def rank_program(g, core, T, topo):
 
     to = [T.cores[(rank + 1) % n], T.cores[(rank + 2) % n]]
     eng = [e for e in topo.engines(core, to[0]) if e in topo.engines(core, to[1])]
-    per = len(eng) // 2
-    masks = [sum(1 << e for e in eng[:per]), sum(1 << e for e in eng[per:2 * per])]
-    nsent = [0]
 
-    def send(m, s):
-        src, dst, sem = "o%d" % m, ("m1", "m2", "W")[m - 1], "r%d_%d" % (m, s + 1)
-        w = (64, MW // 2, 128)[m - 1]
-        so, do = 2 * w * s, (WW * (s + 1) + 2 * S - 64 if m == 3 else 2 * w * (s + 1))
+    def send(m, s, src, so, dst, do, w, parts):
+        sem = "r%d_%d" % (m, s + 1)
+        per = len(eng) // parts
 
         def call(e):
             trs = []
-            for h in range(2):
-                rid, pid = topo.addr(to[h], core)
+            for h in range(parts):
+                rid, pid = topo.addr(to[h % 2], core)
                 trs.append(RemoteDMATransfer(
-                    dst_ids=[DstId(rid=rid, pnc=pid)], dma_engine_mask=masks[h], remote_sem=T.sem[sem],
+                    dst_ids=[DstId(rid=rid, pnc=pid)], dma_engine_mask=sum(1 << x for x in eng[per * h:per * h + per]),
+                    remote_sem=T.sem[sem],
                     src=T[src][:, so + w * h:so + w * h + w], dst=T[dst][:, do + w * h:do + w * h + w]))
             return e.remote_dma_fused(trs, local_sem=T.sem.sent)
-        nsent[0] += 2 * per
-        add("G", call, {"r": []}, [v(src, so, so + 2 * w)], ("sent", nsent[0], "remote"))
-        add("X", None, v(dst, do, do + 2 * w), [], (sem, 2 * per, "arrive"))
+        add("G", call, {"r": []}, [v(src, so, so + parts * w)], ("sent", parts * per, "remote"))
+        add("X", None, v(dst, do, do + parts * w), [], (sem, parts * per, "arrive"))
 
+    Wm, P1, Po, Qo, Q2 = v("W", 0, 128), v("W", S, S + 128), v("W", 2 * S - 128, 2 * S), v("W", 2 * S, 2 * S + 128), v("W", 3 * S)
     fill(v("Fi"), 0)
-    dma("S", v("X"), T.xr[:])
-    dma("A", v("PQi", 64, 192), T.ql[:])
-    dma("A", v("m2", 72, 200), T.zq[:])
+    dma("A", Qo, T.ql[:])
+    dma("S", v("zl"), T.zq[:])
     dma("S", v("Fi", p=slice(0, 128, 16)), T.sd[:])
+    dma("S", v("X"), T.xr[:])
     dma("S", v("Di"), T.dr[:])
-    dma("S", v("PQi", 0, 64), T.pl[:, 0:64])
-    dma("S", v("PQi", 192, 256), T.pl[:, 64:128])
-
-    iota(v("A2"), [[-16, 8]], 0, 1)
-    iota(v("A1"), [[0, 16], [-1, 16]], 128, 1)
-    iota(v("col", 0, 1), [[0, 1]], 0, 1, True)
-    iota(v("A4"), [[1, 128]], 0, -1, True)
-    iota(v("A3"), [[1, 16]], 0, 0)
-    for r in range(0, 16, 2):
-        iota(v("wrow", r, r + 2), [[WT[r + 1] - WT[r], 2]], WT[r], 0, True)
-    iota(v("krow"), [[0, 8], [1, 16]], 0, 0, True)
+    dma("S", Po, T.pl[:])
+    late.append(1)
 
     def mk(j):
-        return v("mask", j, j + 1)
+        return v("m16", j, j + 1)
 
-    Dq = v("Dq")
-    CN = {"sel0": 0, "g16": 1, "gB": 2, "128th": 3, "h": 4, "vb": 5, "4": 6, "rs": 7}
+    Dq, I, nI, hI, m128, cq = v("Dq"), v("I"), v("nI"), v("hI"), v("mask", 0, 128), v("cq")
+    M1 = v("cM", 0, 128)
+    KV = "D" in OPT["ord"]
+    U = -131072.0 if KV else 1.0
+    bo8 = v("bo", 0, 8)
+    CN = ["W8", "W8b", "nW8", "nW8b", "v1", "v1b", "v2", "v2b", "vM", "vMb", "Rm", "c0", "c0b", "Ry", "Ryb", "oM", "oMb",
+          "Rl", "kP", "kQ", "k3", "k4", "aP", "aQ", "a3", "a4", "bP", "bQ", "b3", "b4", "h", "q", "g16", "s1", "s2"]
 
-    def C(k, a=0, e=8):
-        return v("C", 8 * CN[k] + a, 8 * CN[k] + e)
+    def C(k, w=8):
+        a = 8 * CN.index(k)
+        return v("C", a, a + w)
 
-    fill(v("rmax"), 1.0)
+    iota(v("A2"), [[-16, 8]], 0, 1)
+    iota(v("A1", 0, 16), [[-1, 16]], 128, 1)
+    iota(v("A1", 16, 32), [[0, 16]], 0, 1)
+    iota(v("A3"), [[1, 16]], 0, 0)
+    iota(v("col", 0, 1), [[0, 1]], 0, 1, True)
     ts(v("A2"), v("A2"), 4, ALU.arith_shift_right)
-    fill(v("rmin"), 0.0)
-    for name, c in (("c30", 30.5 * BIG), ("half", 0.5), ("cq", -0.25), ("cM", MAGIC)):
-        fill(v(name), c)
+    fill(v("one"), 1.0)
     ts(Dq, v("A2"), 0.0, ALU.is_equal)
     ts(v("A1"), v("A1"), 15, ALU.bitwise_and)
+    gsel(I, v("one"), [[-1, 128]], ALU.is_equal, 0.0, 0, 1)
+    for r in range(0, 16, 2):
+        iota(v("wrow", r, r + 2), [[WT[r + 1] - WT[r], 2]], WT[r], 0, True)
+    cp(v("bo"), v("A3"))
+    ts(v("m16"), v("A1", 0, 16), 0.0, ALU.is_equal)
+    cp(v("bx"), v("A1", 16, 32))
+    for k, c in (("c0", 256.0), ("c0b", 1024.0), ("Ry", -2.0), ("Ryb", 1.0), ("h", 0.5 * U), ("q", 0.25 * U), ("g16", 16.0)):
+        act(C(k), Dq, scale=c)
+    act(v("mask"), ind(v("m16"), v("bx")))
+    act(v("B"), ind(Dq, bo8))
+    act(v("col", 4, 5), v("col", 0, 1), scale=16.0)
+    act(v("col", 3, 4), v("col", 0, 1), scale=2.0)
+    act(C("Rl"), Dq, scale=-512.0)
+    for k, cP, cQ in (("kP", -float(S), float(S)), ("aP", v("col", 0, 1), v("col", 0, 1)), ("bP", 3.0 * S, 0.0)):
+        a = 8 * CN.index(k)
+        act(v("C", a, a + 4), v("Dq", 0, 4), scale=cP)
+        act(v("C", a + 4, a + 12), Dq, scale=cQ)
+        act(v("C", a + 12, a + 16), v("Dq", 4, 8), scale=cP)
+    act(C("a3"), Dq, scale=v("col", 3, 4))
+    act(C("a4"), Dq, scale=v("col", 4, 5))
+    act(nI, I, scale=-1.0)
+    act(v("Bk"), v("B"), scale=1.0 / 6.0)
+    cp(v("m1", 64, 192), Qo)
+    fill(v("rmax"), 1.0)
+    fill(v("rmin"), 0.0)
+    for k, c in (("v1", 2048.0), ("v1b", 128.0), ("v2", -0.5), ("v2b", 0.5), ("vM", 4096 * MAGIC), ("vMb", 2 * MAGIC),
+                 ("oM", 256 * MAGIC), ("oMb", 128 * MAGIC)):
+        fill(C(k), c)
     fill(v("rmax", 0, 512, 16), 0.0)
     fill(v("rmin", 0, 512, 16), 4194304.0)
-    ts(v("mask"), v("A1"), 0.0, ALU.is_equal)
-    act(C("128th"), Dq, scale=1.0 / 128)
-    act(C("g16"), Dq, scale=16.0)
-    act(C("gB"), Dq, scale=-BIG)
-    act(C("h"), Dq, scale=0.5)
-    act(C("vb"), Dq, scale=-1.0 / 2048)
-    act(C("4"), Dq, scale=4.0)
-    act(v("Rk", 0, 8), Dq)
-    act(v("Rk", 8, 16), Dq, scale=128.0)
-    act(v("Rk", 16, 20), v("Dq", 0, 4), scale=-float(S))
-    act(v("Rk", 20, 28), Dq, scale=float(S))
-    act(v("Rk", 28, 32), v("Dq", 4, 8), scale=-float(S))
-    act(v("Rc", 16, 24), Dq, scale=v("col", 0, 1))
-    act(v("Rc", 8, 16), Dq, scale=0.0)
-    act(v("Rd", 0, 4), v("Dq", 0, 4), scale=3.0 * S)
-    act(v("Rc", 0, 8), v("Rc", 16, 24), scale=16.0)
-    act(v("Rc", 24, 28), v("Rc", 16, 20))
-    act(v("Rc", 28, 36), v("Rc", 16, 24))
-    act(v("Rc", 36, 40), v("Rc", 20, 24))
-    act(v("Rd", 4, 12), Dq, scale=0.0)
-    act(v("Rd", 12, 16), v("Dq", 4, 8), scale=3.0 * S)
-    act(v("Re", 8, 16), v("Rc", 16, 24), scale=-1.0 / 64)
-    ts(C("sel0"), Dq, mk(0), ALU.mult)
-    ts(v("R8", 0, 8), Dq, mk(1), ALU.mult, BIG / 2, ALU.mult)
-    fill(v("m2", 0, 8), -1.0)
-    fill(v("m2", MW - 8, MW), -1.0)
-    ts(v("I"), v("A4"), 0.0, ALU.is_equal)
-    cp(v("bo"), v("A3"))
-    ts(v("kwin"), v("A3", 0, 8), 0.5, ALU.mult)
-    ts(v("col", 2, 3), v("A1", 0, 1), 1184.0, ALU.mult)
-    red(v("col", 3, 4), v("mask", 2, 6))
-    ts(v("m2", 8, 72), v("Fi", 0, 64), 2.0, ALU.mult, -1.0, ALU.add)
-    ts(v("m2", 200, 264), v("Fi", 64, 128), 2.0, ALU.mult, -1.0, ALU.add)
-    cp(v("m1", 0, 128), v("PQi", 64, 192))
-    tt(v("wrow"), v("wrow"), v("mask", 0, 16), ALU.mult)
+    fill(v("mul", 0, 8), 2741.0)
+    fill(v("mul", 8, 16), 32.0)
+    z0, f0 = v("Z", 16, ZH, 2), v("Z", 17, ZH, 2)
+    cp(z0, v("zl"))
+    cp(f0, v("Fi"))
+    ts(C("Rm"), Dq, mk(0), ALU.mult, 128.0, ALU.mult)
+    tt(v("wrow"), v("wrow"), v("m16"), ALU.mult)
+    ts(v("col", 2, 3), v("A1", 16, 17), 1184.0, ALU.mult)
     red(v("col", 1, 2), v("wrow"))
-    ts(v("W8", 0, 8), Dq, v("col", 1, 2), ALU.mult)
-    bo8 = v("bo", 0, 8)
-    act(v("col", 5, 6), mk(0), scale=-1.25, bias=0.5)
-    act(v("nI"), v("I"), scale=-1.0)
-    act(v("col", 6, 7), mk(1), scale=-0.75, bias=v("col", 5, 6))
-    act(v("hI"), v("I"), scale=0.5)
-    act(v("cb", 0, 4), v("mask", 2, 6), scale=-0.75, bias=v("col", 6, 7))
-    act(v("If"), v("I"))
-    act(v("cs", 0, 4), v("cb", 0, 4), scale=-1.0, bias=-0.75)
-    act(v("RL"), ind(v("R8", 0, 8), bo8))
-    act(v("shift"), ind(v("cs", 0, 4), v("bo", 0, 4)))
+    fill(v("cM"), MAGIC)
+    for k in ("W8", "W8b"):
+        ts(C(k), Dq, v("col", 1, 2), ALU.mult)
+    ts(C("nW8", 16), C("W8", 16), -1.0, ALU.mult)
+    ts(v("Wp"), v("B"), v("col", 1, 2), ALU.mult)
+    ts(v("Wn"), v("B"), v("col", 1, 2), ALU.mult, -1.0, ALU.mult)
+    ts(v("RLp"), v("B"), mk(1), ALU.mult, 0.5 * U, ALU.mult)
+    ts(v("RLn"), v("B"), mk(1), ALU.mult, -0.5 * U, ALU.mult)
+    gfill(v("c2k"), 2048.0)
+    gfill(v("half"), 0.5)
+    gfill(v("M4k"), 4096 * MAGIC)
+    gcopy(v("D", 0, 512), v("Di"), 512)
+    gfill(v("c32"), 32.0)
+    gfill(v("c15"), -15.25 * U)
+    if KV:
+        gfill(v("MB"), -U * MAGIC)
+    SG = [(3, 1), (3, 0), (2, 1)][:OPT["nsg"]]
+    for m in sorted(set(x[0] for x in SG)):
+        c = 4.0 * len([x for x in SG if x[0] == m])
+        gsel(v("c15", m, 128, 4), v("one", 0, 32), [[0, 32]], ALU.is_gt, (c - 15.25) * U, 0, 0)
+    iota(v("krow"), [[0, 8], [1, 16]], 0, 0, True)
 
     def late_constants(part):
         if part == 0:
-            cp(v("D", 0, 512), v("Di"))
-            return
-        if part == 1:
-            cp(v("W", 2 * S - 64, 3 * S), v("PQi"))
-            return
-        act(v("col", 4, 5), mk(0), scale=0.5, bias=v("col", 3, 4))
-        act(v("W2", 0, 8), v("W8", 0, 8), scale=2.0)
-        act(v("W2", 8, 16), v("W8", 0, 8), scale=16.0)
-        act(C("rs"), Dq, scale=v("col", 4, 5))
+            gfill(cq, -0.25)
+            gfill(v("Bf"), 0.0)
+            if not KV:
+                gsel(v("nBI"), v("Bf"), [[-1, 128]], ALU.not_equal, -32768.0 * (1 + OPT["okv"]), 0, 1)
+            gsel(hI, v("half"), [[-1, 128]], ALU.is_equal, 0.0, 0, 1)
+            gfill(v("M16"), 16 * MAGIC)
+            iota(v("r16"), [[16, 128]], 0, 0, True)
+        else:
+            ts(v("col", 5, 6), mk(0), 1.15625, ALU.mult)
+            ts(v("nm"), m128, 4103.5, ALU.mult, -4096.0, ALU.add)
+            ts(v("col", 6, 7), mk(1), 0.640625, ALU.mult, v("col", 5, 6), ALU.add)
+            ts(v("Bf", 0, 128, 16), Dq, -1.0 / 16, ALU.mult)
+            ts(v("Bf", 1, 128, 16), Dq, -1.0 / 32, ALU.mult)
+            ts(v("cf"), v("one"), v("col", 6, 7), ALU.mult)
 
-    LO, HI = slice(0, 64), slice(64, 128)
-    I, m128 = v("I"), v("mask", 0, 128)
     Xw = v("X")
-    later = []
-    PE = "pK" if OPT["bp"] else "pA"
-    DB = (("pD0", "pD1"), ("pT", "pS"))
+    DB = (("pD0", "pD1"), ("pD2", "pD3"))
+    pv, po = v("pD1", 128, 144), v("pK", 384, 400)
+
+    def v_pre(f):
+        mm(pv, I, C("v1", 16), True)
+        mm(pv, I, C("v2", 16))
+        mm(v("pD1", 136, 144), f, C("Rm"))
+
+    def v_post(zn):
+        mm(pv, zn, C("nW8", 16))
+        mm(pv, I, C("vM", 16))
+        mm(pv, nI, C("vM", 16))
+        mm(pv, zn, C("W8", 16), False, True)
+
+    def o_pre(case):
+        mm(po, m128, C("c0", 16), True)
+        if case:
+            mm(v("pK", 392, 400), v("lk"), C("Rl"))
+
+    def o_post():
+        mm(po, v("lv", 128, 256), C("Ry", 16))
+        mm(po, I, C("oM", 16))
+        mm(po, nI, C("oM", 16))
+        mm(v("pK", 384, 392), v("lv", 0, 128), Dq)
+        mm(v("pK", 392, 400), v("lv", 128, 256), Dq)
+        mm(v("pK", 392, 400), m128, C("a3"), False, True)
+
+    def v_int(part):
+        if part == 0:
+            tt(v("vi"), pv, v("mul"), ALU.mult)
+        elif part == 1:
+            ts(v("vj"), v("vi"), 5, ALU.arith_shift_right, 255, ALU.bitwise_and)
+        else:
+            tt(v("lv"), ind(v("vj"), v("bo")), v("mask"), ALU.mult)
+
+    v_pre(f0)
+    v_post(z0)
+    o_pre(False)
+    v_int(0)
 
     for s in range(STEPS):
-        b = MW * s
         last = s == STEPS - 1
-        z, Flo, Fhi = v("m2", b + 72, b + 200), v("m2", b + 8, b + 72), v("m2", b + 200, b + 264)
-        Llo, Lhi = v("m2", b + 4, b + 8), v("m2", b + 264, b + 268)
+        zb = ZS * s
+        z, f = v("Z", zb + 16, zb + ZH, 2), v("Z", zb + 17, zb + ZH, 2)
+        ce = v("m3", 8 * s, 8 * s + 8)
+        kN, fn = v("o2", 512 * s + 1, 512 * s + 256, 2), v("o2", 512 * s + 257, 512 * s + 512, 2)
+        zn = v("zl") if last else v("o2", 512 * s + 256, 512 * s + 512, 2)
+        pu, pl, pb, pz = v("pL", 256, 384), v("pL", 0, 128), v("pB", 0, 128), v("pD3", 0, 128)
 
-        def W(a=0, e=WW):
-            return v("W", WW * s + a, WW * s + e)
+        def hs(a, e, st=1):
+            return v("Z", zb + ZH + a, zb + ZH + e, st)
 
-        Plo, Phi, Qa, P1 = W(2 * S - 64, 2 * S), W(2 * S + 128, 3 * S), W(2 * S, 2 * S + 128), W(S, S + 128)
+        def ends(h, j):
+            return hs(1024 * h + 15, 1024 * h + 1024, 16) if j else v("ls", 1024 * h + 15, 1024 * h + 1024, 16)
 
         def gy(a, e, q="A"):
-            (act if q == "A" else cp)(v("yy", 16 * a, 16 * e), ind(Xw, v("m1", 128 * s + a, 128 * s + e)))
+            (act if q == "A" else cp)(v("yy", 16 * a, 16 * e), ind(Xw, v("m1", 256 * s + 64 + a, 256 * s + 64 + e)))
 
-        def sc_hi(q):
-            scan(v("hs", 512 * q, 512 * q + 512), v("rmax"), v("yy", 512 * q, 512 * q + 512), ALU.mult, ALU.max)
+        def sc(a, e, j):
+            if j:
+                scan(hs(16 * a, 16 * e), v("rmax", 0, 16 * (e - a)), v("yy", 16 * a, 16 * e), ALU.mult, ALU.max)
+            else:
+                scan(v("ls", 16 * a, 16 * e), v("rmin", 0, 16 * (e - a)), v("yy", 16 * a, 16 * e), ALU.max, ALU.min)
 
-        def sc_lo(q):
-            scan(v("ls", 512 * q, 512 * q + 512), v("rmin"), v("yy", 512 * q, 512 * q + 512), ALU.max, ALU.min)
-
-        def bcast(h, part):
-            pb = ("pA", "pB")[h]
-            for j, src in enumerate(("ls", "hs")):
-                ends = v(src, 1024 * h + 15, 1024 * h + 1024, 16)
-                if OPT["bp"] and part == 0:
-                    tr(v(pb, 512 + 128 * j, 640 + 128 * j, p=LO), ends, I)
+        def bcast(h):
+            for j in range(2):
                 for kk in range(4):
-                    out = v(pb, 256 * j + kk, 256 * j + 256, 4)
-                    if OPT["bp"] and part == 2:
-                        tr(out, v("eT", 256 * h + 128 * j, 256 * h + 128 * j + 128, p=LO), v("I", 0, 64, p=LO))
-                    if not OPT["bp"] and part == 0:
-                        mm(out, I, ends)
-            if OPT["bp"] and part == 1:
-                cp(v("eT", 256 * h, 256 * h + 256, p=LO), v(pb, 512, 768, p=LO))
+                    mm(v(("pA", "pB")[h], 256 * j + kk, 256 * j + 256, 4), I, ends(h, j), True, True)
 
         def gx(a, e, q="A"):
             (act if q == "A" else cp)(v("xx", 16 * a, 16 * e), ind(Xw, v("E", a, e)))
 
         def dz(h, m):
             for kk in range(8):
-                mm(v(DB[h][m], kk, 512, 8), v("nI"), v("m2", b + 72 + 64 * h, b + 136 + 64 * h), kk == 0, False)
+                mm(v(DB[h][m], kk, 512, 8), nI, v("Z", zb + 16 + 128 * h, zb + 144 + 128 * h, 2), kk == 0)
 
         def dx(h, m):
             mm(v(DB[h][m]), I, v("xx", 1024 * h + m, 1024 * h + 1024, 2), False, True)
@@ -302,22 +375,30 @@ def rank_program(g, core, T, topo):
             o = 1024 * m + 512 * h
             act(v("ad", o, o + 512), v(DB[h][m]), AF.Abs)
 
+        def sg_fill(i):
+            m, j = SG[i]
+            bank = ("pD0", "pD1", "pD2")[i]
+            for h in range(2):
+                for kk in range(4):
+                    mm(v(bank, 256 * h + kk, 256 * h + 256, 4), I if j else nI, ends(h, j), h + kk == 0)
+            for h in range(2):
+                mm(v(bank, 256 * h, 256 * h + 256), nI if j else I, v("xx", 1024 * h + m, 1024 * h + 1024, 4), False, h == 1)
+
+        def sg(i):
+            m, j = SG[i]
+            act(v(("aa", "bb")[j], 512 * m, 512 * m + 512), v(("pD0", "pD1", "pD2")[i]), AF.Sign, bias=0.5)
+
         def made(part):
             if part == 0:
-                tt(v("pK", 256, 384), v("pK", 256, 384), Qa, ALU.mult)
+                tt(v("u1"), pu, Qo, ALU.mult)
             elif part == 1:
-                ts(v("u1"), v("pK", 256, 384), v("col", 2, 3), ALU.add)
-                mm(v("pK", 0, 128), I, v("krow"), True, False)
-            elif part == 2:
-                ts(v("u2"), v("u1"), 5, ALU.arith_shift_right, 2047, ALU.bitwise_and)
-            elif OPT["gc"]:
-                gcopy(W(0, 128), v("u2"))
+                ts(v("u2"), v("u1"), v("col", 2, 3), ALU.add)
             else:
-                cp(W(0, 128), v("u2"))
+                ts(Wm, v("u2"), 5, ALU.arith_shift_right, 2047, ALU.bitwise_and)
 
         def sum_d(m):
             for kk in range(8):
-                mm(v("pK", m + 2 * kk, 128, 16), v("ad", 1024 * m + kk, 1024 * m + 1024, 8), C("g16"), False, m == 1 and kk == 7)
+                mm(v("pK", m + 2 * kk, 128, 16), v("ad", 1024 * m + kk, 1024 * m + 1024, 8), C("g16"))
 
         def cmp(h, m, j):
             o = 512 * m + 256 * h
@@ -326,219 +407,229 @@ def rank_program(g, core, T, topo):
 
         def sum_c(m, j):
             for kk in range(4):
-                mm(v("pL", m + 4 * kk, 128, 16), v(("aa", "bb")[j], 512 * m + kk, 512 * m + 512, 4), C("gB"), False,
-                   m == 3 and j == 1 and kk == 3)
+                mm(v("pL", m + 4 * kk, 128, 16), v(("aa", "bb")[j], 512 * m + kk, 512 * m + 512, 4),
+                   C("q" if (m, j) in SG else "h"))
 
-        vy, vx = (OPT["vy"] if s else 0), OPT["vx"]
-        early = OPT["early"] if s else OPT["early0"]
-        if vy and OPT["e"] == 1:
-            gy(0, vy, "V")
-        for q in range(4 - early):
-            if 32 * q + 32 > vy:
-                gy(max(32 * q, vy), 32 * q + 32)
-        mm(v("pS", 0, 8), z, v("W8", 0, 8))
-        if s == 0:
-            mm(v("pS", 8, 16, p=LO), Flo, C("sel0"))
-            mm(v("pS", 8, 16, p=HI), Fhi, C("sel0"))
-            cp(v("ri"), v("pS", 0, 16))
-            tt(v("lr", 128, 256), ind(v("ri"), v("bo", 8, 16)), m128, ALU.mult)
-            mm(v("pT", 0, 8), v("lr", 128, 256), Dq)
-            cp(Llo, v("pT", 0, 4))
-            cp(Lhi, v("pT", 4, 8))
-        else:
-            cp(v("ri", 0, 8), v("pS", 0, 8))
-            if OPT["e"] == 0:
-                gy(0, vy, "V")
-            else:
-                cp(ind(v("D"), v("od")), later.pop())
-        mm(v("pS", 16, 20), I, Llo, True, False)
-        mm(v("pS", 20, 24), I, Lhi, False, False)
-        dz(0, 0)
-        mm(v("pL", 0, 128), I, v("c30"), True, False)
-        mm(v("pL", 0, 128, p=LO), Flo, v("RL"), False, False)
-        ts(v("rt", 0, 8), v("ri", 0, 8), 4095, ALU.bitwise_and)
-        if s > 0 and OPT["e"] == 0:
-            cp(ind(v("D"), v("od")), later.pop())
-        elif s > 0:
-            sc_hi(0)
-        ts(v("rt", 8, 16), v("rt", 0, 8), 2741.0, ALU.mult)
-        ts(v("uw"), v("rt", 0, 8), 32.0, ALU.add)
-        if s > 0 and OPT["e"] == 0:
-            sc_hi(0)
-        ts(v("vj", 0, 8), v("rt", 8, 16), 5, ALU.arith_shift_right, 255, ALU.bitwise_and)
+        vy = OPT["vy"] if s else 0
+        cuts = [0, vy or OPT["y0"]] + OPT["cuts"] + [128]
+        nq = len(cuts) - 1
+        for q in range(nq):
+            gy(cuts[q], cuts[q + 1], "V" if vy and q == 0 else "A")
         if s > 0:
-            sc_lo(0)
-        tt(v("lr", 0, 128), ind(v("vj", 0, 8), bo8), m128, ALU.mult)
-        mm(v("pS", 16, 24), v("lr", 0, 128), C("128th"), False, True)
+            cp(ind(v("D"), v("o3", 16 * s - 8, 16 * s)), P1)
+            gcopy(Qo, v("m1", 256 * s + 64, 256 * s + 192))
+            for h in range(2):
+                gcopy(v("W", 2 * S - 128 + 64 * h, 2 * S - 64 + 64 * h), v("m1", 256 * s + 192 * h, 256 * s + 192 * h + 64), 64)
+        gcopy(Q2, Qo)
         if s == 0:
             late_constants(0)
-        else:
-            sc_hi(1)
-        ts(v("ce"), v("pS", 16, 24), 128.0, ALU.mult, 128.0, ALU.add)
-        if s > 0:
-            sc_lo(1)
-        cp(v("E"), ind(v("D", 0, 512), v("ce")))
+            v_int(1)
+            sc(cuts[0], cuts[1], 1)
+            v_int(2)
+            o_post()
+        mm(pu, I, v("c2k"), True)
+        mm(pu, nI, v("half"))
+        mm(pu, v("Wn"), z)
+        mm(pu, I, v("M4k"))
+        mm(pu, nI, v("M4k"))
+        mm(pu, v("Wp"), z)
+        mm(pu, I, v("c32"), False, True)
+        for h in range(2):
+            for m in range(2):
+                dz(h, m)
+        for q in range(nq):
+            if q == OPT["epos"]:
+                cp(v("E"), ind(v("D", 0, 512), ce))
+            if s or q:
+                sc(cuts[q], cuts[q + 1], 1)
+            sc(cuts[q], cuts[q + 1], 0)
+            if s == 0 and q == 0:
+                cp(ce, v("pK", 384, 392))
+            if cuts[q] < 64 <= cuts[q + 1]:
+                bcast(0)
+            if q == nq - 2:
+                made(0)
+        for i in range(1 if KV else 2 + OPT["okv"]):
+            mm(v("pK", 0, 128), v("B") if i else I, v("c2k") if i else v("krow"), i == 0)
+        mm(pl, I, v("c15"), True)
+        mm(pl, f, v("RLp"))
+        mm(pl, I, v("MB") if KV else M1)
+        mm(pl, nI, v("MB") if KV else M1)
+        mm(pl, f, v("RLn"))
+        if OPT["vx"]:
+            gx(0, OPT["vx"], "V")
+        gx(OPT["vx"], 64)
+        gx(64, 128)
+        bcast(1)
         if s == 0:
             late_constants(1)
-        (cp if OPT["ubp"] else act)(v("ub"), ind(v("uw"), bo8))
-        gx(vx, 64)
-        for q in range(4 - early, 4):
-            gy(32 * q, 32 * q + 32)
-        gx(64, 128)
-        if s == 0:
-            sc_hi(0)
-            sc_lo(0)
-            sc_hi(1)
-            sc_lo(1)
-        sc_hi(2)
-        mm(v("pL", 0, 128, p=HI), Fhi, v("RL"), False, False)
-        bcast(0, 0)
-        dz(0, 1)
-        mm(v("pK", 256, 384), v("ub"), v("If"))
-        dz(1, 0)
-        dz(1, 1)
-        sc_lo(2)
-        gcopy(W(3 * S, 3 * S + 128), Qa)
-        sc_hi(3)
-        if OPT["mp"] == 0:
-            made(0)
-        sc_lo(3)
-        made(1 - OPT["mp"])
-        if vx:
-            gx(0, vx, "V")
 
+        todo = [(m, j) for m in range(4) for j in range(2) if (m, j) not in SG]
         dx(0, 0)
         dx(0, 1)
-        bcast(1, 0)
-        for m in range(4):
-            cmp(0, m, 0)
-            if m + 2 - OPT["mp"] < 4:
-                made(m + 2 - OPT["mp"])
-            cmp(0, m, 1)
+        for m, j in todo:
+            cmp(0, m, j)
         dx(1, 0)
         dx(1, 1)
         absd(0, 0)
+        if len(SG) > 0:
+            sg_fill(0)
         absd(0, 1)
-        absd(1, 0)
-        absd(1, 1)
-        cmp(1, 0, 0)
-        cmp(1, 0, 1)
-        sum_c(0, 0)
-        sum_c(0, 1)
-        sum_d(0)
-        cmp(1, 1, 0)
-        cmp(1, 1, 1)
-        sum_c(1, 0)
-        sum_c(1, 1)
-        act(v("zw", 128, 256), z, scale=0.5)
-        act(v("zw", 256, 384), z, scale=-1.0)
-        if OPT["d1"]:
-            sum_d(1)
-        for j in range(2):
-            cmp(1, 2, j)
-            sum_c(2, j)
-        if not OPT["d1"]:
-            sum_d(1)
-        act(v("DkS"), v("pK", 0, 128))
-        for j in range(2):
-            cmp(1, 3, j)
-            sum_c(3, j)
-        mm(v("pD0", 0, 128), I, v("half"), True, False)
-        mm(v("pT", 0, 40), m128, v("Rc"), True, False)
-        mm(v("pT", 24, 40), m128, v("Rd"), False, False)
-        mm(v("pA", 0, 128), I, z, True, False)
-        mm(v("pA", 0, 128), v("nI"), v("hs", 15, 2048, 16), False, True)
-
-        tt(v("dEP", 0, 64), ind(v("D", 0, 512), v("ce", 0, 4)), Plo, ALU.subtract)
-        tt(v("dEP", 64, 128), ind(v("D", 0, 512), v("ce", 4, 8)), Phi, ALU.subtract)
-        tt(v("key"), v("pL", 0, 128), v("DkS"), ALU.max)
-        act(v("okT"), v("key"), AF.Sign, bias=BIG - 0.5, scale=-1.0)
-        scan(v("ms"), v("rmin", 0, 128), v("key"), ALU.max, ALU.min)
-        mm(v("pD0", 0, 128), v("okT"), v("hI"), False, True)
-        act(v("zw", 0, 128), v("pA", 0, 128))
-        if not OPT["gc"]:
-            act(W(3 * S, 3 * S + 128), Qa)
-        if s == 0:
-            late_constants(2)
-        mm(v("pK", 384, 392), m128, v("Rc", 0, 8), True, False)
-        mm(v("pD1", 0, 8), m128, v("Re", 8, 16), True, False)
-        mm(v("pD1", 0, 4), I, Llo, False, False)
-        mm(v("pD1", 4, 8), I, Lhi, False, False)
-        mm(v("pS", 384, 512), I, v("cq"), True, False)
-        mm(v("pL", 128, 200), I, v("m2", b, b + 72), True, False)
-        mm(v("pL", 200, 272), I, v("m2", b + 200, b + 272), False, False)
-        mm(v("pL", 132, 136), I, v("shift", 16 * s, 16 * s + 4), False, False)
-        mm(v("pL", 264, 268), I, v("shift", 16 * s, 16 * s + 4), False, False)
-        cp(v("wi"), v("ms", 15, 128, 16))
-        scan(v("ns"), v("rmax", 0, 128), v("okT"), ALU.mult, ALU.add)
-        ts(v("wj", 0, 8), v("wi"), 15, ALU.bitwise_and)
-        ts(v("wj", 8, 16), v("ns", 15, 128, 16), 1.0 / 12.0, ALU.mult, 6.5 / 6.0, ALU.add)
-        ts(v("kb", 0, 8), v("ns", 15, 128, 16), 1.0 / 12.0, ALU.mult, 160 + 6.5 / 6.0, ALU.add)
-        act(v("kT"), ind(v("kb", 0, 8), bo8), scale=0.5, bias=-80.0)
-        tt(v("lb"), ind(v("wj"), v("bo")), v("mask"), ALU.mult)
-        mm(v("pB", 0, 128), v("kT"), I)
-        act(v("kN"), v("pB", 0, 128))
-        lk = v("lb", 128, 256)
-        mm(v("pT", 0, 8), v("lb", 0, 128), Dq, False, False)
-        mm(v("pT", 8, 40), lk, v("Rk"), False, True)
-        mm(v("pD1", 0, 8), lk, C("4"), False, False)
-        mm(v("pL", 132, 136), lk, C("h", 0, 4), False, False)
-        mm(v("pL", 264, 268), lk, C("h", 4, 8), False, False)
-        tt(v("pD0", 0, 128), v("pD0", 0, 128), v("dEP"), ALU.mult)
-        mm(v("pL", 136, 264), I, v("kN"), False, True)
-        cp(v("of"), v("pT", 0, 40))
-        act(v("zs"), ind(v("zw"), v("of", 16, 24)))
-        mm(v("pS", 384, 512), I, v("zs"), False, False)
-        tt(W(S, S + 64), v("pD0", 0, 64), Plo, ALU.add)
-        tt(W(S + 64, S + 128), v("pD0", 64, 128), Phi, ALU.add)
-        tt(v("tb"), ind(v("xx"), v("of", 0, 8)), v("kN"), ALU.mult)
-        if not last:
-            cp(v("o1", 128 * s, 128 * s + 128), ind(W(), v("of", 28, 36)))
-            send(1, s)
-        act(v("fa"), v("pL", 128, 272), AF.Abs, bias=v("cb", s, s + 1))
-        zn = v("o2", b + 72, b + 200)
-        if OPT["pm"]:
-            mm(v("pS", 384, 512), I, v("tb"), False, False)
-            mm(v("pS", 384, 512), I, v("cM"), False, True)
-            act(zn, v("pS", 384, 512), AF.Abs, bias=-MAGIC)
-        else:
-            mm(v("pS", 384, 512), I, v("tb"), False, True)
-            act(v("t3"), v("pS", 384, 512), bias=MAGIC)
-            act(zn, v("t3"), AF.Abs, bias=-MAGIC)
-        act(v("o2", b, b + 72), v("fa", 0, 72), AF.Sign, bias=-1.0)
-        act(v("o2", b + 200, b + 272), v("fa", 72, 144), AF.Sign, bias=-1.0)
-        if not last:
-            send(2, s)
-        act(v("o3", 256 * s, 256 * s + 256), ind(W(), v("of", 24, 40)))
-        if not last:
-            send(3, s)
-        else:
-            dma("S", T.yz[:], zn)
-            dma("S", T.yq[:], v("o3", 256 * s + 64, 256 * s + 192))
-            dma("S", T.yp[:, 0:64], v("o3", 256 * s, 256 * s + 64))
-            dma("S", T.yp[:, 64:128], v("o3", 256 * s + 192, 256 * s + 256))
-        mm(v("pS", 0, 16), zn, v("W2"))
+        if len(SG) > 1:
+            sg_fill(1)
+        pend = list(todo)
+        for c in OPT["ord"]:
+            if c in "ab":
+                absd(1, "ab".index(c))
+            elif c in "AB":
+                sum_d("AB".index(c))
+            elif c == "c":
+                cmp(1, *pend[0])
+                sum_c(*pend.pop(0))
+            elif c in "012":
+                sg(int(c))
+                sum_c(*SG[int(c)])
+            elif c == "m":
+                made(1)
+                made(2)
+            elif c == "e":
+                tt(v("dEP"), ind(v("D", 0, 512), ce), Po, ALU.subtract)
+            elif c == "k":
+                close("pL")
+                if KV:
+                    tt(v("key"), pl, v("DkS"), ALU.max)
+                    act(v("okT"), v("key"), AF.Sign, bias=65535.5, scale=-1.0)
+                    mm(v("pA", 0, 128), v("okT"), hI, False, True)
+                    continue
+                if OPT["okv"]:
+                    ts(v("okT"), pl, -0.25, ALU.is_ge)
+                else:
+                    act(v("okT"), pl, AF.Sign, bias=0.25)
+                mm(v("pK", 0, 128), v("nBI"), v("okT"))
+                mm(v("pA", 0, 128), v("okT"), I if OPT["okv"] else hI, bool(OPT["okv"]), True)
+            elif c == "n":
+                (cp if OPT["okn"] else act)(v("okN"), v("pA", 0, 128))
+            elif c == "p":
+                mm(v("pD0", 0, 128), I, cq, True)
+                mm(v("pD0", 128, 256), I, v("cf"))
+                mm(v("pD0", 128, 256), I, f)
+                mm(v("pD1", 0, 128), I, cq, True)
+            elif c == "q":
+                mm(v("pD2", 0, 16), m128, C("aP", 16), True)
+                mm(v("pD2", 0, 16), m128, C("bP", 16))
+            elif c == "N":
+                mm(v("pD1", 0, 128), v("okN"), v("Bk"))
+                mm(v("pD1", 0, 128), I, M1)
+                mm(v("pD1", 0, 128), nI, M1, False, True)
+                mm(v("pD0", 0, 128), v("Bk"), v("okN"))
+                mm(v("pD0", 128, 256), v("Bf"), v("okN"))
+                mm(v("pD0", 0, 256), I, v("cM"), False, True)
+            elif c == "x":
+                tt(v("pA", 0, 128), v("pA", 0, 128), v("dEP"), ALU.mult)
+            elif c == "y":
+                tt(P1, v("pA", 0, 128), Po, ALU.add)
+            elif c == "K":
+                tt(v("lk"), v("pD1", 0, 128), m128, ALU.mult)
+                mm(v("pD2", 0, 16), v("lk"), C("kP", 16), False, True)
+            elif c == "F":
+                act(v("o2", 512 * s + 1, 512 * s + 512, 2), v("pD0", 0, 256), bias=-MAGIC)
+            elif c == "f":
+                cp(v("of"), v("pD2", 0, 16))
+            elif c == "z":
+                act(v("zt"), ind(v("zw"), v("of", 4, 12)))
+            elif c == "h":
+                mm(v("pA", 128, 256), I, hs(15, 2048, 16), True)
+                mm(v("pA", 128, 256), nI, z, False, True)
+                act(v("zw", 0, 128), v("pA", 128, 256))
+                act(v("zw", S, S + 128), z, scale=0.5)
+                act(v("zw", 2 * S, 2 * S + 128), z, scale=-1.0)
+            elif c == "H":
+                mm(v("pA", 0, 128), I, v("half"), True)
+            elif c == "D":
+                close("pK")
+                act(v("DkS"), v("pK", 0, 128))
+            elif c == "s":
+                close("pK")
+                scan(v("mi" if OPT["si"] else "ms"), v("rmin", 0, 128), v("key" if KV else "pK", 0, 128), ALU.max, ALU.min)
+            elif c == "r":
+                mm(v("pL", 128, 136), m128, C("a4"), True)
+                mm(pz, I, cq, True)
+            elif c == "w" and not OPT["si"]:
+                cp(v("wi"), v("ms", 15, 128, 16))
+            elif c == "j":
+                ts(v("wj"), v("mi", 15, 128, 16) if OPT["si"] else v("wi"), 15, ALU.bitwise_and)
+            elif c == "l":
+                tt(v("lb"), ind(v("wj"), bo8), m128, ALU.mult)
+                mm(v("pL", 128, 136), v("lb"), Dq, False, True)
+            elif c == "o":
+                cp(v("ob"), v("pL", 128, 136))
+            elif c == "P":
+                mm(pb, I, v("r16"), True)
+                mm(pb, I, v("nm"))
+            elif c == "O":
+                o_pre(True)
+            elif c == "V":
+                v_pre(fn)
+            elif c == "Z":
+                mm(pz, I, v("zt"))
+            elif c == "t":
+                tt(v("tb"), ind(v("xx"), v("ob")), kN, ALU.mult)
+                mm(pz, hI, v("tb"))
+                mm(pz, I, M1, False, True)
+                act(zn, pz, AF.Abs, bias=-MAGIC)
+            elif c == "g" and not last:
+                cp(v("o1", 256 * s, 256 * s + 256), ind(v("W"), v("of", 0, 16)))
+                send(1, s, "o1", 256 * s, "m1", 256 * s + 256, 128, 2)
         if last:
-            mm(v("pT", 0, 64, p=slice(0, 8)), C("rs"), v("o2", b + 8, b + 72))
-            mm(v("pT", 64, 128, p=slice(0, 8)), C("rs"), v("o2", b + 200, b + 264))
-            act(v("sS", p=slice(0, 8)), v("pT", 0, 128, p=slice(0, 8)), bias=4.5)
-            dma("S", T.ys[:], v("sS", p=slice(0, 8)))
-        cp(v("vi"), v("pS", 0, 16))
-        ts(v("vj"), v("vi"), 31, ALU.bitwise_and)
-        tt(v("lv", 0, 128), ind(v("vj"), bo8), m128, ALU.mult)
-        mm(v("pK", 384, 392), v("lv", 0, 128), C("h"), False, True)
-        tt(v("lv", 128, 256), ind(v("vj"), v("bo", 8, 16)), m128, ALU.mult)
-        mm(v("pD1", 0, 8), v("lv", 128, 256), C("vb"), False, True)
-        cp(v("oo"), v("pK", 384, 392))
+            cp(v("pq"), ind(v("W"), v("of", 0, 16)))
+            dma("S", T.yp[:, 0:64], v("pq", 0, 64))
+            dma("S", T.yq[:], v("pq", 64, 192))
+            dma("S", T.yp[:, 64:128], v("pq", 192, 256))
+            dma("S", T.yz[:], zn)
+            E8 = slice(0, 8)
+            ps = v("pD2", 128, 256, p=E8)
+            act(C("s1"), C("Rm"), scale=-1.0 / 256)
+            act(v("col", 7, 8), mk(0), scale=0.5, bias=mk(1))
+            act(C("s2"), Dq, scale=v("col", 7, 8))
+            mm(ps, v("nI", 0, 8), cq, True)
+            mm(ps, C("s1"), fn)
+            mm(ps, v("I", 0, 8), M1)
+            mm(ps, v("nI", 0, 8), M1)
+            mm(ps, C("s2"), fn, False, True)
+            act(v("sS", p=E8), ps, scale=2.0)
+            dma("S", T.ys[:], v("sS", p=E8))
+        elif not OPT["zlate"]:
+            send(2, s, "o2", 512 * s + 256, "Z", zb + ZS + 16, 128, 2)
+        mm(pb, v("Wn"), zn)
+        mm(pb, I, v("M16"))
+        mm(pb, nI, v("M16"))
+        mm(pb, v("Wp"), zn, False, True)
+        v_post(zn)
+        scan(v("oS"), v("rmax", 0, 128), pb, ALU.mult, ALU.max)
+        v_int(0)
+        cp(v("oo"), v("oS", 15, 128, 16))
+        v_int(1)
         tt(v("t1"), ind(Xw, v("oo")), zn, ALU.add)
-        ts(v("od"), v("pD1", 0, 8), -128.0, ALU.mult, 1152.0, ALU.add)
+        if OPT["lv"] == 0:
+            v_int(2)
+            o_post()
         ts(v("xn"), v("t1"), 0.5, ALU.mult, -0.25, ALU.add)
+        if OPT["lv"] == 1:
+            v_int(2)
+            o_post()
         cp(ind(Xw, v("oo")), v("xn"))
         if last:
             dma("A", T.yx[:], Xw)
-        later.append(P1)
-        if last:
-            cp(ind(v("D"), v("od")), later.pop())
+        if OPT["lv"] == 2:
+            v_int(2)
+            o_post()
+        cp(v("o3", 16 * s, 16 * s + 16), po)
+        if not last:
+            send(3, s, "o3", 16 * s, "m3", 8 * s + 8, 4, 2)
+            if OPT["zlate"]:
+                send(2, s, "o2", 512 * s + 256, "Z", zb + ZS + 16, 128, 2)
+        else:
+            cp(ind(v("D"), v("o3", 16 * s + 8, 16 * s + 16)), P1)
             dma("S", T.yd[:], v("D", 0, 512))
 
     def meet(r1, r2):
@@ -547,6 +638,70 @@ def rank_program(g, core, T, topo):
                 if x[0] == y[0] and x[1] & y[1]:
                     return True
         return False
+
+    def clash(e, o):
+        return meet(e[3], o[2]) or meet(e[3], o[3]) or meet(e[2], o[3])
+
+    seen, pre, soft = {}, [], set()
+    for j, o in enumerate(ops):
+        p = set()
+        for nm in set(x[0] for x in o[2] + o[3]):
+            if SCRATCH[nm][0] == "psum":
+                for i in reversed(seen.get(nm, [])):
+                    if ops[i][0] != o[0] or o[0] == "P" or clash(ops[i], o):
+                        p.add(i)
+                    if ops[i][0] == "P":
+                        break
+            else:
+                p.update(i for i in seen.get(nm, []) if clash(ops[i], o))
+            seen.setdefault(nm, []).append(j)
+        if o[0] == "X":
+            p.add(j - 1)
+        if o[4] is not None and o[0] != "X":
+            k = o[4][2]
+            if k in seen and seen[k] not in p:
+                p.add(seen[k])
+                soft.add((seen[k], j))
+            seen[k] = j
+        pre.append(p)
+    post = [[] for _ in ops]
+    for j, p in enumerate(pre):
+        for i in p:
+            post[i].append(j)
+
+    def place(rank_of, before, flip):
+        at, busy = {}, {}
+        for j in sorted(range(len(ops)), key=rank_of):
+            q, hold, t = ops[j][0], ops[j][5], ops[j][6]
+            r = max([at[i] + (ops[i][5] if (min(i, j), max(i, j)) in soft else
+                              ops[i][6] + (0 if ops[i][0] == q == "P" else COST["hop"])) for i in before[j]] + [0.0])
+            lead = t - hold if flip else 0.0
+            b = busy.setdefault(q, [])
+            k = 0
+            r += lead
+            while k < len(b) and b[k][0] < r + hold:
+                r = max(r, b[k][1])
+                k += 1
+            if hold:
+                b.insert(k, (r, r + hold))
+            at[j] = r - lead
+        return at
+
+    at = place(lambda j: j, pre, False)
+    for _ in range(OPT["rounds"]):
+        end = []
+        for j in range(len(ops)):
+            end.append(max([at[j] + ops[j][6]] + [end[i] for i in pre[j]]))
+        back = place(lambda j: (-end[j], -j), post, True)
+        for j in range(len(ops) - 1, -1, -1):
+            end[j] = max([back[j] + ops[j][6]] + [end[k] for k in post[j]])
+        at = place(lambda j: (-end[j], j), pre, False)
+    ops = [ops[j] for j in sorted(range(len(ops)), key=lambda j: (at[j], j))]
+    total = 0
+    for o in ops:
+        if o[4] is not None and o[4][2] == "remote":
+            total += o[4][1]
+            o[4] = ("sent", total, "remote")
 
     def lane(o):
         return o[0] if o[4] is None else o[4][0]
@@ -558,9 +713,9 @@ def rank_program(g, core, T, topo):
     for j, o in enumerate(ops):
         best = {}
         names = set(x[0] for x in o[2] + o[3])
-        for i in set(i for nm in names for i in touched.get(nm, [])):
+        for i in sorted(set(i for nm in names for i in touched.get(nm, [])), reverse=True):
             e = ops[i]
-            if best.get(lane(e), -1) > i:
+            if lane(e) in best:
                 continue
             same = e[0] == o[0] and e[4] is None and o[4] is None
             if same and o[0] == "P":

@@ -3,14 +3,13 @@ from concourse.mybir import AluOpType as ALU, AxisListType as AX, ActivationFunc
 
 WT = [37, 101, 59, 203, 83, 149, 11, 173, 67, 229, 127, 43, 191, 23, 251, 109]
 STEPS = 4
-OPT = {"lv": 0, "epos": 2, "y0": 16, "vy": 20, "cuts": [48, 80, 104], "nsg": 0, "zlate": 0, "okv": 0, "okn": 0, "si": 0,
-       "ord": "hHccaAccbccBpqccmekrnNPswxjKFlyfzogOVZt", "rounds": 2, "vx": 24,
+OPT = {"vy": 20, "y0": 16, "cuts": [64, 96], "xs": [(16, "V"), (64, "A"), (128, "A")], "rounds": 2, "tu": 1, "one": 0, "vy0": 16,
+       "sg": [], "sgat": 4, "sgb": ["pD0", "pD1"],
        "cost": {"cyc": 0.9, "fix": 25, "least": 55, "pe": 0.68, "gather": 1.3, "scatter": 2.5, "dma": 900, "byte": 0.43,
-                "issue": 350, "fly": 1700, "hop": 150}}
+                "issue": 350, "first": 1500, "fly": [1500, 2400, 1500], "hop": 150}}
 COST = OPT["cost"]
+RW = 16 * max(b - a for a, b in zip([0, min(OPT["vy"], OPT["y0"])] + OPT["cuts"], [OPT["vy"]] + OPT["cuts"] + [128]))
 S = 256
-ZS = 2576
-ZH = 272
 MAGIC = 12582912.0
 
 
@@ -20,30 +19,28 @@ def _sb(cols, dt):
 
 SCRATCH = {
     "X": _sb(2048, "b"), "Di": _sb(512, "i"), "D": _sb(1536, "f"),
-    "yy": _sb(2048, "b"), "xx": _sb(2048, "b"), "ls": _sb(2048, "b"),
+    "yy": _sb(2048, "b"), "xx": _sb(2048, "b"), "hs": _sb(2048, "b"), "ls": _sb(2048, "b"),
     "aa": _sb(2048, "b"), "bb": _sb(2048, "b"), "ad": _sb(2048, "b"),
-    "Z": _sb(STEPS * ZS + 16, "b"), "W": _sb(3 * S + 128, "i"), "Fi": _sb(128, "i"), "zl": _sb(128, "b"),
-    "m1": _sb(256 * STEPS, "u"), "o1": _sb(256 * STEPS, "u"), "o2": _sb(512 * STEPS, "b"),
+    "W": _sb(3 * S + 128, "i"), "Fi": _sb(128, "i"), "zl": _sb(128, "b"),
+    "m1": _sb(256 * STEPS, "u"), "o1": _sb(256 * STEPS, "u"), "m2": _sb(256 * STEPS, "b"), "o2": _sb(256 * STEPS, "b"),
     "m3": _sb(8 * STEPS, "u"), "o3": _sb(16 * STEPS, "u"), "pq": _sb(256, "f"),
-    "A1": _sb(32, "i"), "A2": _sb(8, "i"), "A3": _sb(16, "i"), "m16": _sb(16, "b"), "mask": _sb(256, "b"),
-    "bo": _sb(16, "u"), "bx": _sb(16, "u"), "col": _sb(8, "f"), "wrow": _sb(16, "f"), "mul": _sb(16, "f"),
-    "rmax": _sb(512, "b"), "rmin": _sb(512, "b"), "cM": _sb(256, "b"),
-    "Dq": _sb(8, "b"), "C": _sb(320, "b"),
-    "E": _sb(128, "u"), "dEP": _sb(128, "f"), "u1": _sb(128, "i"), "u2": _sb(128, "i"),
-    "okT": _sb(128, "b"), "okN": _sb(128, "b"), "ms": _sb(128, "f"), "wi": _sb(8, "i"), "wj": _sb(8, "i"),
-    "lb": _sb(128, "b"), "lk": _sb(128, "b"), "of": _sb(16, "u"), "ob": _sb(8, "u"), "tb": _sb(128, "b"), "zt": _sb(128, "b"),
-    "zw": _sb(2 * S + 128, "b"), "DkS": _sb(128, "f"), "key": _sb(128, "f"), "MB": _sb(128, "b"), "mi": _sb(128, "i"),
-    "oS": _sb(128, "f"), "oo": _sb(8, "u"), "vi": _sb(16, "i"), "vj": _sb(16, "i"), "lv": _sb(256, "b"),
-    "t1": _sb(128, "f"), "xn": _sb(128, "i"), "sS": _sb(128, "f"),
+    "A1": _sb(32, "i"), "A2": _sb(8, "i"), "A3": _sb(16, "i"), "m16": _sb(16, "b"),
+    "bo": _sb(8, "u"), "bx": _sb(8, "u"), "b15": _sb(8, "u"), "col": _sb(16, "f"), "wrow": _sb(16, "f"),
+    "rmax": _sb(RW, "b"), "rmin": _sb(RW, "b"), "r8": _sb(128, "b"), "We": _sb(512, "b"),
+    "Dq": _sb(8, "b"), "C": _sb(192, "b"),
+    "E": _sb(128, "u"), "dEP": _sb(128, "f"), "ub": _sb(128, "f"), "u1": _sb(128, "i"), "u2": _sb(128, "i"),
+    "mi": _sb(128, "i"), "wj": _sb(8, "i"), "of": _sb(16, "u"), "ob": _sb(8, "u"), "zw": _sb(2 * S + 128, "b"),
+    "oS": _sb(128, "i"), "oo": _sb(8, "u"), "vi": _sb(16, "i"), "vj": _sb(16, "i"), "vk": _sb(16, "i"),
+    "lO": _sb(8, "b"), "sO": _sb(16, "f"), "t1": _sb(128, "f"), "xn": _sb(128, "i"), "sS": _sb(128, "f"),
 }
-for _n in ("one", "I", "nI", "hI", "nBI", "B", "Wp", "Wn", "RLp", "RLn", "Bk", "Bf", "cf", "krow", "c15", "cq", "half",
-           "M16", "M4k", "c2k", "c32", "r16", "nm"):
+for _n in ("one", "I", "nI", "hI", "nBI", "B", "mask", "Wp", "Wn", "RLp", "RLn", "Bk", "Bf", "cf", "krow", "c15", "cq",
+           "half", "M1", "M16", "M4k", "c2k", "c32", "r16", "nm", "nm2", "okT", "okN", "ns", "lb", "lk", "kN", "tb", "zt"):
     SCRATCH[_n] = _sb(128, "b")
 for _n in ("pA", "pB", "pD0", "pD1", "pD2", "pD3", "pL", "pK"):
     SCRATCH[_n] = ("psum", [128, 512], "float32")
-NDMA = 16
+NDMA = 13
 SEMAPHORES = (["eV", "eA", "eP", "eG", "sent"] + ["d%d" % i for i in range(NDMA)]
-              + ["r%d_%d" % (m, s) for m in (1, 2, 3, 4) for s in range(1, STEPS)])
+              + ["r%d_%d" % (m, s) for m in (1, 2, 3) for s in range(1, STEPS)])
 
 
 def rank_program(g, core, T, topo):
@@ -76,18 +73,18 @@ def rank_program(g, core, T, topo):
     def a_(x):
         return x["ap"] if isinstance(x, dict) else x
 
-    moved, late = [0], []
-
     def add(q, call, out, ins, token=None, both=False):
         xs = [x for x in [out] + ins if isinstance(x, dict) and "n" in x]
         w = max([x["n"] for x in xs] + [1])
         if token is not None:
-            if token[2] == "dma" and not late:
-                moved[0] += w * (2 if xs[0]["t"][1] == "b" else 4)
-            hold, t = {"dma": (60, COST["dma"] + COST["byte"] * (w * 4 if late else moved[0])), "remote": (COST["issue"], COST["issue"]), "arrive": (0, COST["fly"])}[token[2]]
+            if token[2] == "dma":
+                hold = COST["byte"] * w * (2 if xs[0]["t"][1] == "b" else 4) + 80
+                t = COST["dma"] + hold
+            else:
+                hold = t = COST["issue"] if q == "G" else 0
         else:
             if q == "P":
-                t = COST["pe"] * max(64, out["n"]) * (4 if ins[0]["t"][1] == "f" else 1)
+                t = COST["pe"] * max(64, out["n"])
             elif q == "G":
                 t = 170 + 2 * COST["cyc"] * w
             elif "x" in out:
@@ -129,14 +126,8 @@ def rank_program(g, core, T, topo):
         f = AF.Identity if f is None else f
         add("A", lambda e: e.activation(a_(out), a_(x), f, bias=a_(bias), scale=a_(scale)), out, [x, bias, scale])
 
-    group = {}
-
     def mm(out, l, r, start=False, stop=False):
-        end = group[out["r"][0][0]] = [stop]
-        add("P", lambda e: e.matmul(a_(out), a_(l), a_(r), start, end[0]), out, [l, r])
-
-    def close(bank):
-        group[bank][0] = True
+        add("P", lambda e: e.matmul(a_(out), a_(l), a_(r), start, stop), out, [l, r])
 
     def iota(out, pat, base, cm, small=False):
         if small:
@@ -147,11 +138,11 @@ def rank_program(g, core, T, topo):
     def gsel(out, x, pat, op, c, base, cm):
         add("G", lambda e: e.affine_select(a_(out), a_(x), pat, op, c, base, cm), out, [x])
 
-    def gcopy(out, x, w=128):
-        gsel(out, x, [[0, w]], ALU.is_ge, 0.0, 0, 0)
+    def gcopy(out, x):
+        gsel(out, x, [[0, out["n"]]], ALU.is_ge, 0.0, 0, 0)
 
     def gfill(out, c):
-        gsel(out, v("one"), [[0, 128]], ALU.is_gt, c, 0, 0)
+        gsel(out, v("one", 0, out["n"]), [[0, out["n"]]], ALU.is_gt, c, 0, 0)
 
     nd = [0]
 
@@ -162,22 +153,23 @@ def rank_program(g, core, T, topo):
 
     to = [T.cores[(rank + 1) % n], T.cores[(rank + 2) % n]]
     eng = [e for e in topo.engines(core, to[0]) if e in topo.engines(core, to[1])]
+    per = len(eng) // 2
 
-    def send(m, s, src, so, dst, do, w, parts):
-        sem = "r%d_%d" % (m, s + 1)
-        per = len(eng) // parts
+    def send(m, s, so, do, w):
+        sem, src, dst = "r%d_%d" % (m, s + 1), "o%d" % m, "m%d" % m
 
         def call(e):
             trs = []
-            for h in range(parts):
-                rid, pid = topo.addr(to[h % 2], core)
+            for h in range(2):
+                rid, pid = topo.addr(to[h], core)
                 trs.append(RemoteDMATransfer(
                     dst_ids=[DstId(rid=rid, pnc=pid)], dma_engine_mask=sum(1 << x for x in eng[per * h:per * h + per]),
                     remote_sem=T.sem[sem],
                     src=T[src][:, so + w * h:so + w * h + w], dst=T[dst][:, do + w * h:do + w * h + w]))
             return e.remote_dma_fused(trs, local_sem=T.sem.sent)
-        add("G", call, {"r": []}, [v(src, so, so + parts * w)], ("sent", parts * per, "remote"))
-        add("X", None, v(dst, do, do + parts * w), [], (sem, parts * per, "arrive"))
+        add("G", call, {"r": []}, [v(src, so, so + 2 * w)], ("sent", 2 * per, "remote"))
+        add("X", None, v(dst, do, do + 2 * w), [], (sem, 2 * per, "arrive"))
+        ops[-1][6] = COST["fly"][m - 1] + (COST["first"] if s == 0 and m < 3 else 0)
 
     Wm, P1, Po, Qo, Q2 = v("W", 0, 128), v("W", S, S + 128), v("W", 2 * S - 128, 2 * S), v("W", 2 * S, 2 * S + 128), v("W", 3 * S)
     fill(v("Fi"), 0)
@@ -187,18 +179,16 @@ def rank_program(g, core, T, topo):
     dma("S", v("X"), T.xr[:])
     dma("S", v("Di"), T.dr[:])
     dma("S", Po, T.pl[:])
-    late.append(1)
 
     def mk(j):
         return v("m16", j, j + 1)
 
-    Dq, I, nI, hI, m128, cq = v("Dq"), v("I"), v("nI"), v("hI"), v("mask", 0, 128), v("cq")
-    M1 = v("cM", 0, 128)
-    KV = "D" in OPT["ord"]
-    U = -131072.0 if KV else 1.0
-    bo8 = v("bo", 0, 8)
-    CN = ["W8", "W8b", "nW8", "nW8b", "v1", "v1b", "v2", "v2b", "vM", "vMb", "Rm", "c0", "c0b", "Ry", "Ryb", "oM", "oMb",
-          "Rl", "kP", "kQ", "k3", "k4", "aP", "aQ", "a3", "a4", "bP", "bQ", "b3", "b4", "h", "q", "g16", "s1", "s2"]
+    def col(j):
+        return v("col", j, j + 1)
+
+    Dq, I, nI, hI, B, mask, cq, M1, bo = [v(k) for k in ("Dq", "I", "nI", "hI", "B", "mask", "cq", "M1", "bo")]
+    CN = ["kP", "kQ", "kM", "kMb", "aP", "aQ", "bP", "bQ", "sc", "scb", "sw", "swb", "sM", "sMb", "a2", "a16", "h", "q", "g16",
+          "s1", "s2"]
 
     def C(k, w=8):
         a = 8 * CN.index(k)
@@ -206,167 +196,137 @@ def rank_program(g, core, T, topo):
 
     iota(v("A2"), [[-16, 8]], 0, 1)
     iota(v("A1", 0, 16), [[-1, 16]], 128, 1)
-    iota(v("A1", 16, 32), [[0, 16]], 0, 1)
-    iota(v("A3"), [[1, 16]], 0, 0)
-    iota(v("col", 0, 1), [[0, 1]], 0, 1, True)
+    iota(v("A1", 16, 24), [[0, 8]], 0, 1)
+    iota(v("A3", 0, 8), [[1, 8]], 0, 0)
+    iota(col(0), [[0, 1]], 0, 1, True)
     ts(v("A2"), v("A2"), 4, ALU.arith_shift_right)
     fill(v("one"), 1.0)
     ts(Dq, v("A2"), 0.0, ALU.is_equal)
-    ts(v("A1"), v("A1"), 15, ALU.bitwise_and)
+    ts(v("A1", 0, 24), v("A1", 0, 24), 15, ALU.bitwise_and)
     gsel(I, v("one"), [[-1, 128]], ALU.is_equal, 0.0, 0, 1)
     for r in range(0, 16, 2):
         iota(v("wrow", r, r + 2), [[WT[r + 1] - WT[r], 2]], WT[r], 0, True)
-    cp(v("bo"), v("A3"))
+    cp(bo, v("A3", 0, 8))
+    ts(v("b15"), v("A3", 0, 8), 16.0, ALU.mult, 15.0, ALU.add)
     ts(v("m16"), v("A1", 0, 16), 0.0, ALU.is_equal)
-    cp(v("bx"), v("A1", 16, 32))
-    for k, c in (("c0", 256.0), ("c0b", 1024.0), ("Ry", -2.0), ("Ryb", 1.0), ("h", 0.5 * U), ("q", 0.25 * U), ("g16", 16.0)):
+    cp(v("bx"), v("A1", 16, 24))
+    act(mask, ind(v("m16"), v("bx")))
+    act(B, ind(Dq, bo))
+    act(col(4), col(0), scale=16.0)
+    act(col(3), col(0), scale=2.0, bias=256.0)
+    for k, c in (("h", 0.5), ("q", 0.25), ("g16", 16.0), ("sc", 181.0), ("scb", 724.0), ("sw", -10.6875), ("swb", -42.75),
+                 ("a2", col(3)), ("a16", col(4))):
         act(C(k), Dq, scale=c)
-    act(v("mask"), ind(v("m16"), v("bx")))
-    act(v("B"), ind(Dq, bo8))
-    act(v("col", 4, 5), v("col", 0, 1), scale=16.0)
-    act(v("col", 3, 4), v("col", 0, 1), scale=2.0)
-    act(C("Rl"), Dq, scale=-512.0)
-    for k, cP, cQ in (("kP", -float(S), float(S)), ("aP", v("col", 0, 1), v("col", 0, 1)), ("bP", 3.0 * S, 0.0)):
+    for k, c in (("kM", S), ("kMb", S), ("sM", 256), ("sMb", 1024)):
+        fill(C(k), c * MAGIC)
+    for k, cP, cQ in (("kP", -21.375, 21.375), ("aP", col(0), col(0)), ("bP", 3.0 * S - 276.0, 276.0)):
         a = 8 * CN.index(k)
         act(v("C", a, a + 4), v("Dq", 0, 4), scale=cP)
         act(v("C", a + 4, a + 12), Dq, scale=cQ)
         act(v("C", a + 12, a + 16), v("Dq", 4, 8), scale=cP)
-    act(C("a3"), Dq, scale=v("col", 3, 4))
-    act(C("a4"), Dq, scale=v("col", 4, 5))
     act(nI, I, scale=-1.0)
-    act(v("Bk"), v("B"), scale=1.0 / 6.0)
+    act(hI, I, scale=0.5)
+    act(v("Bk"), B, scale=1.0 / 6.0)
     cp(v("m1", 64, 192), Qo)
     fill(v("rmax"), 1.0)
     fill(v("rmin"), 0.0)
-    for k, c in (("v1", 2048.0), ("v1b", 128.0), ("v2", -0.5), ("v2b", 0.5), ("vM", 4096 * MAGIC), ("vMb", 2 * MAGIC),
-                 ("oM", 256 * MAGIC), ("oMb", 128 * MAGIC)):
-        fill(C(k), c)
-    fill(v("rmax", 0, 512, 16), 0.0)
-    fill(v("rmin", 0, 512, 16), 4194304.0)
-    fill(v("mul", 0, 8), 2741.0)
-    fill(v("mul", 8, 16), 32.0)
-    z0, f0 = v("Z", 16, ZH, 2), v("Z", 17, ZH, 2)
-    cp(z0, v("zl"))
-    cp(f0, v("Fi"))
-    ts(C("Rm"), Dq, mk(0), ALU.mult, 128.0, ALU.mult)
+    fill(v("rmax", 0, RW, 16), 0.0)
+    fill(v("rmin", 0, RW, 16), 4194304.0)
+    fill(v("r8"), 1.0)
+    fill(v("r8", 0, 128, 8), 0.0)
+    cp(v("m2", 0, 256, 2), v("zl"))
+    cp(v("m2", 1, 256, 2), v("Fi"))
     tt(v("wrow"), v("wrow"), v("m16"), ALU.mult)
-    ts(v("col", 2, 3), v("A1", 16, 17), 1184.0, ALU.mult)
-    red(v("col", 1, 2), v("wrow"))
-    fill(v("cM"), MAGIC)
-    for k in ("W8", "W8b"):
-        ts(C(k), Dq, v("col", 1, 2), ALU.mult)
-    ts(C("nW8", 16), C("W8", 16), -1.0, ALU.mult)
-    ts(v("Wp"), v("B"), v("col", 1, 2), ALU.mult)
-    ts(v("Wn"), v("B"), v("col", 1, 2), ALU.mult, -1.0, ALU.mult)
-    ts(v("RLp"), v("B"), mk(1), ALU.mult, 0.5 * U, ALU.mult)
-    ts(v("RLn"), v("B"), mk(1), ALU.mult, -0.5 * U, ALU.mult)
+    ts(col(2), v("A1", 16, 17), 1184.0, ALU.mult)
+    red(col(1), v("wrow"))
+    fill(M1, MAGIC)
+    fill(cq, -0.25)
+    ts(v("Wp"), B, col(1), ALU.mult)
+    ts(v("Wn"), B, col(1), ALU.mult, -1.0, ALU.mult)
+    fill(v("We"), 0.0)
+    for e in (2, 3, 0, 1):
+        cp(v("We", 128 * e + e % 2, 128 * e + 128, 2), v("Wp" if e > 1 else "Wn", e % 2, 128, 2))
+    act(v("nm2"), mask, scale=1048576.0, bias=-1048576.0)
+    ts(v("lb"), B, mk(0), ALU.mult, 256.0, ALU.mult)
+    tt(v("nm", 64, 128), v("nm2", 0, 128, 2), v("nm2", 1, 128, 2), ALU.max)
+    act(col(8), mk(1), scale=0.5)
+    act(v("RLp"), B, scale=col(8))
+    act(v("RLn"), v("RLp"), scale=-1.0)
+    act(v("tb", 0, 64), v("mask", 1, 128, 2), scale=4119.5, bias=-4096.0)
+    act(v("dEP", 0, 64), v("mask", 0, 128, 2), scale=4103.5)
+    tt(v("nm", 0, 64), v("dEP", 0, 64), v("tb", 0, 64), ALU.add)
+    act(col(9), mk(0), scale=1.15625)
+    act(col(6), mk(1), scale=0.640625, bias=col(9))
+    act(v("cf"), v("one"), scale=col(6))
+    act(col(5), mk(0), scale=-0.5)
+    act(col(7), mk(0), scale=0.5, bias=mk(1))
+    act(C("s1"), Dq, scale=col(5))
+    act(C("s2"), Dq, scale=col(7))
     gfill(v("c2k"), 2048.0)
     gfill(v("half"), 0.5)
     gfill(v("M4k"), 4096 * MAGIC)
-    gcopy(v("D", 0, 512), v("Di"), 512)
     gfill(v("c32"), 32.0)
-    gfill(v("c15"), -15.25 * U)
-    if KV:
-        gfill(v("MB"), -U * MAGIC)
-    SG = [(3, 1), (3, 0), (2, 1)][:OPT["nsg"]]
-    for m in sorted(set(x[0] for x in SG)):
-        c = 4.0 * len([x for x in SG if x[0] == m])
-        gsel(v("c15", m, 128, 4), v("one", 0, 32), [[0, 32]], ALU.is_gt, (c - 15.25) * U, 0, 0)
+    gfill(v("c15"), -15.25)
+    for m in OPT["sg"]:
+        gfill(v("c15", m, 128, 4), -11.25)
     iota(v("krow"), [[0, 8], [1, 16]], 0, 0, True)
-
-    def late_constants(part):
-        if part == 0:
-            gfill(cq, -0.25)
-            gfill(v("Bf"), 0.0)
-            if not KV:
-                gsel(v("nBI"), v("Bf"), [[-1, 128]], ALU.not_equal, -32768.0 * (1 + OPT["okv"]), 0, 1)
-            gsel(hI, v("half"), [[-1, 128]], ALU.is_equal, 0.0, 0, 1)
-            gfill(v("M16"), 16 * MAGIC)
-            iota(v("r16"), [[16, 128]], 0, 0, True)
-        else:
-            ts(v("col", 5, 6), mk(0), 1.15625, ALU.mult)
-            ts(v("nm"), m128, 4103.5, ALU.mult, -4096.0, ALU.add)
-            ts(v("col", 6, 7), mk(1), 0.640625, ALU.mult, v("col", 5, 6), ALU.add)
-            ts(v("Bf", 0, 128, 16), Dq, -1.0 / 16, ALU.mult)
-            ts(v("Bf", 1, 128, 16), Dq, -1.0 / 32, ALU.mult)
-            ts(v("cf"), v("one"), v("col", 6, 7), ALU.mult)
+    gfill(v("Bf"), 0.0)
+    gsel(v("nBI"), v("Bf"), [[-1, 128]], ALU.not_equal, -32768.0, 0, 1)
+    gfill(v("M16", 0, 64), 16 * MAGIC)
+    iota(v("r16", 0, 64), [[32, 64]], 0, 0, True)
+    gcopy(v("D", 0, 512), v("Di"))
+    ts(v("Bf", 0, 128, 16), Dq, -1.0 / 16, ALU.mult)
+    ts(v("Bf", 1, 128, 16), Dq, -1.0 / 32, ALU.mult)
 
     Xw = v("X")
     DB = (("pD0", "pD1"), ("pD2", "pD3"))
-    pv, po = v("pD1", 128, 144), v("pK", 384, 400)
+    o1_, o2_ = 0, 64
+    pv = v("pB", 64, 128) if OPT["one"] else v("pD1", 0, 64)
 
-    def v_pre(f):
-        mm(pv, I, C("v1", 16), True)
-        mm(pv, I, C("v2", 16))
-        mm(v("pD1", 136, 144), f, C("Rm"))
+    def number(zz, stop=True):
+        for e in range(2):
+            mm(pv, v("We", 256 + 128 * e, 384 + 128 * e), zz[e], False, stop and e == 1)
 
-    def v_post(zn):
-        mm(pv, zn, C("nW8", 16))
-        mm(pv, I, C("vM", 16))
-        mm(pv, nI, C("vM", 16))
-        mm(pv, zn, C("W8", 16), False, True)
-
-    def o_pre(case):
-        mm(po, m128, C("c0", 16), True)
-        if case:
-            mm(v("pK", 392, 400), v("lk"), C("Rl"))
-
-    def o_post():
-        mm(po, v("lv", 128, 256), C("Ry", 16))
-        mm(po, I, C("oM", 16))
-        mm(po, nI, C("oM", 16))
-        mm(v("pK", 384, 392), v("lv", 0, 128), Dq)
-        mm(v("pK", 392, 400), v("lv", 128, 256), Dq)
-        mm(v("pK", 392, 400), m128, C("a3"), False, True)
-
-    def v_int(part):
-        if part == 0:
-            tt(v("vi"), pv, v("mul"), ALU.mult)
-        elif part == 1:
-            ts(v("vj"), v("vi"), 5, ALU.arith_shift_right, 255, ALU.bitwise_and)
+    def columns(out, w):
+        u = v("oS", o2_ + 7, o2_ + 64, 8)
+        if w != -8:
+            ts(v("vi", 0, 8), u, 4095, ALU.bitwise_and)
+        if w != 8:
+            ts(v("vj", 8, 16), u, 1, ALU.bitwise_and)
+        if w != -8:
+            ts(v("vi", 8, 16), v("vi", 0, 8), 2741.0, ALU.mult)
+            ts(v("vj", 0, 8), v("vi", 8, 16), 5, ALU.arith_shift_right, 255, ALU.bitwise_and)
+        a, b = (8, 16) if w < 0 else (0, w)
+        if OPT["tu"]:
+            tt(out, v("vj", a, b), v("sO", a, b), ALU.add)
         else:
-            tt(v("lv"), ind(v("vj"), v("bo")), v("mask"), ALU.mult)
+            tt(v("vk", a, b), v("vj", a, b), v("sO", a, b), ALU.add)
+            cp(out, v("vk", a, b))
 
-    v_pre(f0)
-    v_post(z0)
-    o_pre(False)
-    v_int(0)
+    mm(v("pA", 0, 128), I, v("nm2"), True)
+    mm(v("pA", 0, 128), v("lb"), v("m2", 1, 256, 2), False, True)
+    scan(v("t1"), v("rmax", 0, 128), v("pA", 0, 128), ALU.mult, ALU.max)
+    cp(v("sO", 0, 8), v("t1", 15, 128, 16))
+    mm(pv, I, v("nm", 64, 128), True)
+    number([v("m2", 2 * e, 256, 4) for e in range(2)])
+    scan(v("oS", o2_, o2_ + 64), v("r8", 0, 64), pv, ALU.mult, ALU.max)
+    columns(v("m3", 0, 8), 8)
 
     for s in range(STEPS):
         last = s == STEPS - 1
-        zb = ZS * s
-        z, f = v("Z", zb + 16, zb + ZH, 2), v("Z", zb + 17, zb + ZH, 2)
+        b = 256 * s
+        z, f = v("m2", b, b + 256, 2), v("m2", b + 1, b + 256, 2)
         ce = v("m3", 8 * s, 8 * s + 8)
-        kN, fn = v("o2", 512 * s + 1, 512 * s + 256, 2), v("o2", 512 * s + 257, 512 * s + 512, 2)
-        zn = v("zl") if last else v("o2", 512 * s + 256, 512 * s + 512, 2)
-        pu, pl, pb, pz = v("pL", 256, 384), v("pL", 0, 128), v("pB", 0, 128), v("pD3", 0, 128)
-
-        def hs(a, e, st=1):
-            return v("Z", zb + ZH + a, zb + ZH + e, st)
+        zn, fn = v("zl") if last else v("o2", b, b + 256, 2), v("o2", b + 1, b + 256, 2)
+        pu, pl, pk, pz = v("pL", 256, 384), v("pL", 0, 128), v("pK", 0, 128), v("pD3", 0, 128)
 
         def ends(h, j):
-            return hs(1024 * h + 15, 1024 * h + 1024, 16) if j else v("ls", 1024 * h + 15, 1024 * h + 1024, 16)
-
-        def gy(a, e, q="A"):
-            (act if q == "A" else cp)(v("yy", 16 * a, 16 * e), ind(Xw, v("m1", 256 * s + 64 + a, 256 * s + 64 + e)))
-
-        def sc(a, e, j):
-            if j:
-                scan(hs(16 * a, 16 * e), v("rmax", 0, 16 * (e - a)), v("yy", 16 * a, 16 * e), ALU.mult, ALU.max)
-            else:
-                scan(v("ls", 16 * a, 16 * e), v("rmin", 0, 16 * (e - a)), v("yy", 16 * a, 16 * e), ALU.max, ALU.min)
+            return v(("ls", "hs")[j], 1024 * h + 15, 1024 * h + 1024, 16)
 
         def bcast(h):
             for j in range(2):
                 for kk in range(4):
                     mm(v(("pA", "pB")[h], 256 * j + kk, 256 * j + 256, 4), I, ends(h, j), True, True)
-
-        def gx(a, e, q="A"):
-            (act if q == "A" else cp)(v("xx", 16 * a, 16 * e), ind(Xw, v("E", a, e)))
-
-        def dz(h, m):
-            for kk in range(8):
-                mm(v(DB[h][m], kk, 512, 8), nI, v("Z", zb + 16 + 128 * h, zb + 144 + 128 * h, 2), kk == 0)
 
         def dx(h, m):
             mm(v(DB[h][m]), I, v("xx", 1024 * h + m, 1024 * h + 1024, 2), False, True)
@@ -375,260 +335,197 @@ def rank_program(g, core, T, topo):
             o = 1024 * m + 512 * h
             act(v("ad", o, o + 512), v(DB[h][m]), AF.Abs)
 
-        def sg_fill(i):
-            m, j = SG[i]
-            bank = ("pD0", "pD1", "pD2")[i]
-            for h in range(2):
-                for kk in range(4):
-                    mm(v(bank, 256 * h + kk, 256 * h + 256, 4), I if j else nI, ends(h, j), h + kk == 0)
-            for h in range(2):
-                mm(v(bank, 256 * h, 256 * h + 256), nI if j else I, v("xx", 1024 * h + m, 1024 * h + 1024, 4), False, h == 1)
-
-        def sg(i):
-            m, j = SG[i]
-            act(v(("aa", "bb")[j], 512 * m, 512 * m + 512), v(("pD0", "pD1", "pD2")[i]), AF.Sign, bias=0.5)
-
-        def made(part):
-            if part == 0:
-                tt(v("u1"), pu, Qo, ALU.mult)
-            elif part == 1:
-                ts(v("u2"), v("u1"), v("col", 2, 3), ALU.add)
-            else:
-                ts(Wm, v("u2"), 5, ALU.arith_shift_right, 2047, ALU.bitwise_and)
-
         def sum_d(m):
             for kk in range(8):
                 mm(v("pK", m + 2 * kk, 128, 16), v("ad", 1024 * m + kk, 1024 * m + 1024, 8), C("g16"))
 
-        def cmp(h, m, j):
+        def cmp(h, m, j, k0=0, st=1):
             o = 512 * m + 256 * h
-            tt(v(("aa", "bb")[j], o, o + 256), v("xx", 1024 * h + m, 1024 * h + 1024, 4),
-               v(("pA", "pB")[h], 256 * j, 256 * j + 256), (ALU.is_ge, ALU.is_le)[j])
+            tt(v(("aa", "bb")[j], o + k0, o + 256, st), v("xx", 1024 * h + m + 4 * k0, 1024 * h + 1024, 4 * st),
+               v(("pA", "pB")[h], 256 * j + k0, 256 * j + 256, st), (ALU.is_ge, ALU.is_le)[j])
 
-        def sum_c(m, j):
-            for kk in range(4):
-                mm(v("pL", m + 4 * kk, 128, 16), v(("aa", "bb")[j], 512 * m + kk, 512 * m + 512, 4),
-                   C("q" if (m, j) in SG else "h"))
+        def sum_c(m, j, kk, stop=False):
+            mm(v("pL", m + 4 * kk, 128, 16), v(("aa", "bb")[j], 512 * m + kk, 512 * m + 512, 4),
+               C("q" if j and m in OPT["sg"] else "h"), False, stop)
 
-        vy = OPT["vy"] if s else 0
+        vy = OPT["vy"] if s else OPT["vy0"]
         cuts = [0, vy or OPT["y0"]] + OPT["cuts"] + [128]
-        nq = len(cuts) - 1
-        for q in range(nq):
-            gy(cuts[q], cuts[q + 1], "V" if vy and q == 0 else "A")
+        for a, e in zip(cuts, cuts[1:]):
+            (cp if vy and a == 0 else act)(v("yy", 16 * a, 16 * e), ind(Xw, v("m1", b + 64 + a, b + 64 + e)))
         if s > 0:
             cp(ind(v("D"), v("o3", 16 * s - 8, 16 * s)), P1)
-            gcopy(Qo, v("m1", 256 * s + 64, 256 * s + 192))
+            gcopy(Qo, v("m1", b + 64, b + 192))
             for h in range(2):
-                gcopy(v("W", 2 * S - 128 + 64 * h, 2 * S - 64 + 64 * h), v("m1", 256 * s + 192 * h, 256 * s + 192 * h + 64), 64)
+                gcopy(v("W", 2 * S - 128 + 64 * h, 2 * S - 64 + 64 * h), v("m1", b + 192 * h, b + 192 * h + 64))
         gcopy(Q2, Qo)
-        if s == 0:
-            late_constants(0)
-            v_int(1)
-            sc(cuts[0], cuts[1], 1)
-            v_int(2)
-            o_post()
-        mm(pu, I, v("c2k"), True)
-        mm(pu, nI, v("half"))
-        mm(pu, v("Wn"), z)
-        mm(pu, I, v("M4k"))
-        mm(pu, nI, v("M4k"))
-        mm(pu, v("Wp"), z)
-        mm(pu, I, v("c32"), False, True)
+        for i, (l, r) in enumerate(((I, v("c2k")), (nI, v("half")), (v("Wn"), z), (I, v("M4k")), (nI, v("M4k")),
+                                    (v("Wp"), z), (I, v("c32")))):
+            mm(pu, l, r, i == 0, i == 6)
         for h in range(2):
             for m in range(2):
-                dz(h, m)
-        for q in range(nq):
-            if q == OPT["epos"]:
-                cp(v("E"), ind(v("D", 0, 512), ce))
-            if s or q:
-                sc(cuts[q], cuts[q + 1], 1)
-            sc(cuts[q], cuts[q + 1], 0)
-            if s == 0 and q == 0:
-                cp(ce, v("pK", 384, 392))
-            if cuts[q] < 64 <= cuts[q + 1]:
+                for kk in range(8):
+                    mm(v(DB[h][m], kk, 512, 8), nI, v("m2", b + 128 * h, b + 128 * h + 128, 2), kk == 0)
+        Dw = v("D", 0, 512) if s else v("Di")
+        cp(v("E"), ind(Dw, ce))
+        for a, e in zip(cuts, cuts[1:]):
+            scan(v("hs", 16 * a, 16 * e), v("rmax", 0, 16 * (e - a)), v("yy", 16 * a, 16 * e), ALU.mult, ALU.max)
+            scan(v("ls", 16 * a, 16 * e), v("rmin", 0, 16 * (e - a)), v("yy", 16 * a, 16 * e), ALU.max, ALU.min)
+            if a < 64 <= e:
                 bcast(0)
-            if q == nq - 2:
-                made(0)
-        for i in range(1 if KV else 2 + OPT["okv"]):
-            mm(v("pK", 0, 128), v("B") if i else I, v("c2k") if i else v("krow"), i == 0)
-        mm(pl, I, v("c15"), True)
-        mm(pl, f, v("RLp"))
-        mm(pl, I, v("MB") if KV else M1)
-        mm(pl, nI, v("MB") if KV else M1)
-        mm(pl, f, v("RLn"))
-        if OPT["vx"]:
-            gx(0, OPT["vx"], "V")
-        gx(OPT["vx"], 64)
-        gx(64, 128)
+        act(v("ub"), pu)
+        mm(v("pK", 128, 256), I, v("hs", 15, 2048, 16), True)
+        mm(v("pK", 128, 256), nI, z, False, True)
+        act(v("zw", 0, 128), v("pK", 128, 256))
+        mm(pk, I, v("krow"), True)
+        mm(pk, B, v("c2k"))
+        for i, (l, r) in enumerate(((I, v("c15")), (f, v("RLp")), (I, M1), (nI, M1), (f, v("RLn")))):
+            mm(pl, l, r, i == 0)
+        a = 0
+        for e, q in OPT["xs"]:
+            (cp if q == "V" else act)(v("xx", 16 * a, 16 * e), ind(Xw, v("E", a, e)))
+            a = e
         bcast(1)
-        if s == 0:
-            late_constants(1)
+        ts(v("lO"), ce, 256.0, ALU.is_ge, -256.0, ALU.mult)
 
-        todo = [(m, j) for m in range(4) for j in range(2) if (m, j) not in SG]
         dx(0, 0)
         dx(0, 1)
-        for m, j in todo:
-            cmp(0, m, j)
+        SG = OPT["sg"]
+
+        def sg(h):
+            for m in SG:
+                bank = OPT["sgb"][h]
+                for kk in range(4):
+                    mm(v(bank, kk, 256, 4), I, ends(h, 1), kk == 0)
+                mm(v(bank, 0, 256), nI, v("xx", 1024 * h + m, 1024 * h + 1024, 4), False, True)
+                act(v("bb", 512 * m + 256 * h, 512 * m + 256 * h + 256), v(bank, 0, 256), AF.Sign, bias=0.5)
+
+        for m in range(4):
+            cmp(0, m, 0)
+            if m not in SG:
+                cmp(0, m, 1)
         dx(1, 0)
         dx(1, 1)
         absd(0, 0)
-        if len(SG) > 0:
-            sg_fill(0)
         absd(0, 1)
-        if len(SG) > 1:
-            sg_fill(1)
-        pend = list(todo)
-        for c in OPT["ord"]:
-            if c in "ab":
-                absd(1, "ab".index(c))
-            elif c in "AB":
-                sum_d("AB".index(c))
-            elif c == "c":
-                cmp(1, *pend[0])
-                sum_c(*pend.pop(0))
-            elif c in "012":
-                sg(int(c))
-                sum_c(*SG[int(c)])
-            elif c == "m":
-                made(1)
-                made(2)
-            elif c == "e":
-                tt(v("dEP"), ind(v("D", 0, 512), ce), Po, ALU.subtract)
-            elif c == "k":
-                close("pL")
-                if KV:
-                    tt(v("key"), pl, v("DkS"), ALU.max)
-                    act(v("okT"), v("key"), AF.Sign, bias=65535.5, scale=-1.0)
-                    mm(v("pA", 0, 128), v("okT"), hI, False, True)
-                    continue
-                if OPT["okv"]:
-                    ts(v("okT"), pl, -0.25, ALU.is_ge)
-                else:
-                    act(v("okT"), pl, AF.Sign, bias=0.25)
-                mm(v("pK", 0, 128), v("nBI"), v("okT"))
-                mm(v("pA", 0, 128), v("okT"), I if OPT["okv"] else hI, bool(OPT["okv"]), True)
-            elif c == "n":
-                (cp if OPT["okn"] else act)(v("okN"), v("pA", 0, 128))
-            elif c == "p":
-                mm(v("pD0", 0, 128), I, cq, True)
-                mm(v("pD0", 128, 256), I, v("cf"))
-                mm(v("pD0", 128, 256), I, f)
-                mm(v("pD1", 0, 128), I, cq, True)
-            elif c == "q":
-                mm(v("pD2", 0, 16), m128, C("aP", 16), True)
-                mm(v("pD2", 0, 16), m128, C("bP", 16))
-            elif c == "N":
-                mm(v("pD1", 0, 128), v("okN"), v("Bk"))
-                mm(v("pD1", 0, 128), I, M1)
-                mm(v("pD1", 0, 128), nI, M1, False, True)
-                mm(v("pD0", 0, 128), v("Bk"), v("okN"))
-                mm(v("pD0", 128, 256), v("Bf"), v("okN"))
-                mm(v("pD0", 0, 256), I, v("cM"), False, True)
-            elif c == "x":
-                tt(v("pA", 0, 128), v("pA", 0, 128), v("dEP"), ALU.mult)
-            elif c == "y":
-                tt(P1, v("pA", 0, 128), Po, ALU.add)
-            elif c == "K":
-                tt(v("lk"), v("pD1", 0, 128), m128, ALU.mult)
-                mm(v("pD2", 0, 16), v("lk"), C("kP", 16), False, True)
-            elif c == "F":
-                act(v("o2", 512 * s + 1, 512 * s + 512, 2), v("pD0", 0, 256), bias=-MAGIC)
-            elif c == "f":
-                cp(v("of"), v("pD2", 0, 16))
-            elif c == "z":
-                act(v("zt"), ind(v("zw"), v("of", 4, 12)))
-            elif c == "h":
-                mm(v("pA", 128, 256), I, hs(15, 2048, 16), True)
-                mm(v("pA", 128, 256), nI, z, False, True)
-                act(v("zw", 0, 128), v("pA", 128, 256))
-                act(v("zw", S, S + 128), z, scale=0.5)
-                act(v("zw", 2 * S, 2 * S + 128), z, scale=-1.0)
-            elif c == "H":
-                mm(v("pA", 0, 128), I, v("half"), True)
-            elif c == "D":
-                close("pK")
-                act(v("DkS"), v("pK", 0, 128))
-            elif c == "s":
-                close("pK")
-                scan(v("mi" if OPT["si"] else "ms"), v("rmin", 0, 128), v("key" if KV else "pK", 0, 128), ALU.max, ALU.min)
-            elif c == "r":
-                mm(v("pL", 128, 136), m128, C("a4"), True)
-                mm(pz, I, cq, True)
-            elif c == "w" and not OPT["si"]:
-                cp(v("wi"), v("ms", 15, 128, 16))
-            elif c == "j":
-                ts(v("wj"), v("mi", 15, 128, 16) if OPT["si"] else v("wi"), 15, ALU.bitwise_and)
-            elif c == "l":
-                tt(v("lb"), ind(v("wj"), bo8), m128, ALU.mult)
-                mm(v("pL", 128, 136), v("lb"), Dq, False, True)
-            elif c == "o":
-                cp(v("ob"), v("pL", 128, 136))
-            elif c == "P":
-                mm(pb, I, v("r16"), True)
-                mm(pb, I, v("nm"))
-            elif c == "O":
-                o_pre(True)
-            elif c == "V":
-                v_pre(fn)
-            elif c == "Z":
-                mm(pz, I, v("zt"))
-            elif c == "t":
-                tt(v("tb"), ind(v("xx"), v("ob")), kN, ALU.mult)
-                mm(pz, hI, v("tb"))
-                mm(pz, I, M1, False, True)
-                act(zn, pz, AF.Abs, bias=-MAGIC)
-            elif c == "g" and not last:
-                cp(v("o1", 256 * s, 256 * s + 256), ind(v("W"), v("of", 0, 16)))
-                send(1, s, "o1", 256 * s, "m1", 256 * s + 256, 128, 2)
+        sg(0)
+        act(v("zw", S, S + 128), z, scale=0.5)
+        act(v("zw", 2 * S, 2 * S + 128), z, scale=-1.0)
+        mm(v("pA", 0, 128), I, v("half"), True)
+        todo = [(m, j) for m in range(4) for j in range(2) if not (j and m in SG)]
+        absd(1, 1)
+        sg(1)
+        absd(1, 0)
+        for i, (m, j) in enumerate(todo):
+            fin = i == len(todo) - 1
+            if not fin:
+                cmp(1, m, j)
+            if i == OPT["sgat"]:
+                for m2 in SG:
+                    for kk in range(4):
+                        sum_c(m2, 1, kk)
+            for kk in range(4):
+                if fin:
+                    cmp(1, m, j, kk, 4)
+                sum_c(m, j, kk, fin and kk == 3)
+            if i == 2:
+                sum_d(1)
+            if i == 4:
+                sum_d(0)
+        mm(v("pD0", 0, 128), I, cq, True)
+        mm(v("pD1", 0, 128), I, v("cf"), True)
+        mm(v("pD1", 0, 128), I, f)
+        mm(v("pD2", 0, 16), mask, C("bP", 16), True)
+        tt(v("u1"), v("ub"), Qo, ALU.mult)
+        ts(v("u2"), v("u1"), col(2), ALU.add)
+        ts(Wm, v("u2"), 5, ALU.arith_shift_right, 2047, ALU.bitwise_and)
+        tt(v("dEP"), ind(Dw, ce), Po, ALU.subtract)
+
+        act(v("okT"), pl, AF.Sign, bias=0.25)
+        mm(pk, v("nBI"), v("okT"), False, True)
+        mm(v("pA", 0, 128), v("okT"), hI, False, True)
+        scan(v("ns"), v("rmax", 0, 128), v("okT"), ALU.mult, ALU.add)
+        mm(v("pL", 128, 136), mask, C("a16"), True)
+        mm(pz, I, cq, True)
+        act(v("okN"), v("pA", 0, 128))
+        mm(v("pD0", 0, 128), v("Bk"), v("okN"))
+        mm(v("pD0", 0, 128), I, M1, False, True)
+        mm(v("pD1", 0, 128), v("Bf"), v("okN"))
+        mm(v("pD1", 0, 128), I, M1, False, True)
+        ph = v("pB", 0, 64)
+        mm(ph, I, v("r16", 0, 64), True)
+        mm(ph, I, v("nm", 0, 64))
+        if OPT["one"]:
+            mm(pv, I, v("nm", 64, 128))
+        scan(v("mi"), v("rmin", 0, 128), pk, ALU.max, ALU.min)
+        tt(v("lk"), ind(v("ns"), v("b15")), mask, ALU.mult)
+        for i, (l, r) in enumerate(((v("lk"), C("kP", 16)), (I, C("kM", 16)), (nI, C("kM", 16)), (mask, C("aP", 16)))):
+            mm(v("pD2", 0, 16), l, r, False, i == 3)
+        tt(v("pA", 0, 128), v("pA", 0, 128), v("dEP"), ALU.mult)
+        ts(v("wj"), v("mi", 15, 128, 16), 15, ALU.bitwise_and)
+        act(v("kN"), v("pD0", 0, 128), bias=-MAGIC)
+        cp(v("of"), v("pD2", 0, 16))
+        tt(v("lb"), ind(v("wj"), bo), mask, ALU.mult)
+        mm(v("pL", 128, 136), v("lb"), Dq, False, True)
+        tt(P1, v("pA", 0, 128), Po, ALU.add)
+        act(v("zt"), ind(v("zw"), v("of", 4, 12)))
+        cp(v("ob"), v("pL", 128, 136))
+        if not last:
+            cp(v("o1", b, b + 256), ind(v("W"), v("of")))
+            send(1, s, b, b + 256, 128)
+        act(fn, v("pD1", 0, 128), bias=-MAGIC)
+        po = v("pK", 384, 400)
+        for i, (l, r) in enumerate(((mask, C("sc", 16)), (v("lk"), C("sw", 16)), (I, C("sM", 16)), (nI, C("sM", 16)))):
+            mm(po, l, r, i == 0)
+        mm(v("pK", 384, 392), I, v("lO"))
+        mm(v("pK", 392, 400), I, v("lO"))
+        mm(v("pK", 392, 400), mask, C("a2"), False, True)
+        act(v("sO"), po, AF.Abs)
+        if not OPT["one"]:
+            mm(pv, I, v("nm", 64, 128), True)
+
+        mm(pz, I, v("zt"))
+        tt(v("tb"), ind(v("xx"), v("ob")), v("kN"), ALU.mult)
+        mm(pz, hI, v("tb"))
+        mm(pz, I, M1, False, True)
+        act(zn, pz, AF.Abs, bias=-MAGIC)
         if last:
-            cp(v("pq"), ind(v("W"), v("of", 0, 16)))
+            cp(v("pq"), ind(v("W"), v("of")))
             dma("S", T.yp[:, 0:64], v("pq", 0, 64))
             dma("S", T.yq[:], v("pq", 64, 192))
             dma("S", T.yp[:, 64:128], v("pq", 192, 256))
             dma("S", T.yz[:], zn)
             E8 = slice(0, 8)
-            ps = v("pD2", 128, 256, p=E8)
-            act(C("s1"), C("Rm"), scale=-1.0 / 256)
-            act(v("col", 7, 8), mk(0), scale=0.5, bias=mk(1))
-            act(C("s2"), Dq, scale=v("col", 7, 8))
-            mm(ps, v("nI", 0, 8), cq, True)
-            mm(ps, C("s1"), fn)
-            mm(ps, v("I", 0, 8), M1)
-            mm(ps, v("nI", 0, 8), M1)
-            mm(ps, C("s2"), fn, False, True)
+            ps = v("pA", 128, 256, p=E8)
+            for i, (l, r) in enumerate(((v("nI", 0, 8), cq), (C("s1"), fn), (v("I", 0, 8), M1), (v("nI", 0, 8), M1), (C("s2"), fn))):
+                mm(ps, l, r, i == 0, i == 4)
             act(v("sS", p=E8), ps, scale=2.0)
             dma("S", T.ys[:], v("sS", p=E8))
-        elif not OPT["zlate"]:
-            send(2, s, "o2", 512 * s + 256, "Z", zb + ZS + 16, 128, 2)
-        mm(pb, v("Wn"), zn)
-        mm(pb, I, v("M16"))
-        mm(pb, nI, v("M16"))
-        mm(pb, v("Wp"), zn, False, True)
-        v_post(zn)
-        scan(v("oS"), v("rmax", 0, 128), pb, ALU.mult, ALU.max)
-        v_int(0)
-        cp(v("oo"), v("oS", 15, 128, 16))
-        v_int(1)
-        tt(v("t1"), ind(Xw, v("oo")), zn, ALU.add)
-        if OPT["lv"] == 0:
-            v_int(2)
-            o_post()
-        ts(v("xn"), v("t1"), 0.5, ALU.mult, -0.25, ALU.add)
-        if OPT["lv"] == 1:
-            v_int(2)
-            o_post()
-        cp(ind(Xw, v("oo")), v("xn"))
-        if last:
-            dma("A", T.yx[:], Xw)
-        if OPT["lv"] == 2:
-            v_int(2)
-            o_post()
-        cp(v("o3", 16 * s, 16 * s + 16), po)
-        if not last:
-            send(3, s, "o3", 16 * s, "m3", 8 * s + 8, 4, 2)
-            if OPT["zlate"]:
-                send(2, s, "o2", 512 * s + 256, "Z", zb + ZS + 16, 128, 2)
         else:
+            send(2, s, b, b + 256, 128)
+
+        zz = [v("zl", e, 128, 2) if last else v("o2", b + 2 * e, b + 256, 4) for e in range(2)]
+        for e in range(2):
+            mm(ph, v("We", 128 * e, 128 * e + 128), zz[e])
+        mm(ph, I, v("M16", 0, 64))
+        mm(ph, nI, v("M16", 0, 64))
+        for e in range(2):
+            mm(ph, v("We", 256 + 128 * e, 384 + 128 * e), zz[e], False, e == 1 and not OPT["one"])
+        number(zz)
+        if OPT["one"]:
+            scan(v("oS"), v("r8"), v("pB", 0, 128), ALU.mult, ALU.max)
+        else:
+            scan(v("oS", o1_, o1_ + 64), v("r8", 0, 64), ph, ALU.mult, ALU.max)
+            scan(v("oS", o2_, o2_ + 64), v("r8", 0, 64), pv, ALU.mult, ALU.max)
+        cp(v("oo"), v("oS", o1_ + 7, o1_ + 64, 8))
+        tt(v("t1"), ind(Xw, v("oo")), zn, ALU.add)
+        ts(v("xn"), v("t1"), 0.5, ALU.mult, -0.25, ALU.add)
+        cp(ind(Xw, v("oo")), v("xn"))
+        if not last:
+            columns(v("o3", 16 * s, 16 * s + 16), 16)
+            send(3, s, 16 * s, 8 * s + 8, 4)
+        else:
+            columns(v("o3", 16 * s + 8, 16 * s + 16), -8)
+            dma("A", T.yx[:], Xw)
             cp(ind(v("D"), v("o3", 16 * s + 8, 16 * s + 16)), P1)
             dma("S", T.yd[:], v("D", 0, 512))
 
@@ -657,12 +554,13 @@ def rank_program(g, core, T, topo):
             seen.setdefault(nm, []).append(j)
         if o[0] == "X":
             p.add(j - 1)
-        if o[4] is not None and o[0] != "X":
-            k = o[4][2]
+        elif o[0] == "G" or o[4] is not None:
+            k = "G" if o[0] == "G" else "dma"
             if k in seen and seen[k] not in p:
                 p.add(seen[k])
                 soft.add((seen[k], j))
-            seen[k] = j
+            if o[4] is not None:
+                seen[k] = j
         pre.append(p)
     post = [[] for _ in ops]
     for j, p in enumerate(pre):
@@ -676,7 +574,7 @@ def rank_program(g, core, T, topo):
             r = max([at[i] + (ops[i][5] if (min(i, j), max(i, j)) in soft else
                               ops[i][6] + (0 if ops[i][0] == q == "P" else COST["hop"])) for i in before[j]] + [0.0])
             lead = t - hold if flip else 0.0
-            b = busy.setdefault(q, [])
+            b = busy.setdefault("S" if ops[j][4] is not None and q == "A" else q, [])
             k = 0
             r += lead
             while k < len(b) and b[k][0] < r + hold:
@@ -720,7 +618,7 @@ def rank_program(g, core, T, topo):
             same = e[0] == o[0] and e[4] is None and o[4] is None
             if same and o[0] == "P":
                 continue
-            if meet(e[3], o[2]) or meet(e[3], o[3]) or meet(e[2], o[3]) or (not same and bk[i] & bk[j]):
+            if clash(e, o) or (not same and bk[i] & bk[j]):
                 best[lane(e)] = i
         for nm in names:
             touched.setdefault(nm, []).append(j)

@@ -3,44 +3,49 @@ from concourse.mybir import AluOpType as ALU, AxisListType as AX, ActivationFunc
 
 WT = [37, 101, 59, 203, 83, 149, 11, 173, 67, 229, 127, 43, 191, 23, 251, 109]
 STEPS = 4
-OPT = {"vy": 20, "y0": 16, "cuts": [64, 96], "xs": [(16, "V"), (64, "A"), (128, "A")], "rounds": 2, "tu": 1, "one": 0, "vy0": 16,
-       "sg": [], "sgat": 4, "sgb": ["pD0", "pD1"],
-       "cost": {"cyc": 0.9, "fix": 25, "least": 55, "pe": 0.68, "gather": 1.3, "scatter": 2.5, "dma": 900, "byte": 0.43,
-                "issue": 350, "first": 1500, "fly": [1500, 2400, 1500], "hop": 150}}
+OPT = {"vy": 20, "cuts": [64, 96], "xs": [(16, "V"), (64, "A"), (128, "A")], "rounds": 2, "vy0": 16,
+       "cmp": [(0, 0), (0, 1), (0, 2), (0, 3), (1, 0), (1, 1), (1, 2), (1, 3)], "abs": [(0, 0), (0, 1), (1, 1), (1, 0)],
+       "sd": [5, 6], "fin": 4, "pe": "pA",
+       "cost": {"cyc": 0.9, "fix": 25, "least": 55, "pe": 0.72, "gather": 1.3, "scatter": 2.5, "dma": 900, "byte": 0.43,
+                "issue": 350, "first": 1500, "fly": [1500, 1700, 1500, 2000], "hop": 150}}
 COST = OPT["cost"]
-RW = 16 * max(b - a for a, b in zip([0, min(OPT["vy"], OPT["y0"])] + OPT["cuts"], [OPT["vy"]] + OPT["cuts"] + [128]))
+RW = 16 * max(b - a for a, b in zip([0, min(OPT["vy"], OPT["vy0"])] + OPT["cuts"], [OPT["vy"]] + OPT["cuts"] + [128]))
 S = 256
 MAGIC = 12582912.0
+XO, AO = 16, 2064
+ZO = 3072.0
+KF = 131072.0
 
 
 def _sb(cols, dt):
-    return ("sbuf", [128, cols], {"b": "bfloat16", "f": "float32", "i": "int32", "u": "uint16"}[dt])
+    return ("sbuf", [128, cols], {"b": "bfloat16", "f": "float32", "i": "int32", "u": "uint16", "h": "float16"}[dt])
 
 
 SCRATCH = {
     "X": _sb(2048, "b"), "Di": _sb(512, "i"), "D": _sb(1536, "f"),
-    "yy": _sb(2048, "b"), "xx": _sb(2048, "b"), "hs": _sb(2048, "b"), "ls": _sb(2048, "b"),
-    "aa": _sb(2048, "b"), "bb": _sb(2048, "b"), "ad": _sb(2048, "b"),
-    "W": _sb(3 * S + 128, "i"), "Fi": _sb(128, "i"), "zl": _sb(128, "b"),
-    "m1": _sb(256 * STEPS, "u"), "o1": _sb(256 * STEPS, "u"), "m2": _sb(256 * STEPS, "b"), "o2": _sb(256 * STEPS, "b"),
+    "yy": _sb(2048, "b"), "xw": _sb(AO + 2048, "b"), "hs": _sb(2048, "b"), "ls": _sb(2048, "b"),
+    "aa": _sb(2048, "b"), "bb": _sb(2048, "b"), "z2": _sb(128, "h"), "zt": _sb(128, "f"), "x2": _sb(128, "h"),
+    "E16": _sb(128, "h"), "P16": _sb(128, "h"), "I16": _sb(128, "h"), "nI16": _sb(128, "h"), "W": _sb(2 * S + 128, "f"), "Fi": _sb(128, "i"), "zl": _sb(128, "b"),
+    "m4": _sb(128 * STEPS, "f"), "o4": _sb(128 * STEPS, "f"),
+    "m1": _sb(128 * STEPS, "u"), "o1": _sb(128 * STEPS, "u"), "m2": _sb(256 * STEPS, "b"), "o2": _sb(256 * STEPS, "b"),
     "m3": _sb(8 * STEPS, "u"), "o3": _sb(16 * STEPS, "u"), "pq": _sb(256, "f"),
     "A1": _sb(32, "i"), "A2": _sb(8, "i"), "A3": _sb(16, "i"), "m16": _sb(16, "b"),
     "bo": _sb(8, "u"), "bx": _sb(8, "u"), "b15": _sb(8, "u"), "col": _sb(16, "f"), "wrow": _sb(16, "f"),
-    "rmax": _sb(RW, "b"), "rmin": _sb(RW, "b"), "r8": _sb(128, "b"), "We": _sb(512, "b"),
+    "rmax": _sb(RW, "b"), "rmin": _sb(RW, "b"), "r8": _sb(128, "b"), "We": _sb(512, "h"),
     "Dq": _sb(8, "b"), "C": _sb(192, "b"),
-    "E": _sb(128, "u"), "dEP": _sb(128, "f"), "ub": _sb(128, "f"), "u1": _sb(128, "i"), "u2": _sb(128, "i"),
+    "E": _sb(128, "u"), "dEP": _sb(128, "f"), "u1": _sb(128, "i"), "u2": _sb(128, "i"),
     "mi": _sb(128, "i"), "wj": _sb(8, "i"), "of": _sb(16, "u"), "ob": _sb(8, "u"), "zw": _sb(2 * S + 128, "b"),
-    "oS": _sb(128, "i"), "oo": _sb(8, "u"), "vi": _sb(16, "i"), "vj": _sb(16, "i"), "vk": _sb(16, "i"),
-    "lO": _sb(8, "b"), "sO": _sb(16, "f"), "t1": _sb(128, "f"), "xn": _sb(128, "i"), "sS": _sb(128, "f"),
+    "oS": _sb(128, "i"), "oo": _sb(8, "u"), "vi": _sb(16, "i"), "vj": _sb(16, "i"),
+    "lO": _sb(8, "b"), "sO": _sb(16, "f"), "t1": _sb(128, "f"), "xn": _sb(128, "b"), "sS": _sb(128, "f"),
 }
-for _n in ("one", "I", "nI", "hI", "nBI", "B", "mask", "Wp", "Wn", "RLp", "RLn", "Bk", "Bf", "cf", "krow", "c15", "cq",
-           "half", "M1", "M16", "M4k", "c2k", "c32", "r16", "nm", "nm2", "okT", "okN", "ns", "lb", "lk", "kN", "tb", "zt"):
+for _n in ("one", "nBI", "c32k", "I", "nI", "J", "B", "mask", "Wp", "Wn", "RLp", "Bf", "cf", "krow", "c15",
+           "M1", "M16", "M4k", "c2k", "c32", "r16", "nm", "nm2", "okT", "okN", "ns", "lb", "lk", "tb"):
     SCRATCH[_n] = _sb(128, "b")
 for _n in ("pA", "pB", "pD0", "pD1", "pD2", "pD3", "pL", "pK"):
     SCRATCH[_n] = ("psum", [128, 512], "float32")
-NDMA = 13
+NDMA = 12
 SEMAPHORES = (["eV", "eA", "eP", "eG", "sent"] + ["d%d" % i for i in range(NDMA)]
-              + ["r%d_%d" % (m, s) for m in (1, 2, 3) for s in range(1, STEPS)])
+              + ["r%d_%d" % (m, s) for m in (1, 2, 3, 4) for s in range(1, STEPS)])
 
 
 def rank_program(g, core, T, topo):
@@ -58,7 +63,8 @@ def rank_program(g, core, T, topo):
         cs = slice(a, b, st) if st != 1 else slice(a, b)
         ap = t[:, cs] if p is None else t[p, cs]
         bits = ((1 << b) - (1 << a)) if st == 1 else sum(1 << c for c in range(a, b, st))
-        return {"ap": ap, "r": [(name, bits)], "n": len(range(a, b, st)), "t": SCRATCH[name][0][0] + SCRATCH[name][2][0]}
+        return {"ap": ap, "r": [(name, bits)], "n": len(range(a, b, st)),
+                "t": SCRATCH[name][0][0] + ("b" if SCRATCH[name][2][-2:] == "16" else "f")}
 
     def ind(win, off):
         return {"ap": win["ap"].indirect(off["ap"]), "r": win["r"], "x": off["r"], "n": 16 * off["n"], "t": win["t"]}
@@ -95,7 +101,7 @@ def rank_program(g, core, T, topo):
                 r = 1.0
                 if both and all(x["t"][0] == "s" for x in xs[1:]):
                     r = 2.0
-                elif q == "V" and not both and all(x["t"][1] in "bu" for x in xs if x["n"] > 1):
+                elif q == "V" and not both and all(x["t"][1] == "b" for x in xs if x["n"] > 1):
                     r = 0.5
                 t = max(COST["least"], COST["fix"] + COST["cyc"] * r * w)
             hold = t
@@ -128,6 +134,10 @@ def rank_program(g, core, T, topo):
 
     def mm(out, l, r, start=False, stop=False):
         add("P", lambda e: e.matmul(a_(out), a_(l), a_(r), start, stop), out, [l, r])
+
+    def mms(out, pairs, start=True, stop=True):
+        for i, (l, r) in enumerate(pairs):
+            mm(out, l, r, start and i == 0, stop and i == len(pairs) - 1)
 
     def iota(out, pat, base, cm, small=False):
         if small:
@@ -171,9 +181,9 @@ def rank_program(g, core, T, topo):
         add("X", None, v(dst, do, do + 2 * w), [], (sem, 2 * per, "arrive"))
         ops[-1][6] = COST["fly"][m - 1] + (COST["first"] if s == 0 and m < 3 else 0)
 
-    Wm, P1, Po, Qo, Q2 = v("W", 0, 128), v("W", S, S + 128), v("W", 2 * S - 128, 2 * S), v("W", 2 * S, 2 * S + 128), v("W", 3 * S)
+    Wm, P1, Po, Qo = v("W", 0, 128), v("W", S, S + 128), v("u2"), v("W", 2 * S, 2 * S + 128)
     fill(v("Fi"), 0)
-    dma("A", Qo, T.ql[:])
+    dma("A", v("u1"), T.ql[:])
     dma("S", v("zl"), T.zq[:])
     dma("S", v("Fi", p=slice(0, 128, 16)), T.sd[:])
     dma("S", v("X"), T.xr[:])
@@ -186,9 +196,9 @@ def rank_program(g, core, T, topo):
     def col(j):
         return v("col", j, j + 1)
 
-    Dq, I, nI, hI, B, mask, cq, M1, bo = [v(k) for k in ("Dq", "I", "nI", "hI", "B", "mask", "cq", "M1", "bo")]
-    CN = ["kP", "kQ", "kM", "kMb", "aP", "aQ", "bP", "bQ", "sc", "scb", "sw", "swb", "sM", "sMb", "a2", "a16", "h", "q", "g16",
-          "s1", "s2"]
+    Dq, I, nI, B, mask, M1, bo = [v(k) for k in ("Dq", "I", "nI", "B", "mask", "M1", "bo")]
+    CN = ["kP", "kQ", "kM", "kMb", "aP", "aQ", "bP", "bQ", "sc", "scb", "sw", "swb", "sM", "sMb", "a2", "a16", "h", "g8",
+          "s2", "kX", "bX", "xM"]
 
     def C(k, w=8):
         a = 8 * CN.index(k)
@@ -212,83 +222,85 @@ def rank_program(g, core, T, topo):
     cp(v("bx"), v("A1", 16, 24))
     act(mask, ind(v("m16"), v("bx")))
     act(B, ind(Dq, bo))
-    act(col(4), col(0), scale=16.0)
+    act(col(4), col(0), scale=16.0, bias=float(XO))
     act(col(3), col(0), scale=2.0, bias=256.0)
-    for k, c in (("h", 0.5), ("q", 0.25), ("g16", 16.0), ("sc", 181.0), ("scb", 724.0), ("sw", -10.6875), ("swb", -42.75),
-                 ("a2", col(3)), ("a16", col(4))):
+    for k, c in (("h", -1.0), ("g8", 8.0), ("sc", 181.0), ("scb", 724.0), ("sw", -10.6875), ("swb", -42.75),
+                 ("kX", 171.0), ("bX", 176.0), ("a2", col(3)), ("a16", col(4))):
         act(C(k), Dq, scale=c)
-    for k, c in (("kM", S), ("kMb", S), ("sM", 256), ("sMb", 1024)):
+    for k, c in (("kM", S), ("kMb", S), ("sM", 256), ("sMb", 1024), ("xM", 2048)):
         fill(C(k), c * MAGIC)
-    for k, cP, cQ in (("kP", -21.375, 21.375), ("aP", col(0), col(0)), ("bP", 3.0 * S - 276.0, 276.0)):
-        a = 8 * CN.index(k)
-        act(v("C", a, a + 4), v("Dq", 0, 4), scale=cP)
-        act(v("C", a + 4, a + 12), Dq, scale=cQ)
-        act(v("C", a + 12, a + 16), v("Dq", 4, 8), scale=cP)
+    for k, c in (("kP", -10.6875), ("kQ", 21.375), ("aP", col(0)), ("aQ", col(0)), ("bP", 436.0), ("bQ", 276.0)):
+        act(C(k), Dq, scale=c)
     act(nI, I, scale=-1.0)
-    act(hI, I, scale=0.5)
-    act(v("Bk"), B, scale=1.0 / 6.0)
-    cp(v("m1", 64, 192), Qo)
+    cp(v("m1", 0, 128), v("u1"))
+    gcopy(Qo, v("u1"))
     fill(v("rmax"), 1.0)
     fill(v("rmin"), 0.0)
     fill(v("rmax", 0, RW, 16), 0.0)
     fill(v("rmin", 0, RW, 16), 4194304.0)
     fill(v("r8"), 1.0)
     fill(v("r8", 0, 128, 8), 0.0)
+    fill(v("xw", 0, XO), 0.0)
     cp(v("m2", 0, 256, 2), v("zl"))
+    ts(v("z2"), v("zl"), 2.0, ALU.mult, ZO, ALU.add)
     cp(v("m2", 1, 256, 2), v("Fi"))
     tt(v("wrow"), v("wrow"), v("m16"), ALU.mult)
     ts(col(2), v("A1", 16, 17), 1184.0, ALU.mult)
     red(col(1), v("wrow"))
     fill(M1, MAGIC)
-    fill(cq, -0.25)
     ts(v("Wp"), B, col(1), ALU.mult)
-    ts(v("Wn"), B, col(1), ALU.mult, -1.0, ALU.mult)
+    act(v("Wn"), v("Wp"), scale=-1.0)
     fill(v("We"), 0.0)
     for e in (2, 3, 0, 1):
-        cp(v("We", 128 * e + e % 2, 128 * e + 128, 2), v("Wp" if e > 1 else "Wn", e % 2, 128, 2))
+        ts(v("We", 128 * e + e % 2, 128 * e + 128, 2), v("Wp", e % 2, 128, 2), 0.5 if e > 1 else -0.5, ALU.mult)
     act(v("nm2"), mask, scale=1048576.0, bias=-1048576.0)
     ts(v("lb"), B, mk(0), ALU.mult, 256.0, ALU.mult)
     tt(v("nm", 64, 128), v("nm2", 0, 128, 2), v("nm2", 1, 128, 2), ALU.max)
-    act(col(8), mk(1), scale=0.5)
-    act(v("RLp"), B, scale=col(8))
-    act(v("RLn"), v("RLp"), scale=-1.0)
     act(v("tb", 0, 64), v("mask", 1, 128, 2), scale=4119.5, bias=-4096.0)
     act(v("dEP", 0, 64), v("mask", 0, 128, 2), scale=4103.5)
     tt(v("nm", 0, 64), v("dEP", 0, 64), v("tb", 0, 64), ALU.add)
+    act(col(8), mk(2))
+    act(v("RLp"), B, scale=col(8))
+    act(col(5), mk(1), bias=mk(2))
     act(col(9), mk(0), scale=1.15625)
-    act(col(6), mk(1), scale=0.640625, bias=col(9))
+    act(col(6), col(5), scale=0.640625, bias=col(9))
     act(v("cf"), v("one"), scale=col(6))
-    act(col(5), mk(0), scale=-0.5)
-    act(col(7), mk(0), scale=0.5, bias=mk(1))
-    act(C("s1"), Dq, scale=col(5))
+    act(col(7), mk(1), scale=2.0, bias=mk(0))
     act(C("s2"), Dq, scale=col(7))
-    gfill(v("c2k"), 2048.0)
-    gfill(v("half"), 0.5)
+    act(col(10), mk(1), scale=2.0, bias=-1.0)
+    act(v("J"), I, scale=col(10))
+    act(col(11), mk(1), scale=-0.5)
+    act(col(12), mk(0), scale=2048.0, bias=col(11))
+    act(v("c2k"), v("one"), scale=col(12))
     gfill(v("M4k"), 4096 * MAGIC)
     gfill(v("c32"), 32.0)
-    gfill(v("c15"), -15.25)
-    for m in OPT["sg"]:
-        gfill(v("c15", m, 128, 4), -11.25)
+    gfill(v("c15"), 30.0)
+    gfill(v("c32k"), 32768.0)
+    gcopy(v("P16"), Po)
+    act(v("nBI"), I, scale=-32768.0)
+    cp(v("I16"), I)
+    cp(v("nI16"), nI)
     iota(v("krow"), [[0, 8], [1, 16]], 0, 0, True)
     gfill(v("Bf"), 0.0)
-    gsel(v("nBI"), v("Bf"), [[-1, 128]], ALU.not_equal, -32768.0, 0, 1)
+    gfill(v("zw", 2 * S, 2 * S + 128), 0.0)
     gfill(v("M16", 0, 64), 16 * MAGIC)
     iota(v("r16", 0, 64), [[32, 64]], 0, 0, True)
     gcopy(v("D", 0, 512), v("Di"))
-    ts(v("Bf", 0, 128, 16), Dq, -1.0 / 16, ALU.mult)
-    ts(v("Bf", 1, 128, 16), Dq, -1.0 / 32, ALU.mult)
+    for r, c in enumerate((16, 32, 32)):
+        act(v("Bf", r, 128, 16), Dq, scale=-1.0 / c)
 
     Xw = v("X")
     DB = (("pD0", "pD1"), ("pD2", "pD3"))
-    o1_, o2_ = 0, 64
-    pv = v("pB", 64, 128) if OPT["one"] else v("pD1", 0, 64)
+    pv, ph = v("pD1", 0, 64), v("pB", 0, 64)
+    zz = [v("z2", e, 128, 2) for e in range(2)]
 
-    def number(zz, stop=True):
+    def weights(out, neg, stop):
         for e in range(2):
-            mm(pv, v("We", 256 + 128 * e, 384 + 128 * e), zz[e], False, stop and e == 1)
+            a = 128 * e + (0 if neg else 256)
+            mm(out, v("We", a, a + 128), zz[e], False, stop and e == 1)
 
     def columns(out, w):
-        u = v("oS", o2_ + 7, o2_ + 64, 8)
+        u = v("oS", 64 + 7, 128, 8)
         if w != -8:
             ts(v("vi", 0, 8), u, 4095, ALU.bitwise_and)
         if w != 8:
@@ -297,28 +309,29 @@ def rank_program(g, core, T, topo):
             ts(v("vi", 8, 16), v("vi", 0, 8), 2741.0, ALU.mult)
             ts(v("vj", 0, 8), v("vi", 8, 16), 5, ALU.arith_shift_right, 255, ALU.bitwise_and)
         a, b = (8, 16) if w < 0 else (0, w)
-        if OPT["tu"]:
-            tt(out, v("vj", a, b), v("sO", a, b), ALU.add)
-        else:
-            tt(v("vk", a, b), v("vj", a, b), v("sO", a, b), ALU.add)
-            cp(out, v("vk", a, b))
+        tt(out, v("vj", a, b), v("sO", a, b), ALU.add)
 
-    mm(v("pA", 0, 128), I, v("nm2"), True)
-    mm(v("pA", 0, 128), v("lb"), v("m2", 1, 256, 2), False, True)
+    mms(v("pA", 0, 128), ((I, v("nm2")), (v("lb"), v("m2", 1, 256, 2))))
     scan(v("t1"), v("rmax", 0, 128), v("pA", 0, 128), ALU.mult, ALU.max)
     cp(v("sO", 0, 8), v("t1", 15, 128, 16))
     mm(pv, I, v("nm", 64, 128), True)
-    number([v("m2", 2 * e, 256, 4) for e in range(2)])
-    scan(v("oS", o2_, o2_ + 64), v("r8", 0, 64), pv, ALU.mult, ALU.max)
+    weights(pv, False, True)
+    scan(v("oS", 64, 128), v("r8", 0, 64), pv, ALU.mult, ALU.max)
     columns(v("m3", 0, 8), 8)
 
     for s in range(STEPS):
         last = s == STEPS - 1
-        b = 256 * s
+        b, c = 256 * s, 128 * s
         z, f = v("m2", b, b + 256, 2), v("m2", b + 1, b + 256, 2)
         ce = v("m3", 8 * s, 8 * s + 8)
         zn, fn = v("zl") if last else v("o2", b, b + 256, 2), v("o2", b + 1, b + 256, 2)
-        pu, pl, pk, pz = v("pL", 256, 384), v("pL", 0, 128), v("pK", 0, 128), v("pD3", 0, 128)
+        pu, pl, pk, pe = v("pL", 256, 384), v("pL", 0, 128), v("pK", 0, 128), v(OPT["pe"], 256, 384)
+
+        def xx(a, e, st=1):
+            return v("xw", XO + a, XO + e, st)
+
+        def ad(a, e, st=1):
+            return v("xw", AO + a, AO + e, st)
 
         def ends(h, j):
             return v(("ls", "hs")[j], 1024 * h + 15, 1024 * h + 1024, 16)
@@ -328,39 +341,34 @@ def rank_program(g, core, T, topo):
                 for kk in range(4):
                     mm(v(("pA", "pB")[h], 256 * j + kk, 256 * j + 256, 4), I, ends(h, j), True, True)
 
-        def dx(h, m):
-            mm(v(DB[h][m]), I, v("xx", 1024 * h + m, 1024 * h + 1024, 2), False, True)
-
         def absd(h, m):
-            o = 1024 * m + 512 * h
-            act(v("ad", o, o + 512), v(DB[h][m]), AF.Abs)
+            mm(v(DB[h][m]), I, xx(1024 * h + m, 1024 * h + 1024, 2), False, True)
+            act(ad(1024 * h + m, 1024 * h + 1024, 2), v(DB[h][m]), AF.Abs, scale=2.0)
 
-        def sum_d(m):
+        def sum_d(m, stop):
             for kk in range(8):
-                mm(v("pK", m + 2 * kk, 128, 16), v("ad", 1024 * m + kk, 1024 * m + 1024, 8), C("g16"))
+                mm(v("pK", m + 2 * kk, 128, 16), ad(m + 2 * kk, 2048, 16), C("g8"), False, stop and kk == 7)
 
         def cmp(h, m, j, k0=0, st=1):
             o = 512 * m + 256 * h
-            tt(v(("aa", "bb")[j], o + k0, o + 256, st), v("xx", 1024 * h + m + 4 * k0, 1024 * h + 1024, 4 * st),
+            tt(v(("aa", "bb")[j], o + k0, o + 256, st), xx(1024 * h + m + 4 * k0, 1024 * h + 1024, 4 * st),
                v(("pA", "pB")[h], 256 * j + k0, 256 * j + 256, st), (ALU.is_ge, ALU.is_le)[j])
 
         def sum_c(m, j, kk, stop=False):
-            mm(v("pL", m + 4 * kk, 128, 16), v(("aa", "bb")[j], 512 * m + kk, 512 * m + 512, 4),
-               C("q" if j and m in OPT["sg"] else "h"), False, stop)
+            mm(v("pL", m + 4 * kk, 128, 16), v(("aa", "bb")[j], 512 * m + kk, 512 * m + 512, 4), C("h"), False, stop)
 
         vy = OPT["vy"] if s else OPT["vy0"]
-        cuts = [0, vy or OPT["y0"]] + OPT["cuts"] + [128]
+        cuts = [0, vy] + OPT["cuts"] + [128]
         for a, e in zip(cuts, cuts[1:]):
-            (cp if vy and a == 0 else act)(v("yy", 16 * a, 16 * e), ind(Xw, v("m1", b + 64 + a, b + 64 + e)))
+            (cp if a == 0 else act)(v("yy", 16 * a, 16 * e), ind(Xw, v("m1", c + a, c + e)))
         if s > 0:
             cp(ind(v("D"), v("o3", 16 * s - 8, 16 * s)), P1)
-            gcopy(Qo, v("m1", b + 64, b + 192))
-            for h in range(2):
-                gcopy(v("W", 2 * S - 128 + 64 * h, 2 * S - 64 + 64 * h), v("m1", b + 192 * h, b + 192 * h + 64))
-        gcopy(Q2, Qo)
-        for i, (l, r) in enumerate(((I, v("c2k")), (nI, v("half")), (v("Wn"), z), (I, v("M4k")), (nI, v("M4k")),
-                                    (v("Wp"), z), (I, v("c32")))):
-            mm(pu, l, r, i == 0, i == 6)
+            gcopy(Qo, v("m1", c, c + 128))
+        gcopy(v("zw", S, S + 128), z)
+        if s > 0:
+            gcopy(v("P16"), v("m4", c, c + 128))
+        mms(pu, ((B, v("c2k")), (v("Wn"), z), (I, v("M4k")), (nI, v("M4k")), (v("Wp"), z), (I, v("c32"))))
+        tt(v("u1"), pu, Qo, ALU.mult)
         for h in range(2):
             for m in range(2):
                 for kk in range(8):
@@ -372,157 +380,108 @@ def rank_program(g, core, T, topo):
             scan(v("ls", 16 * a, 16 * e), v("rmin", 0, 16 * (e - a)), v("yy", 16 * a, 16 * e), ALU.max, ALU.min)
             if a < 64 <= e:
                 bcast(0)
-        act(v("ub"), pu)
-        mm(v("pK", 128, 256), I, v("hs", 15, 2048, 16), True)
-        mm(v("pK", 128, 256), nI, z, False, True)
-        act(v("zw", 0, 128), v("pK", 128, 256))
-        mm(pk, I, v("krow"), True)
-        mm(pk, B, v("c2k"))
-        for i, (l, r) in enumerate(((I, v("c15")), (f, v("RLp")), (I, M1), (nI, M1), (f, v("RLn")))):
-            mm(pl, l, r, i == 0)
+        mms(v("pK", 128, 256), ((I, v("hs", 15, 2048, 16)), (nI, z)))
+        act(v("zw", 0, 128), v("pK", 128, 256), AF.Abs, scale=2.0)
+        if OPT["pe"] != "pA":
+            cp(v("E16"), v("E"))
+            mms(pe, ((v("I16"), v("E16")), (v("nI16"), v("P16"))))
+        mms(pk, ((I, v("krow")), (I, v("c32k"))), True, False)
+        mms(pl, ((I, v("c15")), (f, v("RLp"))), True, False)
         a = 0
         for e, q in OPT["xs"]:
-            (cp if q == "V" else act)(v("xx", 16 * a, 16 * e), ind(Xw, v("E", a, e)))
+            (cp if q == "V" else act)(xx(16 * a, 16 * e), ind(Xw, v("E", a, e)))
             a = e
         bcast(1)
         ts(v("lO"), ce, 256.0, ALU.is_ge, -256.0, ALU.mult)
 
-        dx(0, 0)
-        dx(0, 1)
-        SG = OPT["sg"]
-
-        def sg(h):
-            for m in SG:
-                bank = OPT["sgb"][h]
-                for kk in range(4):
-                    mm(v(bank, kk, 256, 4), I, ends(h, 1), kk == 0)
-                mm(v(bank, 0, 256), nI, v("xx", 1024 * h + m, 1024 * h + 1024, 4), False, True)
-                act(v("bb", 512 * m + 256 * h, 512 * m + 256 * h + 256), v(bank, 0, 256), AF.Sign, bias=0.5)
-
-        for m in range(4):
-            cmp(0, m, 0)
-            if m not in SG:
-                cmp(0, m, 1)
-        dx(1, 0)
-        dx(1, 1)
-        absd(0, 0)
-        absd(0, 1)
-        sg(0)
-        act(v("zw", S, S + 128), z, scale=0.5)
-        act(v("zw", 2 * S, 2 * S + 128), z, scale=-1.0)
-        mm(v("pA", 0, 128), I, v("half"), True)
-        todo = [(m, j) for m in range(4) for j in range(2) if not (j and m in SG)]
-        absd(1, 1)
-        sg(1)
-        absd(1, 0)
-        for i, (m, j) in enumerate(todo):
-            fin = i == len(todo) - 1
-            if not fin:
-                cmp(1, m, j)
-            if i == OPT["sgat"]:
-                for m2 in SG:
-                    for kk in range(4):
-                        sum_c(m2, 1, kk)
-            for kk in range(4):
-                if fin:
-                    cmp(1, m, j, kk, 4)
-                sum_c(m, j, kk, fin and kk == 3)
-            if i == 2:
-                sum_d(1)
-            if i == 4:
-                sum_d(0)
-        mm(v("pD0", 0, 128), I, cq, True)
-        mm(v("pD1", 0, 128), I, v("cf"), True)
-        mm(v("pD1", 0, 128), I, f)
+        for h, m in OPT["abs"]:
+            absd(h, m)
+        seen_m = set()
+        for i, (h, m) in enumerate(OPT["cmp"]):
+            for j in range(2):
+                fin = OPT["fin"] if i == 7 and j == 1 else 1
+                for k0 in range(fin):
+                    cmp(h, m, j, k0, fin)
+                    if m in seen_m:
+                        for kk in range(k0, 4, fin):
+                            sum_c(m, j, kk, i == 7 and j == 1 and kk == 3)
+            seen_m.add(m)
+            for k in range(2):
+                if OPT["sd"][k] == i:
+                    sum_d(OPT["abs"][2 + k][1], False)
+        mms(v("pD1", 0, 128), ((I, v("cf")), (v("J"), f)), True, False)
         mm(v("pD2", 0, 16), mask, C("bP", 16), True)
-        tt(v("u1"), v("ub"), Qo, ALU.mult)
+        mm(v("pD3", 0, 8), mask, C("bX"), True)
         ts(v("u2"), v("u1"), col(2), ALU.add)
-        ts(Wm, v("u2"), 5, ALU.arith_shift_right, 2047, ALU.bitwise_and)
-        tt(v("dEP"), ind(Dw, ce), Po, ALU.subtract)
+        ts(v("u1"), v("u2"), 5, ALU.arith_shift_right, 2047, ALU.bitwise_and)
+        gcopy(Wm, v("u1"))
+        if OPT["pe"] == "pA":
+            cp(v("E16"), v("E"))
+            mms(pe, ((v("I16"), v("E16")), (v("nI16"), v("P16"))))
 
-        act(v("okT"), pl, AF.Sign, bias=0.25)
+        act(v("okT"), pl, AF.Sign, bias=0.5, scale=-1.0)
         mm(pk, v("nBI"), v("okT"), False, True)
-        mm(v("pA", 0, 128), v("okT"), hI, False, True)
         scan(v("ns"), v("rmax", 0, 128), v("okT"), ALU.mult, ALU.add)
-        mm(v("pL", 128, 136), mask, C("a16"), True)
-        mm(pz, I, cq, True)
-        act(v("okN"), v("pA", 0, 128))
-        mm(v("pD0", 0, 128), v("Bk"), v("okN"))
-        mm(v("pD0", 0, 128), I, M1, False, True)
-        mm(v("pD1", 0, 128), v("Bf"), v("okN"))
-        mm(v("pD1", 0, 128), I, M1, False, True)
-        ph = v("pB", 0, 64)
-        mm(ph, I, v("r16", 0, 64), True)
-        mm(ph, I, v("nm", 0, 64))
-        if OPT["one"]:
-            mm(pv, I, v("nm", 64, 128))
         scan(v("mi"), v("rmin", 0, 128), pk, ALU.max, ALU.min)
+        mm(v("pD0", 0, 128), v("okT"), I, True, True)
+        act(v("okN"), v("pD0", 0, 128), scale=0.5, bias=0.5)
+        mms(ph, ((I, v("r16", 0, 64)), (I, v("nm", 0, 64))), True, False)
         tt(v("lk"), ind(v("ns"), v("b15")), mask, ALU.mult)
-        for i, (l, r) in enumerate(((v("lk"), C("kP", 16)), (I, C("kM", 16)), (nI, C("kM", 16)), (mask, C("aP", 16)))):
-            mm(v("pD2", 0, 16), l, r, False, i == 3)
-        tt(v("pA", 0, 128), v("pA", 0, 128), v("dEP"), ALU.mult)
         ts(v("wj"), v("mi", 15, 128, 16), 15, ALU.bitwise_and)
-        act(v("kN"), v("pD0", 0, 128), bias=-MAGIC)
-        cp(v("of"), v("pD2", 0, 16))
+        mms(v("pD2", 0, 16), ((v("lk"), C("kP", 16)), (I, C("kM", 16)), (nI, C("kM", 16)), (mask, C("aP", 16))), False)
+        mms(v("pD3", 0, 8), ((v("lk"), C("kX")), (I, C("xM")), (nI, C("xM")), (mask, C("a16"))), False, False)
         tt(v("lb"), ind(v("wj"), bo), mask, ALU.mult)
-        mm(v("pL", 128, 136), v("lb"), Dq, False, True)
-        tt(P1, v("pA", 0, 128), Po, ALU.add)
-        act(v("zt"), ind(v("zw"), v("of", 4, 12)))
-        cp(v("ob"), v("pL", 128, 136))
+        mm(v("pD3", 0, 8), v("lb"), Dq, False, True)
+        tt(pe, pe, v("okN"), ALU.mult)
+        cp(v("of"), v("pD2", 0, 16))
+        tt(P1, pe, v("P16"), ALU.add)
+        act(v("zt"), ind(v("zw"), v("of", 8, 16)), bias=ZO - 0.5)
+        cp(v("ob"), v("pD3", 0, 8))
         if not last:
-            cp(v("o1", b, b + 256), ind(v("W"), v("of")))
-            send(1, s, b, b + 256, 128)
-        act(fn, v("pD1", 0, 128), bias=-MAGIC)
+            cp(v("o1", c, c + 128), ind(v("W"), v("of", 8, 16)))
+            send(1, s, c, c + 128, 64)
+        mms(v("pD1", 0, 128), ((v("Bf"), v("okN")), (I, M1)), False)
+        act(fn, v("pD1", 0, 128), AF.Abs, bias=-MAGIC)
         po = v("pK", 384, 400)
-        for i, (l, r) in enumerate(((mask, C("sc", 16)), (v("lk"), C("sw", 16)), (I, C("sM", 16)), (nI, C("sM", 16)))):
-            mm(po, l, r, i == 0)
+        mms(po, ((mask, C("sc", 16)), (v("lk"), C("sw", 16)), (I, C("sM", 16)), (nI, C("sM", 16))), True, False)
         mm(v("pK", 384, 392), I, v("lO"))
         mm(v("pK", 392, 400), I, v("lO"))
         mm(v("pK", 392, 400), mask, C("a2"), False, True)
         act(v("sO"), po, AF.Abs)
-        if not OPT["one"]:
-            mm(pv, I, v("nm", 64, 128), True)
+        mm(pv, I, v("nm", 64, 128), True)
 
-        mm(pz, I, v("zt"))
-        tt(v("tb"), ind(v("xx"), v("ob")), v("kN"), ALU.mult)
-        mm(pz, hI, v("tb"))
-        mm(pz, I, M1, False, True)
-        act(zn, pz, AF.Abs, bias=-MAGIC)
+        tt(v("z2"), ind(v("xw"), v("ob")), v("zt"), ALU.add)
+        weights(ph, True, False)
+        mms(ph, ((I, v("M16", 0, 64)), (nI, v("M16", 0, 64))), False, False)
+        weights(ph, False, True)
+        mm(v("pD0", 0, 128), v("I16"), v("z2"), True, True)
+        act(v("zt"), v("pD0", 0, 128), scale=0.5, bias=0.5 * ZO - 0.5)
+        act(zn, v("pD0", 0, 128), scale=0.5, bias=-0.5 * ZO)
         if last:
-            cp(v("pq"), ind(v("W"), v("of")))
-            dma("S", T.yp[:, 0:64], v("pq", 0, 64))
-            dma("S", T.yq[:], v("pq", 64, 192))
-            dma("S", T.yp[:, 64:128], v("pq", 192, 256))
+            act(v("pq"), ind(v("W"), v("of")))
+            dma("S", T.yp[:], v("pq", 0, 128))
+            dma("S", T.yq[:], v("pq", 128, 256))
             dma("S", T.yz[:], zn)
             E8 = slice(0, 8)
             ps = v("pA", 128, 256, p=E8)
-            for i, (l, r) in enumerate(((v("nI", 0, 8), cq), (C("s1"), fn), (v("I", 0, 8), M1), (v("nI", 0, 8), M1), (C("s2"), fn))):
-                mm(ps, l, r, i == 0, i == 4)
-            act(v("sS", p=E8), ps, scale=2.0)
+            mm(ps, C("s2"), fn, True, True)
+            act(v("sS", p=E8), ps)
             dma("S", T.ys[:], v("sS", p=E8))
         else:
             send(2, s, b, b + 256, 128)
 
-        zz = [v("zl", e, 128, 2) if last else v("o2", b + 2 * e, b + 256, 4) for e in range(2)]
-        for e in range(2):
-            mm(ph, v("We", 128 * e, 128 * e + 128), zz[e])
-        mm(ph, I, v("M16", 0, 64))
-        mm(ph, nI, v("M16", 0, 64))
-        for e in range(2):
-            mm(ph, v("We", 256 + 128 * e, 384 + 128 * e), zz[e], False, e == 1 and not OPT["one"])
-        number(zz)
-        if OPT["one"]:
-            scan(v("oS"), v("r8"), v("pB", 0, 128), ALU.mult, ALU.max)
-        else:
-            scan(v("oS", o1_, o1_ + 64), v("r8", 0, 64), ph, ALU.mult, ALU.max)
-            scan(v("oS", o2_, o2_ + 64), v("r8", 0, 64), pv, ALU.mult, ALU.max)
-        cp(v("oo"), v("oS", o1_ + 7, o1_ + 64, 8))
-        tt(v("t1"), ind(Xw, v("oo")), zn, ALU.add)
-        ts(v("xn"), v("t1"), 0.5, ALU.mult, -0.25, ALU.add)
+        weights(pv, False, True)
+        scan(v("oS", 0, 64), v("r8", 0, 64), ph, ALU.mult, ALU.max)
+        scan(v("oS", 64, 128), v("r8", 0, 64), pv, ALU.mult, ALU.max)
+        cp(v("oo"), v("oS", 7, 64, 8))
+        tt(v("x2"), ind(Xw, v("oo")), v("zt"), ALU.add)
+        ts(v("xn"), v("x2"), 0.5, ALU.mult, -0.5 * ZO, ALU.add)
         cp(ind(Xw, v("oo")), v("xn"))
         if not last:
             columns(v("o3", 16 * s, 16 * s + 16), 16)
             send(3, s, 16 * s, 8 * s + 8, 4)
+            act(v("o4", c, c + 128), ind(v("W"), v("of", 0, 8)))
+            send(4, s, c, c + 128, 64)
         else:
             columns(v("o3", 16 * s + 8, 16 * s + 16), -8)
             dma("A", T.yx[:], Xw)

from concourse.bass import DstId, RemoteDMATransfer
from concourse.mybir import AluOpType as ALU, AxisListType as AX, ActivationFunctionType as AF

WT = [37, 101, 59, 203, 83, 149, 11, 173, 67, 229, 127, 43, 191, 23, 251, 109]
STEPS = 4
OPT = {"vy": 20, "cuts": [64, 96], "xs": [(16, "V"), (64, "A"), (128, "A")], "rounds": 2, "vy0": 16,
       "cmp": [(0, 0), (0, 1), (0, 2), (0, 3), (1, 0), (1, 1), (1, 2), (1, 3)], "abs": [(0, 0), (0, 1), (1, 1), (1, 0)],
       "sd": [5, 6], "fin": 4, "pe": "pA",
       "cost": {"cyc": 0.9, "fix": 25, "least": 55, "pe": 0.72, "gather": 1.3, "scatter": 2.5, "dma": 900, "byte": 0.43,
                "issue": 350, "first": 1500, "fly": [1500, 1700, 1500, 2000], "hop": 150}}
COST = OPT["cost"]
RW = 16 * max(b - a for a, b in zip([0, min(OPT["vy"], OPT["vy0"])] + OPT["cuts"], [OPT["vy"]] + OPT["cuts"] + [128]))
S = 256
MAGIC = 12582912.0
XO, AO = 16, 2064
ZO = 3072.0
KF = 131072.0


def _sb(cols, dt):
    return ("sbuf", [128, cols], {"b": "bfloat16", "f": "float32", "i": "int32", "u": "uint16", "h": "float16"}[dt])


SCRATCH = {
    "X": _sb(2048, "b"), "Di": _sb(512, "i"), "D": _sb(1536, "f"),
    "yy": _sb(2048, "b"), "xw": _sb(AO + 2048, "b"), "hs": _sb(2048, "b"), "ls": _sb(2048, "b"),
    "aa": _sb(2048, "b"), "bb": _sb(2048, "b"), "z2": _sb(128, "h"), "zt": _sb(128, "f"), "x2": _sb(128, "h"),
    "E16": _sb(128, "h"), "P16": _sb(128, "h"), "I16": _sb(128, "h"), "nI16": _sb(128, "h"), "W": _sb(2 * S + 128, "f"), "Fi": _sb(128, "i"), "zl": _sb(128, "b"),
    "m4": _sb(128 * STEPS, "f"), "o4": _sb(128 * STEPS, "f"),
    "m1": _sb(128 * STEPS, "u"), "o1": _sb(128 * STEPS, "u"), "m2": _sb(256 * STEPS, "b"), "o2": _sb(256 * STEPS, "b"),
    "m3": _sb(8 * STEPS, "u"), "o3": _sb(16 * STEPS, "u"), "pq": _sb(256, "f"),
    "A1": _sb(32, "i"), "A2": _sb(8, "i"), "A3": _sb(16, "i"), "m16": _sb(16, "b"),
    "bo": _sb(8, "u"), "bx": _sb(8, "u"), "b15": _sb(8, "u"), "col": _sb(16, "f"), "wrow": _sb(16, "f"),
    "rmax": _sb(RW, "b"), "rmin": _sb(RW, "b"), "r8": _sb(128, "b"), "We": _sb(512, "h"),
    "Dq": _sb(8, "b"), "C": _sb(192, "b"),
    "E": _sb(128, "u"), "dEP": _sb(128, "f"), "u1": _sb(128, "i"), "u2": _sb(128, "i"),
    "mi": _sb(128, "i"), "wj": _sb(8, "i"), "of": _sb(16, "u"), "ob": _sb(8, "u"), "zw": _sb(2 * S + 128, "b"),
    "oS": _sb(128, "i"), "oo": _sb(8, "u"), "vi": _sb(16, "i"), "vj": _sb(16, "i"),
    "lO": _sb(8, "b"), "sO": _sb(16, "f"), "t1": _sb(128, "f"), "xn": _sb(128, "b"), "sS": _sb(128, "f"),
}
for _n in ("one", "nBI", "c32k", "I", "nI", "J", "B", "mask", "Wp", "Wn", "RLp", "Bf", "cf", "krow", "c15",
           "M1", "M16", "M4k", "c2k", "c32", "r16", "nm", "nm2", "okT", "okN", "ns", "lb", "lk", "tb"):
    SCRATCH[_n] = _sb(128, "b")
for _n in ("pA", "pB", "pD0", "pD1", "pD2", "pD3", "pL", "pK"):
    SCRATCH[_n] = ("psum", [128, 512], "float32")
NDMA = 12
SEMAPHORES = (["eV", "eA", "eP", "eG", "sent"] + ["d%d" % i for i in range(NDMA)]
              + ["r%d_%d" % (m, s) for m in (1, 2, 3, 4) for s in range(1, STEPS)])


def rank_program(g, core, T, topo):
    rank = T.rank_of(core)
    if rank is None:
        return
    n = len(T.cores)
    Q = {"V": g.vector, "A": g.scalar, "P": g.tensor, "G": g, "S": g.sync}
    ops = []

    def v(name, a=None, b=None, st=1, p=None):
        t = T[name]
        a = 0 if a is None else a
        b = t.shape[1] if b is None else b
        cs = slice(a, b, st) if st != 1 else slice(a, b)
        ap = t[:, cs] if p is None else t[p, cs]
        bits = ((1 << b) - (1 << a)) if st == 1 else sum(1 << c for c in range(a, b, st))
        return {"ap": ap, "r": [(name, bits)], "n": len(range(a, b, st)),
                "t": SCRATCH[name][0][0] + ("b" if SCRATCH[name][2][-2:] == "16" else "f")}

    def ind(win, off):
        return {"ap": win["ap"].indirect(off["ap"]), "r": win["r"], "x": off["r"], "n": 16 * off["n"], "t": win["t"]}

    def regs(xs):
        out = []
        for x in xs:
            if isinstance(x, dict):
                out += x["r"] + x.get("x", [])
        return out

    def a_(x):
        return x["ap"] if isinstance(x, dict) else x

    def add(q, call, out, ins, token=None, both=False):
        xs = [x for x in [out] + ins if isinstance(x, dict) and "n" in x]
        w = max([x["n"] for x in xs] + [1])
        if token is not None:
            if token[2] == "dma":
                hold = COST["byte"] * w * (2 if xs[0]["t"][1] == "b" else 4) + 80
                t = COST["dma"] + hold
            else:
                hold = t = COST["issue"] if q == "G" else 0
        else:
            if q == "P":
                t = COST["pe"] * max(64, out["n"])
            elif q == "G":
                t = 170 + 2 * COST["cyc"] * w
            elif "x" in out:
                t = 50 + COST["scatter"] * w
            elif any("x" in x for x in xs):
                t = 60 + COST["gather"] * w
            else:
                r = 1.0
                if both and all(x["t"][0] == "s" for x in xs[1:]):
                    r = 2.0
                elif q == "V" and not both and all(x["t"][1] == "b" for x in xs if x["n"] > 1):
                    r = 0.5
                t = max(COST["least"], COST["fix"] + COST["cyc"] * r * w)
            hold = t
        ops.append([q, call, regs(ins) + out.get("x", []), out["r"], token, hold, t])

    def cp(out, x):
        add("V", lambda e: e.tensor_copy(a_(out), a_(x)), out, [x])

    def tt(out, x, y, op):
        add("V", lambda e: e.tensor_tensor(a_(out), a_(x), a_(y), op), out, [x, y], None, True)

    def ts(out, x, s1, op0, s2=None, op1=None):
        if op1 is None:
            add("V", lambda e: e.tensor_scalar(a_(out), a_(x), a_(s1), None, op0), out, [x, s1])
        else:
            add("V", lambda e: e.tensor_scalar(a_(out), a_(x), a_(s1), a_(s2), op0, op1), out, [x, s1, s2])

    def scan(out, d0, d1, op0, op1):
        add("V", lambda e: e.tensor_tensor_scan(a_(out), a_(d0), a_(d1), 0.0, op0, op1), out, [d0, d1])

    def red(out, x):
        add("V", lambda e: e.tensor_reduce(a_(out), a_(x), AX.X, ALU.add), out, [x])

    def fill(out, c):
        add("V", lambda e: e.memset(a_(out), c), out, [])

    def act(out, x, f=None, bias=0.0, scale=1.0):
        f = AF.Identity if f is None else f
        add("A", lambda e: e.activation(a_(out), a_(x), f, bias=a_(bias), scale=a_(scale)), out, [x, bias, scale])

    def mm(out, l, r, start=False, stop=False):
        add("P", lambda e: e.matmul(a_(out), a_(l), a_(r), start, stop), out, [l, r])

    def mms(out, pairs, start=True, stop=True):
        for i, (l, r) in enumerate(pairs):
            mm(out, l, r, start and i == 0, stop and i == len(pairs) - 1)

    def iota(out, pat, base, cm, small=False):
        if small:
            add("G", lambda e: e.iota(a_(out), pat, base, cm, allow_small_or_imprecise_dtypes=True), out, [])
        else:
            add("G", lambda e: e.iota(a_(out), pat, base, cm), out, [])

    def gsel(out, x, pat, op, c, base, cm):
        add("G", lambda e: e.affine_select(a_(out), a_(x), pat, op, c, base, cm), out, [x])

    def gcopy(out, x):
        gsel(out, x, [[0, out["n"]]], ALU.is_ge, 0.0, 0, 0)

    def gfill(out, c):
        gsel(out, v("one", 0, out["n"]), [[0, out["n"]]], ALU.is_gt, c, 0, 0)

    nd = [0]

    def dma(q, out, x):
        sem = "d%d" % nd[0]
        nd[0] += 1
        add(q, lambda e: e.dma_start(a_(out), a_(x)), out if isinstance(out, dict) else {"r": []}, [x], (sem, 16, "dma"))

    to = [T.cores[(rank + 1) % n], T.cores[(rank + 2) % n]]
    eng = [e for e in topo.engines(core, to[0]) if e in topo.engines(core, to[1])]
    per = len(eng) // 2

    def send(m, s, so, do, w):
        sem, src, dst = "r%d_%d" % (m, s + 1), "o%d" % m, "m%d" % m

        def call(e):
            trs = []
            for h in range(2):
                rid, pid = topo.addr(to[h], core)
                trs.append(RemoteDMATransfer(
                    dst_ids=[DstId(rid=rid, pnc=pid)], dma_engine_mask=sum(1 << x for x in eng[per * h:per * h + per]),
                    remote_sem=T.sem[sem],
                    src=T[src][:, so + w * h:so + w * h + w], dst=T[dst][:, do + w * h:do + w * h + w]))
            return e.remote_dma_fused(trs, local_sem=T.sem.sent)
        add("G", call, {"r": []}, [v(src, so, so + 2 * w)], ("sent", 2 * per, "remote"))
        add("X", None, v(dst, do, do + 2 * w), [], (sem, 2 * per, "arrive"))
        ops[-1][6] = COST["fly"][m - 1] + (COST["first"] if s == 0 and m < 3 else 0)

    Wm, P1, Po, Qo = v("W", 0, 128), v("W", S, S + 128), v("u2"), v("W", 2 * S, 2 * S + 128)
    fill(v("Fi"), 0)
    dma("A", v("u1"), T.ql[:])
    dma("S", v("zl"), T.zq[:])
    dma("S", v("Fi", p=slice(0, 128, 16)), T.sd[:])
    dma("S", v("X"), T.xr[:])
    dma("S", v("Di"), T.dr[:])
    dma("S", Po, T.pl[:])

    def mk(j):
        return v("m16", j, j + 1)

    def col(j):
        return v("col", j, j + 1)

    Dq, I, nI, B, mask, M1, bo = [v(k) for k in ("Dq", "I", "nI", "B", "mask", "M1", "bo")]
    CN = ["kP", "kQ", "kM", "kMb", "aP", "aQ", "bP", "bQ", "sc", "scb", "sw", "swb", "sM", "sMb", "a2", "a16", "h", "g8",
          "s2", "kX", "bX", "xM"]

    def C(k, w=8):
        a = 8 * CN.index(k)
        return v("C", a, a + w)

    iota(v("A2"), [[-16, 8]], 0, 1)
    iota(v("A1", 0, 16), [[-1, 16]], 128, 1)
    iota(v("A1", 16, 24), [[0, 8]], 0, 1)
    iota(v("A3", 0, 8), [[1, 8]], 0, 0)
    iota(col(0), [[0, 1]], 0, 1, True)
    ts(v("A2"), v("A2"), 4, ALU.arith_shift_right)
    fill(v("one"), 1.0)
    ts(Dq, v("A2"), 0.0, ALU.is_equal)
    ts(v("A1", 0, 24), v("A1", 0, 24), 15, ALU.bitwise_and)
    gsel(I, v("one"), [[-1, 128]], ALU.is_equal, 0.0, 0, 1)
    for r in range(0, 16, 2):
        iota(v("wrow", r, r + 2), [[WT[r + 1] - WT[r], 2]], WT[r], 0, True)
    cp(bo, v("A3", 0, 8))
    ts(v("b15"), v("A3", 0, 8), 16.0, ALU.mult, 15.0, ALU.add)
    ts(v("m16"), v("A1", 0, 16), 0.0, ALU.is_equal)
    cp(v("bx"), v("A1", 16, 24))
    act(mask, ind(v("m16"), v("bx")))
    act(B, ind(Dq, bo))
    act(col(4), col(0), scale=16.0, bias=float(XO))
    act(col(3), col(0), scale=2.0, bias=256.0)
    for k, c in (("h", -1.0), ("g8", 8.0), ("sc", 181.0), ("scb", 724.0), ("sw", -10.6875), ("swb", -42.75),
                 ("kX", 171.0), ("bX", 176.0), ("a2", col(3)), ("a16", col(4))):
        act(C(k), Dq, scale=c)
    for k, c in (("kM", S), ("kMb", S), ("sM", 256), ("sMb", 1024), ("xM", 2048)):
        fill(C(k), c * MAGIC)
    for k, c in (("kP", -10.6875), ("kQ", 21.375), ("aP", col(0)), ("aQ", col(0)), ("bP", 436.0), ("bQ", 276.0)):
        act(C(k), Dq, scale=c)
    act(nI, I, scale=-1.0)
    cp(v("m1", 0, 128), v("u1"))
    gcopy(Qo, v("u1"))
    fill(v("rmax"), 1.0)
    fill(v("rmin"), 0.0)
    fill(v("rmax", 0, RW, 16), 0.0)
    fill(v("rmin", 0, RW, 16), 4194304.0)
    fill(v("r8"), 1.0)
    fill(v("r8", 0, 128, 8), 0.0)
    fill(v("xw", 0, XO), 0.0)
    cp(v("m2", 0, 256, 2), v("zl"))
    ts(v("z2"), v("zl"), 2.0, ALU.mult, ZO, ALU.add)
    cp(v("m2", 1, 256, 2), v("Fi"))
    tt(v("wrow"), v("wrow"), v("m16"), ALU.mult)
    ts(col(2), v("A1", 16, 17), 1184.0, ALU.mult)
    red(col(1), v("wrow"))
    fill(M1, MAGIC)
    ts(v("Wp"), B, col(1), ALU.mult)
    act(v("Wn"), v("Wp"), scale=-1.0)
    fill(v("We"), 0.0)
    for e in (2, 3, 0, 1):
        ts(v("We", 128 * e + e % 2, 128 * e + 128, 2), v("Wp", e % 2, 128, 2), 0.5 if e > 1 else -0.5, ALU.mult)
    act(v("nm2"), mask, scale=1048576.0, bias=-1048576.0)
    ts(v("lb"), B, mk(0), ALU.mult, 256.0, ALU.mult)
    tt(v("nm", 64, 128), v("nm2", 0, 128, 2), v("nm2", 1, 128, 2), ALU.max)
    act(v("tb", 0, 64), v("mask", 1, 128, 2), scale=4119.5, bias=-4096.0)
    act(v("dEP", 0, 64), v("mask", 0, 128, 2), scale=4103.5)
    tt(v("nm", 0, 64), v("dEP", 0, 64), v("tb", 0, 64), ALU.add)
    act(col(8), mk(2))
    act(v("RLp"), B, scale=col(8))
    act(col(5), mk(1), bias=mk(2))
    act(col(9), mk(0), scale=1.15625)
    act(col(6), col(5), scale=0.640625, bias=col(9))
    act(v("cf"), v("one"), scale=col(6))
    act(col(7), mk(1), scale=2.0, bias=mk(0))
    act(C("s2"), Dq, scale=col(7))
    act(col(10), mk(1), scale=2.0, bias=-1.0)
    act(v("J"), I, scale=col(10))
    act(col(11), mk(1), scale=-0.5)
    act(col(12), mk(0), scale=2048.0, bias=col(11))
    act(v("c2k"), v("one"), scale=col(12))
    gfill(v("M4k"), 4096 * MAGIC)
    gfill(v("c32"), 32.0)
    gfill(v("c15"), 30.0)
    gfill(v("c32k"), 32768.0)
    gcopy(v("P16"), Po)
    act(v("nBI"), I, scale=-32768.0)
    cp(v("I16"), I)
    cp(v("nI16"), nI)
    iota(v("krow"), [[0, 8], [1, 16]], 0, 0, True)
    gfill(v("Bf"), 0.0)
    gfill(v("zw", 2 * S, 2 * S + 128), 0.0)
    gfill(v("M16", 0, 64), 16 * MAGIC)
    iota(v("r16", 0, 64), [[32, 64]], 0, 0, True)
    gcopy(v("D", 0, 512), v("Di"))
    for r, c in enumerate((16, 32, 32)):
        act(v("Bf", r, 128, 16), Dq, scale=-1.0 / c)

    Xw = v("X")
    DB = (("pD0", "pD1"), ("pD2", "pD3"))
    pv, ph = v("pD1", 0, 64), v("pB", 0, 64)
    zz = [v("z2", e, 128, 2) for e in range(2)]

    def weights(out, neg, stop):
        for e in range(2):
            a = 128 * e + (0 if neg else 256)
            mm(out, v("We", a, a + 128), zz[e], False, stop and e == 1)

    def columns(out, w):
        u = v("oS", 64 + 7, 128, 8)
        if w != -8:
            ts(v("vi", 0, 8), u, 4095, ALU.bitwise_and)
        if w != 8:
            ts(v("vj", 8, 16), u, 1, ALU.bitwise_and)
        if w != -8:
            ts(v("vi", 8, 16), v("vi", 0, 8), 2741.0, ALU.mult)
            ts(v("vj", 0, 8), v("vi", 8, 16), 5, ALU.arith_shift_right, 255, ALU.bitwise_and)
        a, b = (8, 16) if w < 0 else (0, w)
        tt(out, v("vj", a, b), v("sO", a, b), ALU.add)

    mms(v("pA", 0, 128), ((I, v("nm2")), (v("lb"), v("m2", 1, 256, 2))))
    scan(v("t1"), v("rmax", 0, 128), v("pA", 0, 128), ALU.mult, ALU.max)
    cp(v("sO", 0, 8), v("t1", 15, 128, 16))
    mm(pv, I, v("nm", 64, 128), True)
    weights(pv, False, True)
    scan(v("oS", 64, 128), v("r8", 0, 64), pv, ALU.mult, ALU.max)
    columns(v("m3", 0, 8), 8)

    for s in range(STEPS):
        last = s == STEPS - 1
        b, c = 256 * s, 128 * s
        z, f = v("m2", b, b + 256, 2), v("m2", b + 1, b + 256, 2)
        ce = v("m3", 8 * s, 8 * s + 8)
        zn, fn = v("zl") if last else v("o2", b, b + 256, 2), v("o2", b + 1, b + 256, 2)
        pu, pl, pk, pe = v("pL", 256, 384), v("pL", 0, 128), v("pK", 0, 128), v(OPT["pe"], 256, 384)

        def xx(a, e, st=1):
            return v("xw", XO + a, XO + e, st)

        def ad(a, e, st=1):
            return v("xw", AO + a, AO + e, st)

        def ends(h, j):
            return v(("ls", "hs")[j], 1024 * h + 15, 1024 * h + 1024, 16)

        def bcast(h):
            for j in range(2):
                for kk in range(4):
                    mm(v(("pA", "pB")[h], 256 * j + kk, 256 * j + 256, 4), I, ends(h, j), True, True)

        def absd(h, m):
            mm(v(DB[h][m]), I, xx(1024 * h + m, 1024 * h + 1024, 2), False, True)
            act(ad(1024 * h + m, 1024 * h + 1024, 2), v(DB[h][m]), AF.Abs, scale=2.0)

        def sum_d(m, stop):
            for kk in range(8):
                mm(v("pK", m + 2 * kk, 128, 16), ad(m + 2 * kk, 2048, 16), C("g8"), False, stop and kk == 7)

        def cmp(h, m, j, k0=0, st=1):
            o = 512 * m + 256 * h
            tt(v(("aa", "bb")[j], o + k0, o + 256, st), xx(1024 * h + m + 4 * k0, 1024 * h + 1024, 4 * st),
               v(("pA", "pB")[h], 256 * j + k0, 256 * j + 256, st), (ALU.is_ge, ALU.is_le)[j])

        def sum_c(m, j, kk, stop=False):
            mm(v("pL", m + 4 * kk, 128, 16), v(("aa", "bb")[j], 512 * m + kk, 512 * m + 512, 4), C("h"), False, stop)

        vy = OPT["vy"] if s else OPT["vy0"]
        cuts = [0, vy] + OPT["cuts"] + [128]
        for a, e in zip(cuts, cuts[1:]):
            (cp if a == 0 else act)(v("yy", 16 * a, 16 * e), ind(Xw, v("m1", c + a, c + e)))
        if s > 0:
            cp(ind(v("D"), v("o3", 16 * s - 8, 16 * s)), P1)
            gcopy(Qo, v("m1", c, c + 128))
        gcopy(v("zw", S, S + 128), z)
        if s > 0:
            gcopy(v("P16"), v("m4", c, c + 128))
        mms(pu, ((B, v("c2k")), (v("Wn"), z), (I, v("M4k")), (nI, v("M4k")), (v("Wp"), z), (I, v("c32"))))
        tt(v("u1"), pu, Qo, ALU.mult)
        for h in range(2):
            for m in range(2):
                for kk in range(8):
                    mm(v(DB[h][m], kk, 512, 8), nI, v("m2", b + 128 * h, b + 128 * h + 128, 2), kk == 0)
        Dw = v("D", 0, 512) if s else v("Di")
        cp(v("E"), ind(Dw, ce))
        for a, e in zip(cuts, cuts[1:]):
            scan(v("hs", 16 * a, 16 * e), v("rmax", 0, 16 * (e - a)), v("yy", 16 * a, 16 * e), ALU.mult, ALU.max)
            scan(v("ls", 16 * a, 16 * e), v("rmin", 0, 16 * (e - a)), v("yy", 16 * a, 16 * e), ALU.max, ALU.min)
            if a < 64 <= e:
                bcast(0)
        mms(v("pK", 128, 256), ((I, v("hs", 15, 2048, 16)), (nI, z)))
        act(v("zw", 0, 128), v("pK", 128, 256), AF.Abs, scale=2.0)
        if OPT["pe"] != "pA":
            cp(v("E16"), v("E"))
            mms(pe, ((v("I16"), v("E16")), (v("nI16"), v("P16"))))
        mms(pk, ((I, v("krow")), (I, v("c32k"))), True, False)
        mms(pl, ((I, v("c15")), (f, v("RLp"))), True, False)
        a = 0
        for e, q in OPT["xs"]:
            (cp if q == "V" else act)(xx(16 * a, 16 * e), ind(Xw, v("E", a, e)))
            a = e
        bcast(1)
        ts(v("lO"), ce, 256.0, ALU.is_ge, -256.0, ALU.mult)

        for h, m in OPT["abs"]:
            absd(h, m)
        seen_m = set()
        for i, (h, m) in enumerate(OPT["cmp"]):
            for j in range(2):
                fin = OPT["fin"] if i == 7 and j == 1 else 1
                for k0 in range(fin):
                    cmp(h, m, j, k0, fin)
                    if m in seen_m:
                        for kk in range(k0, 4, fin):
                            sum_c(m, j, kk, i == 7 and j == 1 and kk == 3)
            seen_m.add(m)
            for k in range(2):
                if OPT["sd"][k] == i:
                    sum_d(OPT["abs"][2 + k][1], False)
        mms(v("pD1", 0, 128), ((I, v("cf")), (v("J"), f)), True, False)
        mm(v("pD2", 0, 16), mask, C("bP", 16), True)
        mm(v("pD3", 0, 8), mask, C("bX"), True)
        ts(v("u2"), v("u1"), col(2), ALU.add)
        ts(v("u1"), v("u2"), 5, ALU.arith_shift_right, 2047, ALU.bitwise_and)
        gcopy(Wm, v("u1"))
        if OPT["pe"] == "pA":
            cp(v("E16"), v("E"))
            mms(pe, ((v("I16"), v("E16")), (v("nI16"), v("P16"))))

        act(v("okT"), pl, AF.Sign, bias=0.5, scale=-1.0)
        mm(pk, v("nBI"), v("okT"), False, True)
        scan(v("ns"), v("rmax", 0, 128), v("okT"), ALU.mult, ALU.add)
        scan(v("mi"), v("rmin", 0, 128), pk, ALU.max, ALU.min)
        mm(v("pD0", 0, 128), v("okT"), I, True, True)
        act(v("okN"), v("pD0", 0, 128), scale=0.5, bias=0.5)
        mms(ph, ((I, v("r16", 0, 64)), (I, v("nm", 0, 64))), True, False)
        tt(v("lk"), ind(v("ns"), v("b15")), mask, ALU.mult)
        ts(v("wj"), v("mi", 15, 128, 16), 15, ALU.bitwise_and)
        mms(v("pD2", 0, 16), ((v("lk"), C("kP", 16)), (I, C("kM", 16)), (nI, C("kM", 16)), (mask, C("aP", 16))), False)
        mms(v("pD3", 0, 8), ((v("lk"), C("kX")), (I, C("xM")), (nI, C("xM")), (mask, C("a16"))), False, False)
        tt(v("lb"), ind(v("wj"), bo), mask, ALU.mult)
        mm(v("pD3", 0, 8), v("lb"), Dq, False, True)
        tt(pe, pe, v("okN"), ALU.mult)
        cp(v("of"), v("pD2", 0, 16))
        tt(P1, pe, v("P16"), ALU.add)
        act(v("zt"), ind(v("zw"), v("of", 8, 16)), bias=ZO - 0.5)
        cp(v("ob"), v("pD3", 0, 8))
        if not last:
            cp(v("o1", c, c + 128), ind(v("W"), v("of", 8, 16)))
            send(1, s, c, c + 128, 64)
        mms(v("pD1", 0, 128), ((v("Bf"), v("okN")), (I, M1)), False)
        act(fn, v("pD1", 0, 128), AF.Abs, bias=-MAGIC)
        po = v("pK", 384, 400)
        mms(po, ((mask, C("sc", 16)), (v("lk"), C("sw", 16)), (I, C("sM", 16)), (nI, C("sM", 16))), True, False)
        mm(v("pK", 384, 392), I, v("lO"))
        mm(v("pK", 392, 400), I, v("lO"))
        mm(v("pK", 392, 400), mask, C("a2"), False, True)
        act(v("sO"), po, AF.Abs)
        mm(pv, I, v("nm", 64, 128), True)

        tt(v("z2"), ind(v("xw"), v("ob")), v("zt"), ALU.add)
        weights(ph, True, False)
        mms(ph, ((I, v("M16", 0, 64)), (nI, v("M16", 0, 64))), False, False)
        weights(ph, False, True)
        mm(v("pD0", 0, 128), v("I16"), v("z2"), True, True)
        act(v("zt"), v("pD0", 0, 128), scale=0.5, bias=0.5 * ZO - 0.5)
        act(zn, v("pD0", 0, 128), scale=0.5, bias=-0.5 * ZO)
        if last:
            act(v("pq"), ind(v("W"), v("of")))
            dma("S", T.yp[:], v("pq", 0, 128))
            dma("S", T.yq[:], v("pq", 128, 256))
            dma("S", T.yz[:], zn)
            E8 = slice(0, 8)
            ps = v("pA", 128, 256, p=E8)
            mm(ps, C("s2"), fn, True, True)
            act(v("sS", p=E8), ps)
            dma("S", T.ys[:], v("sS", p=E8))
        else:
            send(2, s, b, b + 256, 128)

        weights(pv, False, True)
        scan(v("oS", 0, 64), v("r8", 0, 64), ph, ALU.mult, ALU.max)
        scan(v("oS", 64, 128), v("r8", 0, 64), pv, ALU.mult, ALU.max)
        cp(v("oo"), v("oS", 7, 64, 8))
        tt(v("x2"), ind(Xw, v("oo")), v("zt"), ALU.add)
        ts(v("xn"), v("x2"), 0.5, ALU.mult, -0.5 * ZO, ALU.add)
        cp(ind(Xw, v("oo")), v("xn"))
        if not last:
            columns(v("o3", 16 * s, 16 * s + 16), 16)
            send(3, s, 16 * s, 8 * s + 8, 4)
            act(v("o4", c, c + 128), ind(v("W"), v("of", 0, 8)))
            send(4, s, c, c + 128, 64)
        else:
            columns(v("o3", 16 * s + 8, 16 * s + 16), -8)
            dma("A", T.yx[:], Xw)
            cp(ind(v("D"), v("o3", 16 * s + 8, 16 * s + 16)), P1)
            dma("S", T.yd[:], v("D", 0, 512))

    def meet(r1, r2):
        for x in r1:
            for y in r2:
                if x[0] == y[0] and x[1] & y[1]:
                    return True
        return False

    def clash(e, o):
        return meet(e[3], o[2]) or meet(e[3], o[3]) or meet(e[2], o[3])

    seen, pre, soft = {}, [], set()
    for j, o in enumerate(ops):
        p = set()
        for nm in set(x[0] for x in o[2] + o[3]):
            if SCRATCH[nm][0] == "psum":
                for i in reversed(seen.get(nm, [])):
                    if ops[i][0] != o[0] or o[0] == "P" or clash(ops[i], o):
                        p.add(i)
                    if ops[i][0] == "P":
                        break
            else:
                p.update(i for i in seen.get(nm, []) if clash(ops[i], o))
            seen.setdefault(nm, []).append(j)
        if o[0] == "X":
            p.add(j - 1)
        elif o[0] == "G" or o[4] is not None:
            k = "G" if o[0] == "G" else "dma"
            if k in seen and seen[k] not in p:
                p.add(seen[k])
                soft.add((seen[k], j))
            if o[4] is not None:
                seen[k] = j
        pre.append(p)
    post = [[] for _ in ops]
    for j, p in enumerate(pre):
        for i in p:
            post[i].append(j)

    def place(rank_of, before, flip):
        at, busy = {}, {}
        for j in sorted(range(len(ops)), key=rank_of):
            q, hold, t = ops[j][0], ops[j][5], ops[j][6]
            r = max([at[i] + (ops[i][5] if (min(i, j), max(i, j)) in soft else
                              ops[i][6] + (0 if ops[i][0] == q == "P" else COST["hop"])) for i in before[j]] + [0.0])
            lead = t - hold if flip else 0.0
            b = busy.setdefault("S" if ops[j][4] is not None and q == "A" else q, [])
            k = 0
            r += lead
            while k < len(b) and b[k][0] < r + hold:
                r = max(r, b[k][1])
                k += 1
            if hold:
                b.insert(k, (r, r + hold))
            at[j] = r - lead
        return at

    at = place(lambda j: j, pre, False)
    for _ in range(OPT["rounds"]):
        end = []
        for j in range(len(ops)):
            end.append(max([at[j] + ops[j][6]] + [end[i] for i in pre[j]]))
        back = place(lambda j: (-end[j], -j), post, True)
        for j in range(len(ops) - 1, -1, -1):
            end[j] = max([back[j] + ops[j][6]] + [end[k] for k in post[j]])
        at = place(lambda j: (-end[j], j), pre, False)
    ops = [ops[j] for j in sorted(range(len(ops)), key=lambda j: (at[j], j))]
    total = 0
    for o in ops:
        if o[4] is not None and o[4][2] == "remote":
            total += o[4][1]
            o[4] = ("sent", total, "remote")

    def lane(o):
        return o[0] if o[4] is None else o[4][0]

    bk = [set(x[0] for x in o[2] + o[3] if SCRATCH[x[0]][0] == "psum") for o in ops]
    touched = {}
    known = {q: {} for q in Q}
    clock, waits = [], []
    for j, o in enumerate(ops):
        best = {}
        names = set(x[0] for x in o[2] + o[3])
        for i in sorted(set(i for nm in names for i in touched.get(nm, [])), reverse=True):
            e = ops[i]
            if lane(e) in best:
                continue
            same = e[0] == o[0] and e[4] is None and o[4] is None
            if same and o[0] == "P":
                continue
            if clash(e, o) or (not same and bk[i] & bk[j]):
                best[lane(e)] = i
        for nm in names:
            touched.setdefault(nm, []).append(j)
        k = known.get(o[0], {})
        w = []
        for i in sorted(best.values(), reverse=True):
            if k.get(lane(ops[i]), -1) < i:
                w.append(i)
                for kk, vv in clock[i].items():
                    if k.get(kk, -1) < vv:
                        k[kk] = vv
        waits.append(w)
        c = dict(k)
        c[lane(o)] = j
        clock.append(c)
    needed = set(i for w in waits for i in w)
    count = {q: 0 for q in Q}
    token = {}
    for j, o in enumerate(ops):
        if o[4] is not None:
            token[j] = o[4][:2]
        elif j in needed:
            count[o[0]] += 1
            token[j] = ("e" + o[0], count[o[0]])
    top = {}
    for j, o in enumerate(ops):
        if j in token:
            top[token[j][0]] = max(top.get(token[j][0], 0), token[j][1])
        if o[0] == "X":
            continue
        e = Q[o[0]]
        for i in waits[j]:
            e.wait_ge(T.sem[token[i][0]], token[i][1])
        inst = o[1](e)
        if o[4] is None:
            if j in token:
                inst.then_inc(T.sem[token[j][0]], 1)
        elif o[4][2] == "dma":
            inst.then_inc(T.sem[o[4][0]], 16)
    for name in sorted(top):
        if name[0] != "e":
            g.wait_ge(T.sem[name], top[name])
